import numpy as np, ml_dtypes
CORES = [6,15,38,47]
N = 4
import mx_ref
BF = ml_dtypes.bfloat16
def entries(a):
    return np.ascontiguousarray(a.T).reshape(-1)
def table(e):
    return np.ascontiguousarray(np.reshape(e, (-1, 16)).T).astype(np.int32)
def gcols(t, e):
    v = np.concatenate([t.reshape(8, 16, -1, 4), np.zeros((8, 16, 1, 4), BF)], axis=2)
    return np.ascontiguousarray(np.stack([v[g][:, e[g]] for g in range(8)])).reshape(128, -1)
def tile(rs):
    return np.stack(rs, axis=2).reshape(128, -1).astype(BF)
def pick(q, e):
    c = np.concatenate([q[0].reshape(128, -1, 4), np.zeros((128, 1, 4), np.uint8)], axis=1); s = np.concatenate([q[1], np.ones((16, 1), np.uint8)], axis=1)
    return (np.ascontiguousarray(c[:, e].reshape(128, -1)), np.ascontiguousarray(s[:, e]))
def join(*qs):
    return (np.concatenate([q[0] for q in qs], axis=1), np.concatenate([q[1] for q in qs], axis=1))
def put(q, e, v):
    c, s = q[0].reshape(128, -1, 4).copy(), q[1].copy(); c[:, e] = v[0].reshape(128, -1, 4); s[:, e] = v[1]
    return (c.reshape(128, -1), s)
def pk(c, s):
    return (np.ascontiguousarray(c), mx_ref.live(s))
def emit(q):
    return q[0], q[1]
def packed(v, rng):
    q = [mx_ref.quantize(np.ascontiguousarray(v[r])) for r in range(N)]
    return np.stack([a for a, b in q]), np.stack([mx_ref.plane(b, rng) for a, b in q])
def values_of_codes():
    e, c = np.zeros((128, 128, 4), np.float32), np.zeros((128, 2, 4), np.uint8)
    e[np.arange(128), np.arange(128), 0] = 1
    c[:127, :, 0] = np.arange(256).reshape(2, 128).T[:127]
    return mx_ref.matmul(mx_ref.quantize(e.reshape(128, 512).astype(BF)), (c.reshape(128, 8), np.full((16, 2), 127, np.uint8))).T.reshape(-1).astype(np.float64)
CODE_VALUE, SCALE_VALUE = values_of_codes(), 2.0 ** (np.arange(256) - 127.0)
def decode(q):
    return (CODE_VALUE[q[0]].reshape(16, 8, -1, 4) * SCALE_VALUE[q[1]][:, None, :, None] + 0.0).reshape(128, -1).astype(np.float32)
def f(rng, *shape):
    return mx_ref.flush((rng.standard_normal(shape, dtype=np.float32) * np.exp2(rng.integers(-2, 3, shape[:-1] + (1,)))).astype(BF))
def wide(rng, *shape, cols=0):
    v = rng.standard_normal(shape, dtype=np.float32) * np.exp2(rng.integers(-12, 13, shape)).astype(np.float32)
    if cols: v *= np.repeat(np.exp2(rng.integers(-cols, cols + 1, shape[:-2] + (1, shape[-1] // 4))) * (rng.random(shape[:-2] + (1, shape[-1] // 4)) > 0.0625), 4, axis=-1).astype(np.float32)
    return mx_ref.flush(v.astype(BF))
C, TH, R = 448, 320, 3
def big(v):
    v = v.astype(np.float32)
    v[np.abs(v) < np.float32(2.0 ** -16)] = 0
    return v.astype(BF)
def numbers_of(rng):
    return {"x": big(f(rng, N, 128, 4 * C)), "u": np.array(f(rng, N, 128, 512)), "v": np.array(f(rng, N, 128, 512))}
def offers(rng):
    return np.stack([table(rng.integers(0, C, 8 * R * C)) for r in range(N)])
def layers(rng):
    return big(f(rng, N, 128, 2048)).reshape(N, 8, 16, 4, 8, 16, 4)
def weights(rng, w):
    c, p = packed(np.ascontiguousarray(w).reshape(N, 128, 2048), rng)
    return {"wc": c, "ws": p}
def setup_inputs(rng):
    return {**numbers_of(rng), "cd": offers(rng), **weights(rng, layers(rng))}
def setup_inputs_ties(rng):
    d = numbers_of(rng)
    x = d["x"].astype(np.float32).reshape(N, 8, 16, C, 4)
    x[:, :, 0] = 0
    k = rng.integers(-2, 3, (N, 4, C))
    for r in range(N): x[r, :, 0, :, 0] = k[r][rng.permutation(8) % 4]
    u = d["u"].reshape(N, 128, 128, 4)
    u[:, :, ::16] = 0
    o = rng.permutation(N)
    for r in range(N):
        for h in range(0, 128, 16): u[r, h, h, 0] = 0.0 if r == o[0] else -1.0 if r == o[1] else 1.0
    w = layers(rng)
    w[:, :, :, :, :, 0] = 0
    return {"x": x.reshape(N, 128, 4 * C).astype(BF), "u": u.reshape(N, 128, 512), "v": d["v"], "cd": offers(rng), **weights(rng, w)}
def setup_inputs_near(rng):
    d = numbers_of(rng)
    x = d["x"].astype(np.float32).reshape(N, 8, 16, C, 4)
    x[:, :, 0] = 0
    x[:, :, 8:] = 0
    u = d["u"].reshape(N, 128, 128, 4)
    u[:, :, ::16] = 0
    o = rng.permutation(N) % 4
    for r in range(N):
        s = rng.integers(0, 256, (8, C))
        if o[r] < 3:
            for b in range(8): x[r, :, 8 + b // 4, :, b % 4] = ((s >> b) & 1) * 2.0 ** (b - 23)
        else: x[r, :, 10, :, 0] = (8 + s % 8) * 2.0 ** -33
        if o[r] < 2:
            x[r, :, 0, :, 0] = rng.permutation(8)[:, None] % 2 * 2.0 - 1.0
            x[r, :, 11, :, 0] = 2.0 ** -10
        for g in rng.permutation(8)[:4]:
            j = rng.integers(C)
            x[r, g, 8:, j] = 0
            x[r, g, 8 if o[r] < 3 else 10, j, 0] = rng.choice([-1.0, 1.0]) * 2.0 ** 30
        for h in range(0, 128, 16):
            k = 1.0 if o[r] == 0 else 2.0 ** -30
            if o[r] > 1: k = k * rng.choice([-1.0, 1.0])
            if o[r] < 2:
                u[r, h, h, 0] = k
                u[r, h + 11, h, 0] = k
            if o[r] < 3: u[r, h + 8:h + 10, h] = k
            else: u[r, h + 10, h, 0] = k
    w = layers(rng)
    w[:, :, 0] = 0
    w[:, :, 8:] = 0
    w[:, :, :, :, :, 0] = 0
    w[:, :, :, :, :, 8:] = 0
    return {"x": x.reshape(N, 128, 4 * C).astype(BF), "u": u.reshape(N, 128, 512), "v": d["v"], "cd": offers(rng), **weights(rng, w)}
def setup_inputs_huge(rng):
    d = numbers_of(rng)
    o = rng.permutation(N)
    c = rng.choice([-1.0, 1.0], (N, 1, 1, C, 1))
    c[o < N // 2] = c[o < N // 2][:, :, :, :1]
    x = (0.6 + 0.09 * rng.random((N, 8, 16, C, 4))) * 2.0 ** 30 * c
    u = d["u"].reshape(N, 128, 128, 4)
    for r in range(N):
        a = np.full((128, 8, 4), 2.0 ** 30)
        if 0 < o[r] < N - 1: a = 2.0 ** 29 * (1.0 - 0.1 * rng.random((128, 8, 4)))
        if o[r] < N // 2: a = a * (rng.permutation(8) % 2 * 2.0 - 1.0)[None, :, None]
        u[r, :, ::16] = a.astype(np.float32).astype(BF)
    w = np.zeros((N, 128, 4, 128, 4), np.float32)
    i = np.arange(128)
    for b in range(4): w[:, i, b, i, b] = 4
    return {"x": x.astype(np.float32).reshape(N, 128, 4 * C).astype(BF), "u": u.reshape(N, 128, 512), "v": d["v"], "cd": offers(rng), **weights(rng, w.astype(BF))}
def setup_inputs_few(rng):
    d = numbers_of(rng)
    x = np.zeros((N, 8, 16, C, 4), np.float32)
    x[:, :, 1, :, 0] = 1.96875
    x[:, :, 2:4] = (129 + 2 * rng.integers(0, 64, (N, 8, 2, C, 4))) * np.exp2(-7.0 - rng.integers(8, 15, (N, 8, 2, C, 4))) * rng.choice([-1.0, 1.0], (N, 8, 2, C, 4))
    u = d["u"].reshape(N, 128, 128, 4)
    u[:, :, ::16] = 0
    for h in range(0, 128, 16): u[:, h, h, 0] = 1
    o, lists = rng.permutation(N), []
    for r in range(N):
        p = rng.permutation(C)
        s = rng.integers(8, 16, (8, C)) * 0.125
        s[:, p[TH:]] *= -1.0
        x[r, :, 0, :, 0] = s
        k = (rng.permutation(R * C) % 4).reshape(R, 1, C)
        low, high, e = p[rng.integers(TH, C, (R, 8, C))], p[rng.integers(0, TH, (R, 8, C))], rng.integers(0, C, (R, 8, C))
        e = np.where(k == 0, low, np.where(k == 1, high, np.where(k == 2, e, e[:, :1])))
        if r == o[0]: e = np.zeros((R, 8, C), np.int64)
        if r == o[1]: e = np.full((R, 8, C), C - 1)
        lists.append(table(e))
    w = np.zeros((N, 8, 16, 4, 8, 16, 4), np.float32)
    w[:, :, 2:4, :, :, 8:] = rng.choice([-1.0, 1.0], (N, 8, 2, 4, 8, 8, 4))
    return {"x": x.reshape(N, 128, 4 * C).astype(BF), "u": u.reshape(N, 128, 512), "v": d["v"], "cd": np.stack(lists), **weights(rng, w.astype(BF))}
def setup_inputs_spread(rng):
    d = setup_inputs(rng)
    d["x"] = big(wide(rng, N, 128, 4 * C, cols=6))
    return d
def check_inputs(d):
    b = []
    for k in ("x", "u", "v"):
        a = np.abs(d[k].astype(np.float32))
        if not (np.isfinite(a).all() and ((a == 0) | (a >= 2.0 ** -30) & (a <= 2.0 ** 30)).all()): b.append("a value of " + k)
    if not ((d["cd"] >= 0) & (d["cd"] < C)).all(): b.append("an entry of cd")
    none, least, most = [emit(mx_ref.quantize(np.full((128, 16), k, np.float32).astype(BF)))[1][0, 0] for k in (0.0, 2.0 ** -30, 2.0 ** 30)]
    for r in range(N):
        if ((d["wc"][r] == 0x7F) | (d["wc"][r] == 0xFF)).any(): b.append("wc: a code that is no number")
        s = mx_ref.live(d["ws"][r])
        if ((s != none) & ((s < least) | (s > most))).any(): b.append("ws: a scale out of range")
    return b
def reference(x, u, v, cd, wc, ws):
    qu = [mx_ref.quantize(u[r]) for r in range(N)]
    lay = [pk(wc[r], ws[r]) for r in range(N)]
    give = [entries(cd[r]).reshape(R, 8, C) for r in range(N)]
    now = [x[r] for r in range(N)]
    lead, i = np.zeros((N, 8, C), np.int64), np.arange(C)
    for t in range(R):
        q = [mx_ref.quantize(now[r]) for r in range(N)]
        own = [decode(q[r]) for r in range(N)]
        place = np.zeros((N, 8, C), np.int64)
        for r in range(N):
            s = mx_ref.matmul(qu[r], q[r])[::16] + np.float32(0.0)
            np.put_along_axis(place[r], np.argsort(-s, axis=1, kind="stable"), i[None, :], axis=1)
        made = [None] * N
        for d in range(N):
            r = (d - 1 - t) % N
            c = give[d][t]
            p = place[d][:, c]
            visit = np.argsort(place[r], axis=0, kind="stable")
            left = np.ones((8, C), bool)
            for g in visit:
                a = p[g, :, i].T
                stay = left & (a < TH)
                left = np.where(np.any(stay, axis=0), stay, left)
                k = np.argmin(np.where(left, a, C), axis=0)
                lead[d, g, i] = c[k, i]
            z = mx_ref.quantize(gcols(own[d].astype(BF), lead[d]))
            h = tile([np.maximum(mx_ref.matmul(pick(lay[d], np.arange(128 * b, 128 * b + 128)), z), np.float32(0.0)) * np.float32(0.015625) for b in range(4)])
            made[r] = (own[r] + decode(mx_ref.quantize(h))).astype(BF)
        now = made
    y, el = np.zeros((N, 128, C), np.float32), np.zeros((N, 8, C), np.float32)
    oc, osc = np.zeros((N, 128, 4 * C), np.uint8), np.zeros((N, 16, C), np.uint8)
    for r in range(N):
        q = mx_ref.quantize(now[r])
        y[r] = mx_ref.matmul(mx_ref.quantize(v[r]), q)
        el[r] = lead[r]
        oc[r], osc[r] = emit(q)
    return {"y": y, "el": el, "oc": oc, "osc": osc}

@@ -1,0 +1,560 @@
+import math
+from concourse.mybir import dt, AluOpType as OP, ActivationFunctionType as AF
+
+C, R, TH = 448, 3, 320
+CUT = [224, 192, 192, 256]
+RUNS = [[(0, k), (k, C)] for k in CUT]
+NS = C // 32
+TILES = [[(s - 1, 0), (s, 1), (s - 2, 0) if s > 1 else None, (s - 1, 1)] for s in (13, 11, 9, 7, 5, 3, 1)] + [[("e", 0), ("e", 1), ("r", 0), (13, 0)]]
+WIDTH = [C, 384, 320, 256, 192, 128, 128, C]
+NE = [7, 4, 4]
+NL = [4, 2, 2]
+NA0 = 2
+NOW = 4
+GM = [False, True, True]
+LAYV = "z00 z01 q0 z10 g00 g01 h0 z11 q1 g10 g11 h1"
+LAYA = "z02 z03 z12 g02 g03 z13 g12 g13"
+
+BF, F32, I32, U16, Q, U8 = "bfloat16", "float32", "int32", "uint16", "float8_e4m3fn_x4", "uint8"
+SCRATCH = {"ps": ("psum", [128, 4096], F32)}
+
+
+def _sb(name, n, d):
+    SCRATCH[name] = ("sbuf", [128, n], d)
+
+
+def _mx(name, n):
+    _sb(name + "q", n, Q)
+    _sb(name + "s", n, U8)
+
+
+for _n, _w, _d in [
+    ("xin", 4 * C, BF), ("xt", 4 * C, BF), ("ut", 512, BF), ("vt", 512, BF), ("cds", 128, I32), ("cdg", 128, F32), ("cdt", 128, F32),
+    ("off1", 96, U16), ("et", 2048, BF), ("ones", 128, BF), ("cst", 512, BF), ("csh", 512, BF), ("c2", 512, BF),
+    ("pb", 192, F32), ("pc", 192, F32), ("col", 16, F32), ("ib", 64, F32), ("offc", 64, U16), ("ig", 128, BF), ("ia", 128, BF),
+    ("ca", 384, BF), ("cb", 384, BF), ("r32", 32, BF), ("i32w", 32, F32), ("r32b", 32, BF),
+    ("cm0", C, BF), ("cmask", C, BF), ("j0", C, F32), ("jt", C, F32), ("jrow", C, F32), ("dk", 256, F32),
+    ("m1", 2 * C, F32), ("st", 2 * C, F32), ("sg", 16 * C, BF), ("junk", 5824, BF), ("racc", 28, F32), ("rp", C, BF),
+    ("wo", 512, BF), ("tab", C, F32), ("gx", 512, F32), ("ty", 512, F32), ("fl", 512, BF), ("lcp", 256, F32),
+    ("fs", 512, BF), ("nn", 256, I32), ("key", 256, F32), ("km", 256, F32),
+    ("tmp", 128, F32), ("tp", 32, F32), ("ti", 32, I32), ("tj", 32, I32), ("offz", 32, U16),
+    ("dp", 4 * C, BF), ("zt", 4 * C, BF), ("gt", 4 * C, BF), ("yb", C, F32), ("elb", C, F32),
+]:
+    _sb(_n, _w, _d)
+for _i in range(8):
+    _sb("k%d" % _i, 4 * WIDTH[_i], BF)
+for _n, _w in [("u", 128), ("ub", 256), ("v", 128), ("wl", 512), ("e", 512), ("cs", 256), ("cc", 128), ("k", sum(WIDTH)), ("od", 128), ("z", C)]:
+    _mx(_n, _w)
+for _t in range(R + 1):
+    _mx("t%d" % _t, C)
+for _t in range(R):
+    _mx("h%d" % _t, C)
+    _mx("l%d" % _t, C)
+    _sb("ord%d" % _t, 128, BF)
+    _sb("got%d" % _t, 128, BF)
+
+SEMAPHORES = ["qV", "qA", "qP", "qG", "sent"] + ["d%d" % i for i in range(48)] + ["ao%d" % t for t in range(R)] + ["ah%d_%d" % (t, c) for t in range(R) for c in range(2)]
+
+
+def rank_program(g, core, T, topo):
+    rank = T.rank_of(core)
+    if rank is None:
+        return
+    N = len(T.cores)
+    eng = {"V": g.vector, "A": g.scalar, "P": g.tensor, "G": g, "S": g.sync}
+    total = {}
+    known = {q: {} for q in eng}
+    snap = {}
+    wrote, read, bank = {}, {}, {}
+    ndma = [0]
+
+    def wait(q, ev):
+        s, n = ev
+        if known[q].get(s, 0) >= n:
+            return
+        eng[q].wait_ge(T.sem[s], n)
+        known[q][s] = n
+        for s2, n2 in snap.get(ev, {}).items():
+            if known[q].get(s2, 0) < n2:
+                known[q][s2] = n2
+
+    def deps(q, r, w, b):
+        need = {}
+        evs = [wrote[k] for k in list(r) + list(w) if k in wrote]
+        for k in w:
+            evs += read.get(k, [])
+        for k in b:
+            evs += [ev for q2, ev in bank.get(k, {}).items() if q2 != q]
+        for s, n in evs:
+            need[s] = max(need.get(s, 0), n)
+        for s, n in sorted(need.items(), key=lambda e: e[0] == "q" + q):
+            wait(q, (s, n))
+
+    def note(q, ev, r, w, b):
+        snap[ev] = dict(known[q])
+        for k in r:
+            read.setdefault(k, []).append(ev)
+        for k in w:
+            wrote[k] = ev
+            read[k] = []
+        for k in b:
+            bank.setdefault(k, {})[q] = ev
+
+    def op(q, call, r=(), w=(), b=()):
+        deps(q, r, w, b)
+        s = "q" + q
+        total[s] = total.get(s, 0) + 1
+        call().then_inc(T.sem[s], 1)
+        note(q, (s, total[s]), r, w, b)
+
+    def dma(q, out, in_, r=(), w=()):
+        deps(q, r, w, ())
+        s = "d%d" % ndma[0]
+        ndma[0] += 1
+        total[s] = 16
+        eng[q].dma_start(out, in_).then_inc(T.sem[s], 16)
+        note(q, (s, 16), r, w, ())
+
+    def width(src, dst):
+        return len(topo.engines(src, dst))
+
+    def send(out, in_, sem, dst, r):
+        deps("G", r, (), ())
+        rid, pid, _ = topo.addr(dst)
+        g.remote_dma(out, in_, T.sem[sem], T.sem["sent"], pid, rid, topo.mask(core, dst))
+        total["sent"] = total.get("sent", 0) + width(core, dst)
+
+    def arrives(key, sem, n):
+        total[sem] = n
+        wrote[key] = (sem, n)
+
+    V, A, P = g.vector, g.scalar, g.tensor
+
+    def ps(b, n, a=0, step=1):
+        return T.ps[:, 512 * b + a:512 * b + n:step]
+
+    def ts(out, in0, s1, o0, s2=None, o1=None, **k):
+        if o1 is None:
+            op("V", lambda: V.tensor_scalar(out, in0, s1, None, o0), **k)
+        else:
+            op("V", lambda: V.tensor_scalar(out, in0, s1, s2, o0, o1), **k)
+
+    def tt(out, a, b_, o, **k):
+        op("V", lambda: V.tensor_tensor(out, a, b_, o), **k)
+
+    def cp(out, a, **k):
+        op("V", lambda: V.tensor_copy(out, a), **k)
+
+    def tr(out, a, **k):
+        op("V", lambda: V.transpose(out, a), **k)
+
+    def ms(out, c, **k):
+        op("V", lambda: V.memset(out, c), **k)
+
+    def scan(out, d0, d1, o0, o1, **k):
+        op("V", lambda: V.tensor_tensor_scan(out, d0, d1, 0.0, o0, o1), **k)
+
+    def act(out, a, f, kw=None, **k):
+        op("A", lambda: A.activation(out, a, f, **(kw or {})), **k)
+
+    def qz(name, a, b_, tile, **k):
+        op("V", lambda: V.quantize_mx(T[name + "q"][:, a:b_], T[name + "s"][:, a:b_], tile), **k)
+
+    def mm(b, st, sa, mv, a, b_, start, stop, r):
+        op("P", lambda: P.matmul_mx(ps(b, b_ - a), T[st + "q"][:, sa:sa + 128], T[st + "s"][:, sa:sa + 128],
+                                    T[mv + "q"][:, a:b_], T[mv + "s"][:, a:b_], start, stop), r=r, b=[b])
+
+    def iota(out, pat, base, cm, w):
+        op("G", lambda: g.iota(out, pat, base, cm, allow_small_or_imprecise_dtypes=True), w=w)
+
+    def sel(out, in_, pat, o, cm, **k):
+        op("G", lambda: g.affine_select(out, in_, pat, o, 0.0, 0, cm), **k)
+
+    for c, (a, e) in enumerate(RUNS[0]):
+        dma("S", T.xin[:, 4 * a:4 * e], T.x[:, 4 * a:4 * e], w=["xin%d" % c])
+    dma("A", T.ut[:], T.u[:], w=["ut"])
+    iota(T.ib[:, 0:8], [[32, 4], [0, 2]], 0, 0, ["ibU0"])
+    iota(T.ib[:, 8:16], [[32, 4], [0, 2]], 16, 0, ["ibU1"])
+    iota(T.pb[:, 0:32], [[2, 32]], 0, 0, ["pb0"])
+    iota(T.pb[:, 32:64], [[0, 2], [1, 16]], 0, 0, ["pb1"])
+    iota(T.col[:, 0:1], [[0, 1]], 0, 1, ["p"])
+    iota(T.cm0[:], [[0, NS], [2, 32]], -1, 0, ["cm0"])
+    ms(T.cds[:], 0, w=["cds"])
+    ms(T.et[:, 0:1024], 0.0, w=["et"])
+    cp(T.offc[:, 0:16], T.ib[:, 0:16], r=["ibU0", "ibU1"], w=["offU"])
+    act(T.ones[:], T.et[:, 0:128], AF.Exp, r=["et"], w=["ones"])
+    act(T.et[:, 1024:2048], T.et[:, 0:1024], AF.Copy, r=["et"], w=["etb"])
+    for i in range(6, -1, -1):
+        n, m = 4 * WIDTH[i], 512 if i == 6 else 256
+        dma("S", T["k%d" % i][:, n - m:n], T.et[:, 0:m], r=["et"], w=["kz%d" % i])
+    for a in range(4):
+        dma("S", T.cds[32 * a:32 * a + 24, 0:112], T.cd[a::4, :], r=["cds"], w=["cds%d" % a])
+    dma("S", T.c2[:], T.et[:, 0:512], r=["et"], w=["c2z"])
+    dma("S", T.wo[:], T.et[:, 0:512], r=["et"], w=["wo0", "wo1", "wo2", "wo3"])
+    dma("S", T.rp[:], T.et[:, 0:C], r=["et"], w=["rph", "rpl"])
+    dma("S", T.wlq[:].bitcast(dt.uint8), T.wc[:], w=["wq"])
+    dma("S", T.wls[:], T.ws[:], w=["ws"])
+    dma("S", T.vt[:], T.v[:], w=["vt"])
+    tr(T.pc[:, 0:64], T.pb[:, 0:64], r=["pb0", "pb1"], w=["pc01"])
+    l32x2, l16 = T.pc[:, 0:1], T.pc[:, 32:33]
+    pg, pa0, pa1, tie = T.col[:, 1:2], T.col[:, 2:3], T.col[:, 3:4], T.col[:, 5:6]
+    iota(T.ig[:], [[0, 16], [1, 8]], 0, 0, ["ig"])
+    iota(T.ia[:], [[1, 8], [-100, 2], [0, 8]], 100, 0, ["ia"])
+    iota(T.pb[:, 64:96], [[0, 2], [2000, 2], [0, 8]], 0, 0, ["pb2"])
+    for hf in range(2):
+        iota(T.pb[:, 96 + 16 * hf:112 + 16 * hf], [[64, 2], [6, 4], [32, 2]], 0, 0, ["pb3%d" % hf])
+        iota(T.pb[:, 128 + 16 * hf:144 + 16 * hf], [[32, 2], [128, 4], [16, 2]], 0, 0, ["pb4%d" % hf])
+    iota(T.pb[:, 160:192], [[0, 2], [100, 2], [-1, 8]], -100, 0, ["pb5"])
+    iota(T.i32w[:], [[0, 4], [1, 8]], 0, 0, ["i32w"])
+
+    def counter(n, slots, colap, key, sign):
+        x0, x1 = T.ca[:, 128 * n:128 * n + 128], T.cb[:, 128 * n:128 * n + 128]
+        ts(x0, T.ig[:], colap, OP.is_equal, sign, OP.mult, r=["ig", key], w=["ca" + key])
+        ts(x1, T.ia[:], colap, OP.is_equal, sign, OP.mult, r=["ia", key], w=["cb" + key])
+        nm, t = slots[0]
+        first = T[nm][:, t:512:4]
+        tt(first, x0, x1, OP.subtract, r=["ca" + key, "cb" + key], w=["%s%d" % (nm, t)])
+        for nm2, t2 in slots[1:]:
+            sel(T[nm2][:, t2:512:4], first, [[0, 128]], OP.is_ge, 0, r=["%s%d" % (nm, t)], w=["%s%d" % (nm2, t2)])
+
+    def constants_1():
+        counter(1, [("cst", 1), ("cst", 3), ("csh", 1)], pa1, "pa1", 1.0)
+        counter(2, [("csh", 2)], pg, "pg", -1.0)
+        tr(T.pc[:, 64:192], T.pb[:, 64:192], r=["pb2", "pb30", "pb31", "pb40", "pb41", "pb5"], w=["pc2"])
+        ts(T.col[:, 4:5], T.pc[:, 160:161], pg, OP.add, 0.5, OP.min, r=["pc2", "pg"], w=["tie0"])
+        ts(T.r32[:], T.i32w[:], pg, OP.is_equal, r=["i32w", "pg"], w=["r32"])
+        ts(T.r32b[:], T.i32w[:], -1.0, OP.add, pg, OP.is_equal, r=["i32w", "pg"], w=["r32b"])
+        ts(tie, T.col[:, 4:5], -0.5, OP.max, r=["tie0"], w=["tie"])
+        ts(T.r32b[:, 0:32:8], T.i32w[:, 0:32:8], 7.0, OP.add, pg, OP.is_equal, r=["i32w", "pg"], w=["r32b"])
+        tt(T.r32[:], T.r32[:], T.r32b[:], OP.subtract, r=["r32b"], w=["r32"])
+        iota(T.r32[:, 0:32:16], [[0, 2]], -8, 0, ["r32"])
+        for b in range(4):
+            sel(T.c2[:, 129 * b:128 * b + 128:4], T.r32[:], [[0, 32]], OP.is_ge, 0, r=["r32", "c2z"], w=["c2r%d" % b])
+        iota(T.racc[:, 0:2], [[0, 2]], 0, 0, ["racc0"])
+        iota(T.ib[:, 16:24], [[56, 2], [16, 2], [28, 2]], 0, 0, ["ibA"])
+        iota(T.ib[:, 24:32], [[1, 8]], 0, 0, ["ibB"])
+        iota(T.ib[:, 32:48], [[1, 8], [64, 2]], 0, 0, ["ibL"])
+        iota(T.ib[:, 48:64], [[1, 8], [64, 2]], 8, 0, ["ibN"])
+        iota(T.j0[:], [[32 + 512 * 32, NS], [1, 32]], -512, 0, ["j0"])
+        for b in range(4):
+            sel(T.et[:, 512 * b + b:512 * b + 512:4], T.ones[:], [[-1, 128]], OP.is_equal, 1, r=["ones", "etb"], w=["et"] if b == 0 else ["et%d" % b])
+        iota(T.dk[:], [[0, 256]], 0, 0, ["dk"])
+        iota(T.dk[:, 0:256:8], [[0, 32]], -1000, 0, ["dk"])
+
+    def constants_2():
+        qz("cs", 0, 128, T.cst[:], r=["cst%d" % t for t in range(4)], w=["cs"])
+        qz("cs", 128, 256, T.csh[:], r=["csh%d" % t for t in range(4)], w=["csh"])
+        qz("cc", 0, 128, T.c2[:], r=["c2r%d" % b for b in range(4)], w=["cc"])
+        act(T.jt[:], T.j0[:], AF.Identity, {"scale": 2.0 ** -9, "bias": T.pc[:, 64:65]}, r=["j0", "pc2"], w=["jt"])
+
+    def lists_of_candidates():
+        for nm, a, b_, c in (("A", 16, 24, 32), ("B", 24, 32, 96), ("L", 32, 48, 128), ("N", 48, 64, 128)):
+            ts(T.offc[:, a:b_], T.ib[:, a:b_], T.pc[:, c:c + 1], OP.add, r=["ib" + nm, "pc01", "pc2"], w=["off" + nm])
+        cp(T.cdg[:], T.cds[:].indirect(T.offc[:, 16:24]), r=["offA"] + ["cds%d" % a for a in range(4)], w=["cdg"])
+        tr(T.cdt[:], T.cdg[:], r=["cdg"], w=["cdt"])
+        cp(T.off1[:], T.cdt[:].indirect(T.offc[:, 24:30]), r=["cdt", "offB"], w=["off1"])
+
+    koff = [sum(WIDTH[:i]) for i in range(8)]
+    where = {u: (i, t) for i, tl in enumerate(TILES) for t, u in enumerate(tl) if u}
+    joff = {}
+    for s in range(1, NS):
+        for h in range(2):
+            joff[(s, h)] = sum(32 * a[0] for a in joff)
+    by_act, early, late, act_early, act_late, CH, gm = [], [], [], [], [], [], [False]
+
+    def plan(t):
+        CH[:] = RUNS[t]
+        k = CUT[t] // 32
+        e = [(s, h) for s in range(k - 1, -1, -1) for h in range(2)]
+        l = [(s, h) for s in range(NS - 1, k - 1, -1) for h in range(2)]
+        act_early[:], early[:], act_late[:], late[:] = e[:NE[t]], e[NE[t]:], l[:NL[t]], l[NL[t]:]
+        by_act[:] = act_early + act_late
+        gm[0] = GM[t]
+
+    def slot(u, a, n):
+        i, t = where[u]
+        return T["k%d" % i][:, 4 * a + t:4 * n:4]
+
+    def ukey(u):
+        return "u%s_%d" % u
+
+    def zkey(u):
+        i = where[u][0]
+        return ["kz%d" % i] if i < 7 else []
+
+    def run_of(u):
+        return 0 if 32 * u[0] < CH[0][1] else 1
+
+    def sbank(c, h, q):
+        return (4 if c == 0 else 0) + h + (2 if q == "A" else 0)
+
+    def scores(t, c):
+        tn = "t%d" % t
+        for h, q in ((0, "V"), (1, "V"), (0, "A"), (1, "A")):
+            mm(sbank(c, h, q), "ub", 128 * h, tn, 0, CH[c][1], True, True, [tn + "_%d" % i for i in range(c + 1)] + ["ubq", "ubs"])
+
+    def prelim(c, h):
+        a, e = CH[c]
+        b = sbank(c, h, "V")
+        if gm[0]:
+            tr(T.st[:, C * h + a:C * h + e], ps(b, e, a), w=["st%d%d" % (c, h)], b=[b])
+        else:
+            tt(T.m1[:, C * h + a:C * h + e], ps(b, e, a), T.cmask[:, a:e], OP.min, r=["cmask"], w=["m1%d%d" % (c, h)], b=[b])
+            tr(T.st[:, C * h + a:C * h + e], T.m1[:, C * h + a:C * h + e], r=["m1%d%d" % (c, h)], w=["st%d%d" % (c, h)])
+
+    def sc(u):
+        c = C * u[1] + 32 * u[0] + 31
+        return T.st[:, c:c + 1]
+
+    def stk(u):
+        return ["st%d%d" % (run_of(u), u[1])]
+
+    def v_unit(u):
+        n, b = 32 * u[0] + 32, sbank(run_of(u), u[1], "V")
+        ts(slot(u, 0, n), ps(b, n), sc(u), OP.is_lt, r=stk(u) + zkey(u), w=[ukey(u), ukey(u) + "d"], b=[b])
+
+    def v_eq(c, h):
+        a, e = CH[c]
+        b = sbank(c, h, "V")
+        tt(slot(("e", h), a, e), ps(b, e, a), T.st[:, C * h + a:C * h + e], OP.is_equal, r=["st%d%d" % (c, h)], w=["ue%d%d%d" % (c, h, i) for i in range(4)], b=[b])
+        for i in range(4 if gm[0] else 0):
+            view = T.k7[32 * i:32 * i + 32, 4 * a + h:4 * e:4]
+            wait("G", ("qG", total["qG"]))
+            sel(view, view, [[0, (e - a) // 32], [1, 32]], OP.is_ge, -1, w=["ue%d%d%d" % (c, h, i)])
+
+    def acc(u):
+        c = 2 * u[0] + u[1]
+        return T.racc[:, c:c + 1]
+
+    def a_sum(u):
+        n = 32 * u[0]
+        if n:
+            act(T.junk[:, joff[u]:joff[u] + n], slot(u, 0, n), AF.Copy, {"accum_out": acc(u)}, r=[ukey(u)], w=["racc" + ukey(u), "junk" + ukey(u)])
+
+    def a_one(u):
+        i, n, b = by_act.index(u), 32 * u[0] + 32, sbank(run_of(u), u[1], "A")
+        act(T.sg[:, C * i:C * i + n], ps(b, n), AF.Sign, {"bias": sc(u), "scale": -1.0}, r=stk(u), w=["sg%d" % i], b=[b])
+
+    def a_two(u):
+        i, n = by_act.index(u), 32 * u[0]
+        act(slot(u, 0, n), T.sg[:, C * i:C * i + n], AF.Relu, {"accum_out": acc(u)}, r=["sg%d" % i] + zkey(u), w=[ukey(u), "racc" + ukey(u)])
+        act(slot(u, n, n + 32), T.sg[:, C * i + n:C * i + n + 32], AF.Relu, r=["sg%d" % i] + zkey(u), w=[ukey(u) + "d"])
+
+    def a_made(us):
+        for k, u in enumerate(us):
+            if k == 0:
+                a_one(u)
+            if k + 1 < len(us):
+                a_one(us[k + 1])
+            a_two(u)
+
+    def v_q(i):
+        keys = []
+        for u in TILES[i]:
+            if u and u[0] == "e":
+                keys += ["ue%d%d%d" % (c, u[1], x) for c in range(2) for x in range(4)]
+            elif u:
+                keys += [ukey(u)] + ([ukey(u) + "d"] if u[0] != "r" else []) + zkey(u)
+        qz("k", koff[i], koff[i] + WIDTH[i], T["k%d" % i][:], r=keys, w=["kq%d" % i])
+
+    def places_first(t):
+        plan(t)
+        scores(t, 0)
+        prelim(0, 0)
+        prelim(0, 1)
+        a_made(act_early[:NA0])
+        v_eq(0, 0)
+        v_eq(0, 1)
+        for u in early[:NOW]:
+            v_unit(u)
+
+    def places_rest(t):
+        scores(t, 1)
+        if t == 0:
+            constants_1()
+        for u in early[NOW:]:
+            v_unit(u)
+        a_made(act_early[NA0:])
+        prelim(1, 0)
+        prelim(1, 1)
+        v_eq(1, 0)
+        v_eq(1, 1)
+        for u in early:
+            a_sum(u)
+        a_made(act_late)
+        for u in late:
+            v_unit(u)
+        for u in late:
+            a_sum(u)
+        if t == 0:
+            constants_2()
+        for i in (6, 5, 4, 0, 1, 2, 3):
+            v_q(i)
+        rk = ["racc0"] + ["racc" + ukey((s, h)) for s in range(1, NS) for h in range(2)]
+        big = 1.5 * 2.0 ** 28
+        ts(T.rp[:, 0:C:16], T.racc[:], big, OP.add, big, OP.subtract, r=rk, w=["rph"])
+        tt(T.rp[:, 1:C:16], T.racc[:], T.rp[:, 0:C:16], OP.subtract, r=rk + ["rph"], w=["rpl"])
+        tr(slot(("r", 0), 0, C), T.rp[:], r=["rph", "rpl"], w=[ukey(("r", 0))])
+        v_q(7)
+        for i in range(8):
+            mm(4, "cs", 128 if i == 7 else 0, "k", koff[i], koff[i] + WIDTH[i], i == 0, i == 7, ["kq%d" % i, "csh" if i == 7 else "cs"])
+
+    def order(t, donor):
+        for a in range(4):
+            ts(T.wo[:, 128 * a:128 * a + 112], ps(4, C, a, 4), tie, OP.is_lt, r=["tie"], w=["wo%d" % a], b=[4])
+        qz("od", 0, 128, T.wo[:], r=["wo%d" % a for a in range(4)], w=["oq"])
+        mm(5, "od", 0, "cc", 0, 128, True, True, ["oq", "cc"])
+        act(T["ord%d" % t][:], ps(5, 128), AF.Exp, {"scale": math.log(2.0)}, w=["ord%d" % t], b=[5])
+        send(T["got%d" % t][:], T["ord%d" % t][:], "ao%d" % t, donor, ["ord%d" % t])
+
+    def candidates(t):
+        tn = "t%d" % t
+        tt(T.tab[:], ps(4, C), T.jt[:], OP.add, r=["jt"], w=["tab"], b=[4])
+        if t == 0:
+            for b in range(4):
+                qz("e", 128 * b, 128 * b + 128, T.et[:, 512 * b:512 * b + 512], r=["et", "et%d" % b], w=["eq%d" % b])
+            lists_of_candidates()
+        for b in range(4):
+            mm(b, "e", 128 * b, tn, 0, C, True, True, [tn + "_0", tn + "_1", "eq%d" % b])
+        act(T.gx[:, 256:512], T.tab[:].indirect(T.off1[:, 32 * t + 16:32 * t + 32]), AF.Copy, r=["tab", "off1"], w=["gx1"])
+        cp(T.gx[:, 0:256], T.tab[:].indirect(T.off1[:, 32 * t:32 * t + 16]), r=["tab", "off1"], w=["gx0"])
+        tr(T.ty[:], T.gx[:], r=["gx0", "gx1"], w=["ty"])
+        ts(T.fl[:], T.ty[:], float(TH), OP.is_lt, r=["ty"], w=["fl"])
+        for b in range(2):
+            act(T.dp[:, C * b:C * b + C], ps(b, C), AF.Copy, w=["dp%d" % b], b=[b])
+        act(T.lcp[:], T.ty[:].indirect(T.offc[:, 32:48]), AF.Copy, {"scale": 2.0 ** -9}, r=["ty", "offL"], w=["lcp"])
+        for b in range(2, 4):
+            act(T.dp[:, C * b:C * b + C], ps(b, C), AF.Copy, w=["dp%d" % b], b=[b])
+
+    def leaders(t, child):
+        got = T["got%d" % t]
+        gk = "got%d" % t
+        arrives(gk, "ao%d" % t, width(child, core))
+        for i in range(4):
+            scan(T.fs[:, 128 * i:128 * i + 128], got[:], T.fl[:, 128 * i:128 * i + 128], OP.mult, OP.add, r=[gk, "fl"], w=["fs%d" % i])
+        ts(T.nn[:], T.fs[:].indirect(T.offc[:, 48:64]), 0.5, OP.mult, -63.5 + 2.0 ** -10, OP.add, r=["fs%d" % i for i in range(4)] + ["offN"], w=["nn"])
+        tt(T.key[:], T.nn[:], T.lcp[:], OP.subtract, r=["nn", "lcp"], w=["key"])
+        scan(T.km[:], T.dk[:], T.key[:], OP.add, OP.max, r=["dk", "key"], w=["km"])
+        for a in range(4):
+            args = (T.tmp[0:32, a:128:4], T.km[32 * a:32 * a + 32, 7:256:8])
+            if a >= 2:
+                act(*args, AF.Copy, {"scale": -2.0 ** 18}, r=["km"], w=["tmp%d" % a])
+            else:
+                ts(*args, -2.0 ** 18, OP.mult, r=["km"], w=["tmp%d" % a])
+        for b in range(4):
+            tr(T.tp[32 * b:32 * b + 32, :], T.tmp[0:32, 32 * b:32 * b + 32], r=["tmp%d" % a for a in range(4)], w=["tp%d" % b])
+        cp(T.ti[:], T.tp[:], r=["tp%d" % b for b in range(4)], w=["ti"])
+        ts(T.tj[:], T.ti[:], 511, OP.bitwise_and, r=["ti"], w=["tj"])
+        cp(T.offz[:], T.tj[:], r=["tj"], w=["offz"])
+
+    def banks(c):
+        return 4 * ((c + 1) % 2)
+
+    def layer(t, child):
+        hn = "h%d" % t
+        runs = RUNS[t + 1]
+
+        def z(c, b, onv):
+            a, e = runs[c]
+            args = (T.zt[:, 4 * a + b:4 * e:4], T.dp[:, C * b:C * b + C].indirect(T.offz[:, a // 16:e // 16]))
+            k = {"r": ["offz", "dp%d" % b], "w": ["z%d_%d" % (c, b)]}
+            if onv:
+                cp(*args, **k)
+            else:
+                act(*args, AF.Copy, **k)
+
+        def zq(c):
+            a, e = runs[c]
+            qz("z", a, e, T.zt[:, 4 * a:4 * e], r=["z%d_%d" % (c, b) for b in range(4)], w=["zq%d" % c])
+            for b in (0, 2, 1, 3):
+                mm(banks(c) + b, "wl", 128 * b, "z", a, e, True, True, ["zq%d" % c, "wq", "ws"])
+
+        def gv(c, b, onv):
+            a, e = runs[c]
+            k = {"w": ["g%d_%d" % (c, b)], "b": [banks(c) + b]}
+            if onv:
+                ts(T.gt[:, 4 * a + b:4 * e:4], ps(banks(c) + b, e - a), 0.0, OP.max, 0.015625, OP.mult, **k)
+            else:
+                act(T.gt[:, 4 * a + b:4 * e:4], ps(banks(c) + b, e - a), AF.Relu, {"scale": 0.015625}, **k)
+
+        def hq(c):
+            a, e = runs[c]
+            qz(hn, a, e, T.gt[:, 4 * a:4 * e], r=["g%d_%d" % (c, b) for b in range(4)], w=[hn + "_%d" % c])
+            sem = "ah%d_%d" % (t, c)
+            send(T["l%dq" % t][:, a:e].bitcast(dt.uint8), T[hn + "q"][:, a:e].bitcast(dt.uint8), sem, child, [hn + "_%d" % c])
+            send(T["l%ds" % t][:, a:e], T[hn + "s"][:, a:e], sem, child, [hn + "_%d" % c])
+
+        todo, made = {True: LAYV.split(), False: LAYA.split()}, set()
+        while todo[True] or todo[False]:
+            for onv in (False, True):
+                while todo[onv]:
+                    w = todo[onv][0]
+                    c = int(w[1])
+                    need = {"z": [], "g": ["q%d" % c], "q": ["z%d%d" % (c, b) for b in range(4)], "h": ["g%d%d" % (c, b) for b in range(4)]}[w[0]]
+                    if not all(x in made for x in need):
+                        break
+                    if w[0] == "z":
+                        z(c, int(w[2]), onv)
+                    elif w[0] == "g":
+                        gv(c, int(w[2]), onv)
+                    else:
+                        (zq if w[0] == "q" else hq)(c)
+                    made.add(todo[onv].pop(0))
+
+    def own_part(t):
+        tn = "t%d" % t
+        for c, (a, e) in enumerate(RUNS[t + 1]):
+            for b in range(4):
+                mm(banks(c) + b, "e", 128 * b, tn, a, e, True, False, [tn + "_0", tn + "_1"])
+
+    def state(t, c, donor):
+        ln, nx = "l%d" % t, "t%d" % (t + 1)
+        a, e = RUNS[t + 1][c]
+        arrives(ln + "_%d" % c, "ah%d_%d" % (t, c), 2 * width(donor, core))
+        for b in (0, 2, 1, 3):
+            mm(banks(c) + b, "e", 128 * b, ln, a, e, False, True, [ln + "_%d" % c])
+        for b in (2, 3):
+            act(T.xt[:, 4 * a + b:4 * e:4], ps(banks(c) + b, e - a), AF.Copy, w=["x%d_%d" % (c, b)], b=[banks(c) + b])
+        for b in (0, 1):
+            cp(T.xt[:, 4 * a + b:4 * e:4], ps(banks(c) + b, e - a), w=["x%d_%d" % (c, b)], b=[banks(c) + b])
+        qz(nx, a, e, T.xt[:, 4 * a:4 * e], r=["x%d_%d" % (c, b) for b in range(4)], w=[nx + "_%d" % c])
+        if t == R - 1:
+            mm(banks(c), "v", 0, nx, a, e, True, True, [nx + "_%d" % c, "vq"])
+            dma("S", T.oc[:, 4 * a:4 * e], T[nx + "q"][:, a:e].bitcast(dt.uint8), r=[nx + "_%d" % c])
+            for k in range(4):
+                dma("AS"[k % 2], T.osc[4 * k:4 * k + 4, a:e], T[nx + "s"][32 * k:32 * k + 4, a:e], r=[nx + "_%d" % c])
+            cp(T.yb[:, a:e], ps(banks(c), e - a), w=["yb%d" % c], b=[banks(c)])
+            dma("A", T.y[:, a:e], T.yb[:, a:e], r=["yb%d" % c])
+
+    ts(pg, T.col[:, 0:1], l16, OP.subtract, 1.0 / 16, OP.mult, r=["p", "pc01"], w=["pg"])
+    ts(T.col[:, 6:7], T.col[:, 0:1], 2.0, OP.mult, l32x2, OP.subtract, r=["p", "pc01"], w=["p2"])
+    ts(pa0, T.col[:, 6:7], 1.0 / 32, OP.mult, r=["p2"], w=["pa0"])
+    ts(pa1, T.col[:, 6:7], 1.0 / 32, OP.mult, 1.0, OP.add, r=["p2"], w=["pa1"])
+    ts(T.cmask[:], T.cm0[:], l32x2, OP.subtract, -1e28, OP.mult, r=["cm0", "pc01"], w=["cmask"])
+    qz("u", 0, 128, T.ut[:], r=["ut"], w=["uq"])
+    cp(T.ubq[:].bitcast(dt.uint32), T.uq[:].bitcast(dt.uint32).indirect(T.offc[:, 0:16]), r=["uq", "offU"], w=["ubq"])
+    act(T.ubs[:], T.us[:].indirect(T.offc[:, 0:16]), AF.Copy, r=["uq", "offU"], w=["ubs"])
+    for c, (a, e) in enumerate(RUNS[0]):
+        qz("t0", a, e, T.xin[:, 4 * a:4 * e], r=["xin%d" % c], w=["t0_%d" % c])
+    counter(0, [("cst", 0), ("cst", 2), ("csh", 0), ("csh", 3)], pa0, "pa0", 1.0)
+    places_first(0)
+    for t in range(R):
+        donor, child = T.cores[(rank + 1 + t) % N], T.cores[(rank - 1 - t) % N]
+        places_rest(t)
+        order(t, donor)
+        candidates(t)
+        leaders(t, child)
+        layer(t, child)
+        if t == 0:
+            iota(T.jrow[:], [[1, C]], 0, 0, ["jrow"])
+            qz("v", 0, 128, T.vt[:], r=["vt"], w=["vq"])
+        if t == R - 1:
+            act(T.elb[:], T.jrow[:].indirect(T.offz[:, 0:28]), AF.Copy, r=["jrow", "offz"], w=["elb"])
+            dma("S", T.el[:], T.elb[0:128:16, :], r=["elb"])
+        own_part(t)
+        state(t, 0, donor)
+        if t < R - 1:
+            places_first(t + 1)
+        state(t, 1, donor)
+    for s, n in total.items():
+        wait("G", (s, n))

@@ -2,18 +2,20 @@ import math
 from concourse.mybir import dt, AluOpType as OP, ActivationFunctionType as AF
 
 C, R, TH = 448, 3, 320
-CUT = [224, 192, 192, 256]
+CUT = [192, 192, 192, 256]
 RUNS = [[(0, k), (k, C)] for k in CUT]
 NS = C // 32
-TILES = [[(s - 1, 0), (s, 1), (s - 2, 0) if s > 1 else None, (s - 1, 1)] for s in (13, 11, 9, 7, 5, 3, 1)] + [[("e", 0), ("e", 1), ("r", 0), (13, 0)]]
 WIDTH = [C, 384, 320, 256, 192, 128, 128, C]
-NE = [7, 4, 4]
-NL = [4, 2, 2]
-NA0 = 2
-NOW = 4
-GM = [False, True, True]
+SMALL = 2.0 ** -10
+PLV = "min0 tr0 u3 u2 x1.0 x1.1 u1.0 xq1 q5 u0 u1.1 min1 q6 tr1 u13 u12 q0 u9 u8 q2 q4 u6 u7.0 q3 eq parts trr q1 q7"
+PLA = "s5.1 s5.0 r5.1 r5.0 x1.2 x1.3 s4.0 s4.1 sum3 sum2 r4.0 r4.1 sum1 s11.0 s11.1 r11.0 r11.1 s10.0 s10.1 r10.0 sum13 r10.1 sum12 s7.1 r7.1 sum9 sum8 sum7 sum6"
+PLP = "sm0 sa0.1 sv0.0 sv0.1 sa0.0 dec1 sm1 sv1.0 sa1.0 sv1.1 sa1.1 rs13 rs12 col0 col5 col6 rs9 rs8 col2 col4 col3 col1 col7"
+CANV = "tab gx0 tr fl dl scan f2 nn0 km"
+CANA = "gx1 dp0 lcp dp1 nn1 dp2 dp3"
 LAYV = "z00 z01 q0 z10 g00 g01 h0 z11 q1 g10 g11 h1"
 LAYA = "z02 z03 z12 g02 g03 z13 g12 g13"
+MIXB, VB, AB = [4, 0], [[5, 6], [1, 2]], [[4, 7], [3, 0]]
+SUMB, RANKB, ORDB = [4, 5, 6], 7, 5
 
 BF, F32, I32, U16, Q, U8 = "bfloat16", "float32", "int32", "uint16", "float8_e4m3fn_x4", "uint8"
 SCRATCH = {"ps": ("psum", [128, 4096], F32)}
@@ -30,20 +32,20 @@ def _mx(name, n):
 
 for _n, _w, _d in [
     ("xin", 4 * C, BF), ("xt", 4 * C, BF), ("ut", 512, BF), ("vt", 512, BF), ("cds", 128, I32), ("cdg", 128, F32), ("cdt", 128, F32),
-    ("off1", 96, U16), ("et", 2048, BF), ("ones", 128, BF), ("cst", 512, BF), ("csh", 512, BF), ("c2", 512, BF),
-    ("pb", 192, F32), ("pc", 192, F32), ("col", 16, F32), ("ib", 64, F32), ("offc", 64, U16), ("ig", 128, BF), ("ia", 128, BF),
-    ("ca", 384, BF), ("cb", 384, BF), ("r32", 32, BF), ("i32w", 32, F32), ("r32b", 32, BF),
-    ("cm0", C, BF), ("cmask", C, BF), ("j0", C, F32), ("jt", C, F32), ("jrow", C, F32), ("dk", 256, F32),
-    ("m1", 2 * C, F32), ("st", 2 * C, F32), ("sg", 16 * C, BF), ("junk", 5824, BF), ("racc", 28, F32), ("rp", C, BF),
-    ("wo", 512, BF), ("tab", C, F32), ("gx", 512, F32), ("ty", 512, F32), ("fl", 512, BF), ("lcp", 256, F32),
-    ("fs", 512, BF), ("nn", 256, I32), ("key", 256, F32), ("km", 256, F32),
+    ("off1", 96, U16), ("et", 520, BF), ("rt", 520, BF), ("ones", 520, BF), ("zer", 520, BF), ("cst", 512, BF), ("csh", 512, BF), ("c2", 512, BF),
+    ("pb", 128, F32), ("pc", 128, F32), ("pi", 8, I32), ("ci", 8, I32), ("cf", 8, F32), ("col", 16, F32), ("ib", 72, F32), ("offc", 72, U16),
+    ("ig", 128, BF), ("ia", 128, BF), ("ca", 384, BF), ("cb", 384, BF), ("b1", 128, BF), ("r32", 32, BF), ("i32w", 32, F32), ("r32b", 32, BF),
+    ("cm0", 320, BF), ("cmask", 320, BF), ("j0", C, F32), ("jt", C, F32), ("jrow", C, F32),
+    ("m1", C, F32), ("st", C, F32), ("sg", 16 * C, BF), ("junk", 5824, BF), ("racc", 28, F32), ("ra", 64, F32), ("rp", C, BF),
+    ("wo", 512, BF), ("tab", C, F32), ("gx", 512, F32), ("ty", 512, F32), ("fl", 512, BF), ("lcp", 256, F32), ("dl", 256, F32), ("l7", 32, F32),
+    ("fs", 512, BF), ("f2", 512, BF), ("nn", 256, F32), ("km", 256, F32),
     ("tmp", 128, F32), ("tp", 32, F32), ("ti", 32, I32), ("tj", 32, I32), ("offz", 32, U16),
     ("dp", 4 * C, BF), ("zt", 4 * C, BF), ("gt", 4 * C, BF), ("yb", C, F32), ("elb", C, F32),
 ]:
     _sb(_n, _w, _d)
 for _i in range(8):
     _sb("k%d" % _i, 4 * WIDTH[_i], BF)
-for _n, _w in [("u", 128), ("ub", 256), ("v", 128), ("wl", 512), ("e", 512), ("cs", 256), ("cc", 128), ("k", sum(WIDTH)), ("od", 128), ("z", C)]:
+for _n, _w in [("u", 128), ("ub", 384), ("v", 128), ("wl", 512), ("e", 512), ("cs", 256), ("rs", 256), ("cc", 128), ("k", sum(WIDTH)), ("od", 128), ("z", C)]:
     _mx(_n, _w)
 for _t in range(R + 1):
     _mx("t%d" % _t, C)
@@ -54,6 +56,16 @@ for _t in range(R):
     _sb("got%d" % _t, 128, BF)
 
 SEMAPHORES = ["qV", "qA", "qP", "qG", "sent"] + ["d%d" % i for i in range(48)] + ["ao%d" % t for t in range(R)] + ["ah%d_%d" % (t, c) for t in range(R) for c in range(2)]
+
+
+def parse(w):
+    k = w.rstrip("0123456789.")
+    n = [int(x) for x in w[len(k):].split(".") if x]
+    return (k, n[0] if n else None, n[1] if len(n) > 1 else None)
+
+
+BY_ACT = [parse(w)[1:] for w in PLA.split() if parse(w)[0] == "s"]
+BY_PE = [parse(w)[1] for w in PLP.split() if parse(w)[0] == "rs"]
 
 
 def rank_program(g, core, T, topo):
@@ -128,6 +140,18 @@ def rank_program(g, core, T, topo):
         total[sem] = n
         wrote[key] = (sem, n)
 
+    def weave(queues, need, run):
+        todo, made = {q: s.split() for q, s in queues.items()}, set()
+        every = set(w for q in todo.values() for w in q)
+        while any(todo.values()):
+            moved = False
+            for q, steps in todo.items():
+                while steps and all(x in made or x not in every for x in need(steps[0])):
+                    run(q, steps[0])
+                    made.add(steps.pop(0))
+                    moved = True
+            assert moved, todo
+
     V, A, P = g.vector, g.scalar, g.tensor
 
     def ps(b, n, a=0, step=1):
@@ -157,6 +181,12 @@ def rank_program(g, core, T, topo):
     def act(out, a, f, kw=None, **k):
         op("A", lambda: A.activation(out, a, f, **(kw or {})), **k)
 
+    def move(q, out, a, **k):
+        if q == "V":
+            cp(out, a, **k)
+        else:
+            act(out, a, AF.Copy, **k)
+
     def qz(name, a, b_, tile, **k):
         op("V", lambda: V.quantize_mx(T[name + "q"][:, a:b_], T[name + "s"][:, a:b_], tile), **k)
 
@@ -167,339 +197,124 @@ def rank_program(g, core, T, topo):
     def iota(out, pat, base, cm, w):
         op("G", lambda: g.iota(out, pat, base, cm, allow_small_or_imprecise_dtypes=True), w=w)
 
-    def sel(out, in_, pat, o, cm, **k):
-        op("G", lambda: g.affine_select(out, in_, pat, o, 0.0, 0, cm), **k)
+    def zero(out, w):
+        iota(out, [[0, out.shape[1]]], 0, 0, w)
 
+    def sel(out, in_, pat, o, cm, base=0, **k):
+        op("G", lambda: g.affine_select(out, in_, pat, o, 0.0, base, cm), **k)
+
+    dma("A", T.ut[:], T.u[:], w=["ut"])
     for c, (a, e) in enumerate(RUNS[0]):
         dma("S", T.xin[:, 4 * a:4 * e], T.x[:, 4 * a:4 * e], w=["xin%d" % c])
-    dma("A", T.ut[:], T.u[:], w=["ut"])
-    iota(T.ib[:, 0:8], [[32, 4], [0, 2]], 0, 0, ["ibU0"])
-    iota(T.ib[:, 8:16], [[32, 4], [0, 2]], 16, 0, ["ibU1"])
-    iota(T.pb[:, 0:32], [[2, 32]], 0, 0, ["pb0"])
-    iota(T.pb[:, 32:64], [[0, 2], [1, 16]], 0, 0, ["pb1"])
-    iota(T.col[:, 0:1], [[0, 1]], 0, 1, ["p"])
-    iota(T.cm0[:], [[0, NS], [2, 32]], -1, 0, ["cm0"])
+    op("G", lambda: g.iota(T.pi[:, 0:1], [[0, 1]], 0, 1), w=["pi"])
+    iota(T.ib[:, 0:24], [[16, 3], [32, 4], [0, 2]], 0, 0, ["ibU"])
+    iota(T.ig[:], [[0, 16], [1, 8]], 0, 0, ["ig"])
+    iota(T.ia[:], [[1, 8], [-100, 2], [0, 8]], 100, 0, ["ia"])
+    iota(T.cm0[:], [[0, 10], [2, 32]], -1, 0, ["cm0"])
+    ms(T.zer[:], 0.0, w=["zer"])
+    act(T.ones[:], T.zer[:], AF.Exp, r=["zer"], w=["ones"])
     ms(T.cds[:], 0, w=["cds"])
-    ms(T.et[:, 0:1024], 0.0, w=["et"])
-    cp(T.offc[:, 0:16], T.ib[:, 0:16], r=["ibU0", "ibU1"], w=["offU"])
-    act(T.ones[:], T.et[:, 0:128], AF.Exp, r=["et"], w=["ones"])
-    act(T.et[:, 1024:2048], T.et[:, 0:1024], AF.Copy, r=["et"], w=["etb"])
-    for i in range(6, -1, -1):
-        n, m = 4 * WIDTH[i], 512 if i == 6 else 256
-        dma("S", T["k%d" % i][:, n - m:n], T.et[:, 0:m], r=["et"], w=["kz%d" % i])
     for a in range(4):
         dma("S", T.cds[32 * a:32 * a + 24, 0:112], T.cd[a::4, :], r=["cds"], w=["cds%d" % a])
-    dma("S", T.c2[:], T.et[:, 0:512], r=["et"], w=["c2z"])
-    dma("S", T.wo[:], T.et[:, 0:512], r=["et"], w=["wo0", "wo1", "wo2", "wo3"])
-    dma("S", T.rp[:], T.et[:, 0:C], r=["et"], w=["rph", "rpl"])
     dma("S", T.wlq[:].bitcast(dt.uint8), T.wc[:], w=["wq"])
     dma("S", T.wls[:], T.ws[:], w=["ws"])
     dma("S", T.vt[:], T.v[:], w=["vt"])
-    tr(T.pc[:, 0:64], T.pb[:, 0:64], r=["pb0", "pb1"], w=["pc01"])
-    l32x2, l16 = T.pc[:, 0:1], T.pc[:, 32:33]
-    pg, pa0, pa1, tie = T.col[:, 1:2], T.col[:, 2:3], T.col[:, 3:4], T.col[:, 5:6]
-    iota(T.ig[:], [[0, 16], [1, 8]], 0, 0, ["ig"])
-    iota(T.ia[:], [[1, 8], [-100, 2], [0, 8]], 100, 0, ["ia"])
-    iota(T.pb[:, 64:96], [[0, 2], [2000, 2], [0, 8]], 0, 0, ["pb2"])
-    for hf in range(2):
-        iota(T.pb[:, 96 + 16 * hf:112 + 16 * hf], [[64, 2], [6, 4], [32, 2]], 0, 0, ["pb3%d" % hf])
-        iota(T.pb[:, 128 + 16 * hf:144 + 16 * hf], [[32, 2], [128, 4], [16, 2]], 0, 0, ["pb4%d" % hf])
-    iota(T.pb[:, 160:192], [[0, 2], [100, 2], [-1, 8]], -100, 0, ["pb5"])
-    iota(T.i32w[:], [[0, 4], [1, 8]], 0, 0, ["i32w"])
+    for i, (sh, m) in enumerate([(5, 3), (4, 7), (0, 1), (1, 15), (3, 1), (0, 31), (0, 15)]):
+        ts(T.ci[:, i:i + 1], T.pi[:, 0:1], sh, OP.logical_shift_right, m, OP.bitwise_and, r=["pi"], w=["ci%d" % i])
+    cp(T.cf[:, 0:7], T.ci[:, 0:7], r=["ci%d" % i for i in range(7)], w=["cf"])
+    run32, pg, odd, half, bit3, l32, l16 = [T.cf[:, i:i + 1] for i in range(7)]
+    pa0, pa1, pr, wr, not31, mix, m4, tie = [T.col[:, i:i + 1] for i in range(8)]
+    cp(T.offc[:, 0:16], T.ib[:, 0:16], r=["ibU"], w=["offU"])
+    ts(mix, odd, 16.0, OP.mult, -32.0, OP.add, r=["cf"], w=["mix"])
+    ts(pa0, run32, 2.0, OP.mult, r=["cf"], w=["pa0"])
+    ts(pa1, run32, 2.0, OP.mult, 1.0, OP.add, r=["cf"], w=["pa1"])
+    ts(pr, run32, 2.0, OP.mult, bit3, OP.add, r=["cf"], w=["pr"])
+    ts(wr, bit3, 1.0 - 1.0 / SMALL, OP.mult, -1.0, OP.add, r=["cf"], w=["wr"])
+    ts(m4, half, 4.0, OP.mult, r=["cf"], w=["m4"])
+    ts(not31, l32, 31.0, OP.not_equal, r=["cf"], w=["not31"])
+    ts(T.offc[:, 16:24], T.ib[:, 16:24], mix, OP.add, r=["ibU", "mix"], w=["offM"])
+    act(T.rt[:], T.zer[:], AF.Copy, r=["zer"], w=["rt"])
 
-    def counter(n, slots, colap, key, sign):
+    def counter(n, out, colap, weight, keys, w):
         x0, x1 = T.ca[:, 128 * n:128 * n + 128], T.cb[:, 128 * n:128 * n + 128]
-        ts(x0, T.ig[:], colap, OP.is_equal, sign, OP.mult, r=["ig", key], w=["ca" + key])
-        ts(x1, T.ia[:], colap, OP.is_equal, sign, OP.mult, r=["ia", key], w=["cb" + key])
-        nm, t = slots[0]
-        first = T[nm][:, t:512:4]
-        tt(first, x0, x1, OP.subtract, r=["ca" + key, "cb" + key], w=["%s%d" % (nm, t)])
-        for nm2, t2 in slots[1:]:
-            sel(T[nm2][:, t2:512:4], first, [[0, 128]], OP.is_ge, 0, r=["%s%d" % (nm, t)], w=["%s%d" % (nm2, t2)])
+        ts(x0, T.ig[:], colap, OP.is_equal, weight, OP.mult, r=["ig"] + keys, w=["ca%d" % n])
+        ts(x1, T.ia[:], colap, OP.is_equal, weight, OP.mult, r=["ia"] + keys, w=["cb%d" % n])
+        return lambda: tt(out, x0, x1, OP.subtract, r=["ca%d" % n, "cb%d" % n], w=[w])
+
+    counters = [counter(0, T.cst[:, 0:512:4], pa0, 1.0, ["pa0"], "cst0"), counter(1, T.b1[:], pa1, 1.0, ["pa1"], "b1"),
+                counter(2, T.csh[:, 1:512:4], pr, wr, ["pr", "wr"], "csh1")]
+    ts(T.cmask[:], T.cm0[:], m4, OP.subtract, -1e28, OP.mult, r=["cm0", "m4"], w=["cmask"])
+    qz("u", 0, 128, T.ut[:], r=["ut"], w=["uq"])
+    ms(T.cmask[:, 31:320:32], 1e28, w=["cmask"])
+    cp(T.ubq[:].bitcast(dt.uint32), T.uq[:].bitcast(dt.uint32).indirect(T.offc[:, 0:24]), r=["uq", "offU", "offM"], w=["ubq"])
+    act(T.ubs[:], T.us[:].indirect(T.offc[:, 0:24]), AF.Copy, r=["uq", "offU", "offM"], w=["ubs"])
+    for c, (a, e) in enumerate(RUNS[0]):
+        qz("t0", a, e, T.xin[:, 4 * a:4 * e], r=["xin%d" % c], w=["t0_%d" % c])
+    for last in counters:
+        last()
+    zero(T.k6[:, 256:512], ["kz6"])
+    zero(T.k6[:, 129:256:2], ["kz6b"])
+    for i in (5, 4):
+        zero(T["k%d" % i][:, 4 * WIDTH[i] - 127:4 * WIDTH[i]:2], ["kz%d" % i])
+    zero(T.racc[:], ["racc0"])
+    sel(T.rt[:, 1:513:2], T.ones[:, 0:256], [[-1, 128], [0, 2]], OP.is_equal, 1, r=["ones"], w=["rt"])
+    sel(T.cst[:, 1:512:4], T.cst[:, 0:512:4], [[0, 128]], OP.is_ge, 0, r=["cst0"], w=["cst1"])
+    for i in (0, 2, 3, 1):
+        zero(T["k%d" % i][:, 4 * WIDTH[i] - 127:4 * WIDTH[i]:2], ["kz%d" % i])
+    zero(T.csh[:, 3:512:4], ["csh3"])
+    iota(T.pb[:, 0:32], [[0, 2], [2000, 2], [0, 8]], 0, 0, ["pb2"])
+    iota(T.pb[:, 96:128], [[0, 2], [100, 2], [-1, 8]], -100, 0, ["pb5"])
+    for hf in range(2):
+        iota(T.pb[:, 32 + 16 * hf:48 + 16 * hf], [[64, 2], [6, 4], [32, 2]], 0, 0, ["pb3%d" % hf])
+        iota(T.pb[:, 64 + 16 * hf:80 + 16 * hf], [[32, 2], [128, 4], [16, 2]], 0, 0, ["pb4%d" % hf])
+    iota(T.i32w[:], [[0, 4], [1, 8]], 0, 0, ["i32w"])
+    zero(T.c2[:], ["c2z"])
+    zero(T.rp[:], ["rp0", "rp1", "rp8", "rp9"])
+    zero(T.k7[:, 3:4 * C:4], ["kz7"])
+    zero(T.wo[:], ["wo0", "wo1", "wo2", "wo3"])
+    iota(T.j0[:], [[32 * 513, NS], [2, 16], [513, 2]], -512, 0, ["j0"])
+
+    def constants_0():
+        for t in (2, 3):
+            act(T.cst[:, t:512:4], T.b1[:], AF.Copy, {"scale": 1.0 / SMALL}, r=["b1"], w=["cst%d" % t])
+        act(T.csh[:, 0:512:4], T.cst[:, 0:512:4], AF.Identity, {"scale": not31}, r=["cst0", "not31"], w=["csh0"])
+        act(T.csh[:, 2:512:4], T.b1[:], AF.Identity, {"scale": not31}, r=["b1", "not31"], w=["csh2"])
 
     def constants_1():
-        counter(1, [("cst", 1), ("cst", 3), ("csh", 1)], pa1, "pa1", 1.0)
-        counter(2, [("csh", 2)], pg, "pg", -1.0)
-        tr(T.pc[:, 64:192], T.pb[:, 64:192], r=["pb2", "pb30", "pb31", "pb40", "pb41", "pb5"], w=["pc2"])
-        ts(T.col[:, 4:5], T.pc[:, 160:161], pg, OP.add, 0.5, OP.min, r=["pc2", "pg"], w=["tie0"])
-        ts(T.r32[:], T.i32w[:], pg, OP.is_equal, r=["i32w", "pg"], w=["r32"])
-        ts(T.r32b[:], T.i32w[:], -1.0, OP.add, pg, OP.is_equal, r=["i32w", "pg"], w=["r32b"])
-        ts(tie, T.col[:, 4:5], -0.5, OP.max, r=["tie0"], w=["tie"])
-        ts(T.r32b[:, 0:32:8], T.i32w[:, 0:32:8], 7.0, OP.add, pg, OP.is_equal, r=["i32w", "pg"], w=["r32b"])
+        for o in range(2):
+            qz("rs", 128 * o, 128 * o + 128, T.rt[:, 1 - o:513 - o], r=["rt"], w=["rs%d" % o])
+        qz("cs", 0, 128, T.cst[:], r=["cst%d" % t for t in range(4)], w=["cs"])
+
+    def constants_2():
+        tr(T.pc[:], T.pb[:], r=["pb2", "pb30", "pb31", "pb40", "pb41", "pb5"], w=["pc"])
+        ts(T.r32[:], T.i32w[:], pg, OP.is_equal, r=["i32w", "cf"], w=["r32"])
+        ts(T.r32b[:], T.i32w[:], -1.0, OP.add, pg, OP.is_equal, r=["i32w", "cf"], w=["r32b"])
+        ts(T.col[:, 8:9], T.pc[:, 96:97], pg, OP.add, 0.5, OP.min, r=["pc", "cf"], w=["tie0"])
+        ts(T.r32b[:, 0:32:8], T.i32w[:, 0:32:8], 7.0, OP.add, pg, OP.is_equal, r=["i32w", "cf"], w=["r32b"])
+        ts(tie, T.col[:, 8:9], -0.5, OP.max, r=["tie0"], w=["tie"])
         tt(T.r32[:], T.r32[:], T.r32b[:], OP.subtract, r=["r32b"], w=["r32"])
         iota(T.r32[:, 0:32:16], [[0, 2]], -8, 0, ["r32"])
         for b in range(4):
             sel(T.c2[:, 129 * b:128 * b + 128:4], T.r32[:], [[0, 32]], OP.is_ge, 0, r=["r32", "c2z"], w=["c2r%d" % b])
-        iota(T.racc[:, 0:2], [[0, 2]], 0, 0, ["racc0"])
-        iota(T.ib[:, 16:24], [[56, 2], [16, 2], [28, 2]], 0, 0, ["ibA"])
-        iota(T.ib[:, 24:32], [[1, 8]], 0, 0, ["ibB"])
-        iota(T.ib[:, 32:48], [[1, 8], [64, 2]], 0, 0, ["ibL"])
-        iota(T.ib[:, 48:64], [[1, 8], [64, 2]], 8, 0, ["ibN"])
-        iota(T.j0[:], [[32 + 512 * 32, NS], [1, 32]], -512, 0, ["j0"])
-        for b in range(4):
-            sel(T.et[:, 512 * b + b:512 * b + 512:4], T.ones[:], [[-1, 128]], OP.is_equal, 1, r=["ones", "etb"], w=["et"] if b == 0 else ["et%d" % b])
-        iota(T.dk[:], [[0, 256]], 0, 0, ["dk"])
-        iota(T.dk[:, 0:256:8], [[0, 32]], -1000, 0, ["dk"])
+        iota(T.ib[:, 24:32], [[56, 2], [16, 2], [28, 2]], 0, 0, ["ibA"])
+        iota(T.ib[:, 32:40], [[1, 8]], 0, 0, ["ibB"])
+        iota(T.ib[:, 40:56], [[1, 8], [64, 2]], 0, 0, ["ibL"])
+        iota(T.ib[:, 56:72], [[1, 8], [64, 2]], 8, 0, ["ibN"])
+        sel(T.et[:, 0:516], T.ones[:, 0:516], [[-1, 516]], OP.is_equal, 4, 3, r=["ones"], w=["et"])
 
-    def constants_2():
-        qz("cs", 0, 128, T.cst[:], r=["cst%d" % t for t in range(4)], w=["cs"])
+    def constants_3():
         qz("cs", 128, 256, T.csh[:], r=["csh%d" % t for t in range(4)], w=["csh"])
         qz("cc", 0, 128, T.c2[:], r=["c2r%d" % b for b in range(4)], w=["cc"])
-        act(T.jt[:], T.j0[:], AF.Identity, {"scale": 2.0 ** -9, "bias": T.pc[:, 64:65]}, r=["j0", "pc2"], w=["jt"])
 
     def lists_of_candidates():
-        for nm, a, b_, c in (("A", 16, 24, 32), ("B", 24, 32, 96), ("L", 32, 48, 128), ("N", 48, 64, 128)):
-            ts(T.offc[:, a:b_], T.ib[:, a:b_], T.pc[:, c:c + 1], OP.add, r=["ib" + nm, "pc01", "pc2"], w=["off" + nm])
-        cp(T.cdg[:], T.cds[:].indirect(T.offc[:, 16:24]), r=["offA"] + ["cds%d" % a for a in range(4)], w=["cdg"])
+        for nm, a, b_, c in (("A", 24, 32, l16), ("B", 32, 40, T.pc[:, 32:33]), ("L", 40, 56, T.pc[:, 64:65]), ("N", 56, 72, T.pc[:, 64:65])):
+            ts(T.offc[:, a:b_], T.ib[:, a:b_], c, OP.add, r=["ib" + nm, "cf", "pc"], w=["off" + nm])
+        cp(T.cdg[:], T.cds[:].indirect(T.offc[:, 24:32]), r=["offA"] + ["cds%d" % a for a in range(4)], w=["cdg"])
         tr(T.cdt[:], T.cdg[:], r=["cdg"], w=["cdt"])
-        cp(T.off1[:], T.cdt[:].indirect(T.offc[:, 24:30]), r=["cdt", "offB"], w=["off1"])
-
-    koff = [sum(WIDTH[:i]) for i in range(8)]
-    where = {u: (i, t) for i, tl in enumerate(TILES) for t, u in enumerate(tl) if u}
-    joff = {}
-    for s in range(1, NS):
-        for h in range(2):
-            joff[(s, h)] = sum(32 * a[0] for a in joff)
-    by_act, early, late, act_early, act_late, CH, gm = [], [], [], [], [], [], [False]
-
-    def plan(t):
-        CH[:] = RUNS[t]
-        k = CUT[t] // 32
-        e = [(s, h) for s in range(k - 1, -1, -1) for h in range(2)]
-        l = [(s, h) for s in range(NS - 1, k - 1, -1) for h in range(2)]
-        act_early[:], early[:], act_late[:], late[:] = e[:NE[t]], e[NE[t]:], l[:NL[t]], l[NL[t]:]
-        by_act[:] = act_early + act_late
-        gm[0] = GM[t]
-
-    def slot(u, a, n):
-        i, t = where[u]
-        return T["k%d" % i][:, 4 * a + t:4 * n:4]
-
-    def ukey(u):
-        return "u%s_%d" % u
-
-    def zkey(u):
-        i = where[u][0]
-        return ["kz%d" % i] if i < 7 else []
-
-    def run_of(u):
-        return 0 if 32 * u[0] < CH[0][1] else 1
-
-    def sbank(c, h, q):
-        return (4 if c == 0 else 0) + h + (2 if q == "A" else 0)
-
-    def scores(t, c):
-        tn = "t%d" % t
-        for h, q in ((0, "V"), (1, "V"), (0, "A"), (1, "A")):
-            mm(sbank(c, h, q), "ub", 128 * h, tn, 0, CH[c][1], True, True, [tn + "_%d" % i for i in range(c + 1)] + ["ubq", "ubs"])
-
-    def prelim(c, h):
-        a, e = CH[c]
-        b = sbank(c, h, "V")
-        if gm[0]:
-            tr(T.st[:, C * h + a:C * h + e], ps(b, e, a), w=["st%d%d" % (c, h)], b=[b])
-        else:
-            tt(T.m1[:, C * h + a:C * h + e], ps(b, e, a), T.cmask[:, a:e], OP.min, r=["cmask"], w=["m1%d%d" % (c, h)], b=[b])
-            tr(T.st[:, C * h + a:C * h + e], T.m1[:, C * h + a:C * h + e], r=["m1%d%d" % (c, h)], w=["st%d%d" % (c, h)])
-
-    def sc(u):
-        c = C * u[1] + 32 * u[0] + 31
-        return T.st[:, c:c + 1]
-
-    def stk(u):
-        return ["st%d%d" % (run_of(u), u[1])]
-
-    def v_unit(u):
-        n, b = 32 * u[0] + 32, sbank(run_of(u), u[1], "V")
-        ts(slot(u, 0, n), ps(b, n), sc(u), OP.is_lt, r=stk(u) + zkey(u), w=[ukey(u), ukey(u) + "d"], b=[b])
-
-    def v_eq(c, h):
-        a, e = CH[c]
-        b = sbank(c, h, "V")
-        tt(slot(("e", h), a, e), ps(b, e, a), T.st[:, C * h + a:C * h + e], OP.is_equal, r=["st%d%d" % (c, h)], w=["ue%d%d%d" % (c, h, i) for i in range(4)], b=[b])
-        for i in range(4 if gm[0] else 0):
-            view = T.k7[32 * i:32 * i + 32, 4 * a + h:4 * e:4]
-            wait("G", ("qG", total["qG"]))
-            sel(view, view, [[0, (e - a) // 32], [1, 32]], OP.is_ge, -1, w=["ue%d%d%d" % (c, h, i)])
-
-    def acc(u):
-        c = 2 * u[0] + u[1]
-        return T.racc[:, c:c + 1]
-
-    def a_sum(u):
-        n = 32 * u[0]
-        if n:
-            act(T.junk[:, joff[u]:joff[u] + n], slot(u, 0, n), AF.Copy, {"accum_out": acc(u)}, r=[ukey(u)], w=["racc" + ukey(u), "junk" + ukey(u)])
-
-    def a_one(u):
-        i, n, b = by_act.index(u), 32 * u[0] + 32, sbank(run_of(u), u[1], "A")
-        act(T.sg[:, C * i:C * i + n], ps(b, n), AF.Sign, {"bias": sc(u), "scale": -1.0}, r=stk(u), w=["sg%d" % i], b=[b])
-
-    def a_two(u):
-        i, n = by_act.index(u), 32 * u[0]
-        act(slot(u, 0, n), T.sg[:, C * i:C * i + n], AF.Relu, {"accum_out": acc(u)}, r=["sg%d" % i] + zkey(u), w=[ukey(u), "racc" + ukey(u)])
-        act(slot(u, n, n + 32), T.sg[:, C * i + n:C * i + n + 32], AF.Relu, r=["sg%d" % i] + zkey(u), w=[ukey(u) + "d"])
-
-    def a_made(us):
-        for k, u in enumerate(us):
-            if k == 0:
-                a_one(u)
-            if k + 1 < len(us):
-                a_one(us[k + 1])
-            a_two(u)
-
-    def v_q(i):
-        keys = []
-        for u in TILES[i]:
-            if u and u[0] == "e":
-                keys += ["ue%d%d%d" % (c, u[1], x) for c in range(2) for x in range(4)]
-            elif u:
-                keys += [ukey(u)] + ([ukey(u) + "d"] if u[0] != "r" else []) + zkey(u)
-        qz("k", koff[i], koff[i] + WIDTH[i], T["k%d" % i][:], r=keys, w=["kq%d" % i])
-
-    def places_first(t):
-        plan(t)
-        scores(t, 0)
-        prelim(0, 0)
-        prelim(0, 1)
-        a_made(act_early[:NA0])
-        v_eq(0, 0)
-        v_eq(0, 1)
-        for u in early[:NOW]:
-            v_unit(u)
-
-    def places_rest(t):
-        scores(t, 1)
-        if t == 0:
-            constants_1()
-        for u in early[NOW:]:
-            v_unit(u)
-        a_made(act_early[NA0:])
-        prelim(1, 0)
-        prelim(1, 1)
-        v_eq(1, 0)
-        v_eq(1, 1)
-        for u in early:
-            a_sum(u)
-        a_made(act_late)
-        for u in late:
-            v_unit(u)
-        for u in late:
-            a_sum(u)
-        if t == 0:
-            constants_2()
-        for i in (6, 5, 4, 0, 1, 2, 3):
-            v_q(i)
-        rk = ["racc0"] + ["racc" + ukey((s, h)) for s in range(1, NS) for h in range(2)]
-        big = 1.5 * 2.0 ** 28
-        ts(T.rp[:, 0:C:16], T.racc[:], big, OP.add, big, OP.subtract, r=rk, w=["rph"])
-        tt(T.rp[:, 1:C:16], T.racc[:], T.rp[:, 0:C:16], OP.subtract, r=rk + ["rph"], w=["rpl"])
-        tr(slot(("r", 0), 0, C), T.rp[:], r=["rph", "rpl"], w=[ukey(("r", 0))])
-        v_q(7)
-        for i in range(8):
-            mm(4, "cs", 128 if i == 7 else 0, "k", koff[i], koff[i] + WIDTH[i], i == 0, i == 7, ["kq%d" % i, "csh" if i == 7 else "cs"])
-
-    def order(t, donor):
-        for a in range(4):
-            ts(T.wo[:, 128 * a:128 * a + 112], ps(4, C, a, 4), tie, OP.is_lt, r=["tie"], w=["wo%d" % a], b=[4])
-        qz("od", 0, 128, T.wo[:], r=["wo%d" % a for a in range(4)], w=["oq"])
-        mm(5, "od", 0, "cc", 0, 128, True, True, ["oq", "cc"])
-        act(T["ord%d" % t][:], ps(5, 128), AF.Exp, {"scale": math.log(2.0)}, w=["ord%d" % t], b=[5])
-        send(T["got%d" % t][:], T["ord%d" % t][:], "ao%d" % t, donor, ["ord%d" % t])
-
-    def candidates(t):
-        tn = "t%d" % t
-        tt(T.tab[:], ps(4, C), T.jt[:], OP.add, r=["jt"], w=["tab"], b=[4])
-        if t == 0:
-            for b in range(4):
-                qz("e", 128 * b, 128 * b + 128, T.et[:, 512 * b:512 * b + 512], r=["et", "et%d" % b], w=["eq%d" % b])
-            lists_of_candidates()
-        for b in range(4):
-            mm(b, "e", 128 * b, tn, 0, C, True, True, [tn + "_0", tn + "_1", "eq%d" % b])
-        act(T.gx[:, 256:512], T.tab[:].indirect(T.off1[:, 32 * t + 16:32 * t + 32]), AF.Copy, r=["tab", "off1"], w=["gx1"])
-        cp(T.gx[:, 0:256], T.tab[:].indirect(T.off1[:, 32 * t:32 * t + 16]), r=["tab", "off1"], w=["gx0"])
-        tr(T.ty[:], T.gx[:], r=["gx0", "gx1"], w=["ty"])
-        ts(T.fl[:], T.ty[:], float(TH), OP.is_lt, r=["ty"], w=["fl"])
-        for b in range(2):
-            act(T.dp[:, C * b:C * b + C], ps(b, C), AF.Copy, w=["dp%d" % b], b=[b])
-        act(T.lcp[:], T.ty[:].indirect(T.offc[:, 32:48]), AF.Copy, {"scale": 2.0 ** -9}, r=["ty", "offL"], w=["lcp"])
-        for b in range(2, 4):
-            act(T.dp[:, C * b:C * b + C], ps(b, C), AF.Copy, w=["dp%d" % b], b=[b])
-
-    def leaders(t, child):
-        got = T["got%d" % t]
-        gk = "got%d" % t
-        arrives(gk, "ao%d" % t, width(child, core))
-        for i in range(4):
-            scan(T.fs[:, 128 * i:128 * i + 128], got[:], T.fl[:, 128 * i:128 * i + 128], OP.mult, OP.add, r=[gk, "fl"], w=["fs%d" % i])
-        ts(T.nn[:], T.fs[:].indirect(T.offc[:, 48:64]), 0.5, OP.mult, -63.5 + 2.0 ** -10, OP.add, r=["fs%d" % i for i in range(4)] + ["offN"], w=["nn"])
-        tt(T.key[:], T.nn[:], T.lcp[:], OP.subtract, r=["nn", "lcp"], w=["key"])
-        scan(T.km[:], T.dk[:], T.key[:], OP.add, OP.max, r=["dk", "key"], w=["km"])
-        for a in range(4):
-            args = (T.tmp[0:32, a:128:4], T.km[32 * a:32 * a + 32, 7:256:8])
-            if a >= 2:
-                act(*args, AF.Copy, {"scale": -2.0 ** 18}, r=["km"], w=["tmp%d" % a])
-            else:
-                ts(*args, -2.0 ** 18, OP.mult, r=["km"], w=["tmp%d" % a])
-        for b in range(4):
-            tr(T.tp[32 * b:32 * b + 32, :], T.tmp[0:32, 32 * b:32 * b + 32], r=["tmp%d" % a for a in range(4)], w=["tp%d" % b])
-        cp(T.ti[:], T.tp[:], r=["tp%d" % b for b in range(4)], w=["ti"])
-        ts(T.tj[:], T.ti[:], 511, OP.bitwise_and, r=["ti"], w=["tj"])
-        cp(T.offz[:], T.tj[:], r=["tj"], w=["offz"])
+        cp(T.off1[:], T.cdt[:].indirect(T.offc[:, 32:38]), r=["cdt", "offB"], w=["off1"])
 
     def banks(c):
         return 4 * ((c + 1) % 2)
-
-    def layer(t, child):
-        hn = "h%d" % t
-        runs = RUNS[t + 1]
-
-        def z(c, b, onv):
-            a, e = runs[c]
-            args = (T.zt[:, 4 * a + b:4 * e:4], T.dp[:, C * b:C * b + C].indirect(T.offz[:, a // 16:e // 16]))
-            k = {"r": ["offz", "dp%d" % b], "w": ["z%d_%d" % (c, b)]}
-            if onv:
-                cp(*args, **k)
-            else:
-                act(*args, AF.Copy, **k)
-
-        def zq(c):
-            a, e = runs[c]
-            qz("z", a, e, T.zt[:, 4 * a:4 * e], r=["z%d_%d" % (c, b) for b in range(4)], w=["zq%d" % c])
-            for b in (0, 2, 1, 3):
-                mm(banks(c) + b, "wl", 128 * b, "z", a, e, True, True, ["zq%d" % c, "wq", "ws"])
-
-        def gv(c, b, onv):
-            a, e = runs[c]
-            k = {"w": ["g%d_%d" % (c, b)], "b": [banks(c) + b]}
-            if onv:
-                ts(T.gt[:, 4 * a + b:4 * e:4], ps(banks(c) + b, e - a), 0.0, OP.max, 0.015625, OP.mult, **k)
-            else:
-                act(T.gt[:, 4 * a + b:4 * e:4], ps(banks(c) + b, e - a), AF.Relu, {"scale": 0.015625}, **k)
-
-        def hq(c):
-            a, e = runs[c]
-            qz(hn, a, e, T.gt[:, 4 * a:4 * e], r=["g%d_%d" % (c, b) for b in range(4)], w=[hn + "_%d" % c])
-            sem = "ah%d_%d" % (t, c)
-            send(T["l%dq" % t][:, a:e].bitcast(dt.uint8), T[hn + "q"][:, a:e].bitcast(dt.uint8), sem, child, [hn + "_%d" % c])
-            send(T["l%ds" % t][:, a:e], T[hn + "s"][:, a:e], sem, child, [hn + "_%d" % c])
-
-        todo, made = {True: LAYV.split(), False: LAYA.split()}, set()
-        while todo[True] or todo[False]:
-            for onv in (False, True):
-                while todo[onv]:
-                    w = todo[onv][0]
-                    c = int(w[1])
-                    need = {"z": [], "g": ["q%d" % c], "q": ["z%d%d" % (c, b) for b in range(4)], "h": ["g%d%d" % (c, b) for b in range(4)]}[w[0]]
-                    if not all(x in made for x in need):
-                        break
-                    if w[0] == "z":
-                        z(c, int(w[2]), onv)
-                    elif w[0] == "g":
-                        gv(c, int(w[2]), onv)
-                    else:
-                        (zq if w[0] == "q" else hq)(c)
-                    made.add(todo[onv].pop(0))
 
     def own_part(t):
         tn = "t%d" % t
@@ -507,42 +322,268 @@ def rank_program(g, core, T, topo):
             for b in range(4):
                 mm(banks(c) + b, "e", 128 * b, tn, a, e, True, False, [tn + "_0", tn + "_1"])
 
-    def state(t, c, donor):
-        ln, nx = "l%d" % t, "t%d" % (t + 1)
-        a, e = RUNS[t + 1][c]
-        arrives(ln + "_%d" % c, "ah%d_%d" % (t, c), 2 * width(donor, core))
-        for b in (0, 2, 1, 3):
-            mm(banks(c) + b, "e", 128 * b, ln, a, e, False, True, [ln + "_%d" % c])
-        for b in (2, 3):
-            act(T.xt[:, 4 * a + b:4 * e:4], ps(banks(c) + b, e - a), AF.Copy, w=["x%d_%d" % (c, b)], b=[banks(c) + b])
-        for b in (0, 1):
-            cp(T.xt[:, 4 * a + b:4 * e:4], ps(banks(c) + b, e - a), w=["x%d_%d" % (c, b)], b=[banks(c) + b])
-        qz(nx, a, e, T.xt[:, 4 * a:4 * e], r=["x%d_%d" % (c, b) for b in range(4)], w=[nx + "_%d" % c])
-        if t == R - 1:
-            mm(banks(c), "v", 0, nx, a, e, True, True, [nx + "_%d" % c, "vq"])
-            dma("S", T.oc[:, 4 * a:4 * e], T[nx + "q"][:, a:e].bitcast(dt.uint8), r=[nx + "_%d" % c])
-            for k in range(4):
-                dma("AS"[k % 2], T.osc[4 * k:4 * k + 4, a:e], T[nx + "s"][32 * k:32 * k + 4, a:e], r=[nx + "_%d" % c])
-            cp(T.yb[:, a:e], ps(banks(c), e - a), w=["yb%d" % c], b=[banks(c)])
-            dma("A", T.y[:, a:e], T.yb[:, a:e], r=["yb%d" % c])
+    def state(step, t, c, q="V", b=0):
+        ln, nx = "l%d" % (t - 1), "t%d" % t
+        a, e = RUNS[t][c]
+        if t == 0:
+            return
+        if step == "dec":
+            arrives(ln + "_%d" % c, "ah%d_%d" % (t - 1, c), 2 * width(T.cores[(rank + t) % N], core))
+            for b in (0, 2, 1, 3):
+                mm(banks(c) + b, "e", 128 * b, ln, a, e, False, True, [ln + "_%d" % c])
+        elif step == "x":
+            move(q, T.xt[:, 4 * a + b:4 * e:4], ps(banks(c) + b, e - a), w=["x%d_%d" % (c, b)], b=[banks(c) + b])
+        else:
+            qz(nx, a, e, T.xt[:, 4 * a:4 * e], r=["x%d_%d" % (c, b) for b in range(4)], w=[nx + "_%d" % c])
 
-    ts(pg, T.col[:, 0:1], l16, OP.subtract, 1.0 / 16, OP.mult, r=["p", "pc01"], w=["pg"])
-    ts(T.col[:, 6:7], T.col[:, 0:1], 2.0, OP.mult, l32x2, OP.subtract, r=["p", "pc01"], w=["p2"])
-    ts(pa0, T.col[:, 6:7], 1.0 / 32, OP.mult, r=["p2"], w=["pa0"])
-    ts(pa1, T.col[:, 6:7], 1.0 / 32, OP.mult, 1.0, OP.add, r=["p2"], w=["pa1"])
-    ts(T.cmask[:], T.cm0[:], l32x2, OP.subtract, -1e28, OP.mult, r=["cm0", "pc01"], w=["cmask"])
-    qz("u", 0, 128, T.ut[:], r=["ut"], w=["uq"])
-    cp(T.ubq[:].bitcast(dt.uint32), T.uq[:].bitcast(dt.uint32).indirect(T.offc[:, 0:16]), r=["uq", "offU"], w=["ubq"])
-    act(T.ubs[:], T.us[:].indirect(T.offc[:, 0:16]), AF.Copy, r=["uq", "offU"], w=["ubs"])
-    for c, (a, e) in enumerate(RUNS[0]):
-        qz("t0", a, e, T.xin[:, 4 * a:4 * e], r=["xin%d" % c], w=["t0_%d" % c])
-    counter(0, [("cst", 0), ("cst", 2), ("csh", 0), ("csh", 3)], pa0, "pa0", 1.0)
-    places_first(0)
+    def whole_state(t, c):
+        state("dec", t, c)
+        for b in range(4):
+            state("x", t, c, "VVAA"[b], b)
+        state("xq", t, c)
+
+    koff = [sum(WIDTH[:i]) for i in range(8)]
+
+    def tile_of(s):
+        return (NS - 1 - s) // 2
+
+    def slot(s, h, a, n, step=4):
+        return T["k%d" % tile_of(s)][:, 4 * a + 2 * h + 1 - s % 2:4 * n:step]
+
+    def ukeys(s, h):
+        return ["u%d_%d" % (s, h), "u%d_%dd" % (s, h)]
+
+    def acc(s, which):
+        return T.racc[:, 2 * s + which:2 * s + which + 1]
+
+    def junk(s, n):
+        return T.junk[:, 32 * s * (s - 1):32 * s * (s - 1) + n]
+
+    def pieces(s):
+        m = 32 * s
+        k = m // 128
+        return [0] + [m - 2 * (m // 2 // k) * x for x in range(k - 1, -1, -1)]
+
+    def places(t):
+        tn, CH = "t%d" % t, RUNS[t]
+        cut = CUT[t] // 32
+
+        def made(blocks):
+            return [x % (s, h) for s in blocks for h in range(2) for x in ("u%d.%d", "r%d.%d")] + ["u%d" % s for s in blocks]
+
+        early = made(range(cut))
+
+        def need(w):
+            k, n, h = parse(w)
+            c = int(n is not None and n >= cut)
+            if k in ("u", "s"):
+                return ["tr%d" % c] + ["s%s%d.%d" % ("v" if k == "u" else "a", c, x) for x in range(2) if h in (None, x)]
+            if k in ("sm", "sv", "sa"):
+                return ["xq%d" % n] + (["min%d" % n] if k == "sa" and AB[n][h] == MIXB[n] else [])
+            if k == "rs":
+                return ["q%d" % tile_of(n)] + ["sum%d" % s for s in BY_PE[:max(0, BY_PE.index(n) + 1 - len(SUMB))]] + early
+            if k == "q":
+                return made([NS - 1 - 2 * n, NS - 2 - 2 * n]) if n < 7 else ["trr", "eq"]
+            return {"x": ["dec1"], "xq": ["x1.%d" % b for b in range(4)], "min": ["sm%s" % n], "tr": ["min%s" % n], "r": ["s%s.%s" % (n, h)],
+                    "eq": ["tr0", "tr1", "sv1.0", "sv1.1"], "sum": ["rs%s" % n] + made([n or 0]), "col": ["q%s" % n] + early,
+                    "parts": ["sum%d" % s for s in range(NS)] + made(range(NS)), "trr": ["parts"]}.get(k, [])
+
+        def unit_in(s, h, bk):
+            c = int(s >= cut)
+            return bk[c][h], T.st[:, 32 * s + 30 + h:32 * s + 31 + h], ["st%d" % c], 32 * s + 32
+
+        def run(q, w):
+            k, n, h = parse(w)
+            if k in ("x", "xq", "dec"):
+                state(k, t, n, q, h)
+            elif k == "k":
+                [constants_0, constants_1, constants_2, constants_3][n]()
+            elif k == "jt":
+                act(T.jt[:], T.j0[:], AF.Identity, {"scale": 2.0 ** -9, "bias": T.pc[:, 0:1]}, r=["j0", "pc"], w=["jt"])
+            elif k in ("sm", "sv", "sa"):
+                a, e = CH[n]
+                keys = [tn + "_%d" % i for i in range(n + 1)] + ["ubq", "ubs"]
+                if k == "sm":
+                    mm(MIXB[n], "ub", 256, tn, a, e, True, True, keys)
+                else:
+                    mm((VB if k == "sv" else AB)[n][h], "ub", 128 * h, tn, 0, e, True, True, keys)
+            elif k == "min":
+                a, e = CH[n]
+                tt(T.m1[:, a:e], ps(MIXB[n], e - a), T.cmask[:, 0:e - a], OP.min, r=["cmask"], w=["m1%d" % n], b=[MIXB[n]])
+            elif k == "tr":
+                a, e = CH[n]
+                tr(T.st[:, a:e], T.m1[:, a:e], r=["m1%d" % n], w=["st%d" % n])
+            elif k == "eq":
+                for h in range(2):
+                    for o in range(2):
+                        tt(T.k7[:, 4 * o + 2 * h:4 * C:8], ps(VB[1][h], C, o, 2), T.st[:, h:C:2], OP.is_equal,
+                           r=["st0", "st1"], w=["ue%d%d" % (h, o)], b=[VB[1][h]])
+            elif k == "u":
+                for h in range(2) if h is None else [h]:
+                    b, sc, keys, m = unit_in(n, h, VB)
+                    ts(slot(n, h, 0, m), ps(b, m), sc, OP.is_lt, [1.0, SMALL][h], OP.mult, r=keys, w=ukeys(n, h), b=[b])
+            elif k == "s":
+                b, sc, keys, m = unit_in(n, h, AB)
+                i = BY_ACT.index((n, h))
+                act(T.sg[:, C * i:C * i + m], ps(b, m), AF.Sign, {"bias": sc, "scale": -1.0}, r=keys, w=["sg%d" % i], b=[b])
+            elif k == "r":
+                i, m = BY_ACT.index((n, h)), 32 * n
+                kw, keys = {"scale": [1.0, SMALL][h]}, ["sg%d" % i]
+                if n in BY_PE or n == 0:
+                    act(slot(n, h, 0, m + 32), T.sg[:, C * i:C * i + m + 32], AF.Relu, kw, r=keys, w=ukeys(n, h))
+                else:
+                    act(slot(n, h, 0, m), T.sg[:, C * i:C * i + m], AF.Relu, dict(kw, accum_out=acc(n, h)), r=keys + ["racc0"], w=[ukeys(n, h)[0], "racc%d_%d" % (n, h)])
+                    act(slot(n, h, m, m + 32), T.sg[:, C * i + m:C * i + m + 32], AF.Relu, kw, r=keys, w=[ukeys(n, h)[1]])
+            elif k == "q":
+                keys = ["kz%d" % n, "kz%db" % n]
+                if n < 7:
+                    keys += [x for s in (NS - 1 - 2 * n, NS - 2 - 2 * n) for h in range(2) for x in ukeys(s, h)]
+                else:
+                    keys += ["ur"] + ["ue%d%d" % (h, o) for h in range(2) for o in range(2)]
+                qz("k", koff[n], koff[n] + WIDTH[n], T["k%d" % n][:], r=keys, w=["kq%d" % n])
+            elif k == "rs":
+                i, ends, b = tile_of(n), pieces(n), SUMB[BY_PE.index(n) % len(SUMB)]
+                for x in range(len(ends) - 1):
+                    mm(b, "rs", 128 * (1 - n % 2), "k", koff[i] + ends[x], koff[i] + ends[x + 1], x == 0, x == len(ends) - 2, ["kq%d" % i, "rs0", "rs1"])
+            elif k == "sum":
+                m = 32 * n
+                mine = [h for h in range(2) if (n, h) not in BY_ACT]
+                if n in BY_PE:
+                    m, b = pieces(n)[1], SUMB[BY_PE.index(n) % len(SUMB)]
+                    act(junk(n, m), ps(b, m), AF.Copy, {"accum_out": acc(n, 0)}, r=["racc0"], w=["racc%d_0" % n, "junk%d" % n], b=[b])
+                elif len(mine) == 2:
+                    act(junk(n, 2 * m), slot(n, 0, 0, m, 2), AF.Copy, {"accum_out": acc(n, 0)}, r=["racc0", ukeys(n, 0)[0], ukeys(n, 1)[0]], w=["racc%d_0" % n, "junk%d" % n])
+                else:
+                    act(junk(n, m), slot(n, mine[0], 0, m), AF.Copy, {"accum_out": acc(n, mine[0])}, r=["racc0", ukeys(n, mine[0])[0]], w=["racc%d_%d" % (n, mine[0]), "junk%d" % n])
+            elif k == "parts":
+                rk = ["racc0"] + ["racc%d_%d" % (s, h) for s in range(NS) for h in range(2)]
+                whole, fine = T.ra[:, 0:28], T.ra[:, 32:60]
+                for out, e, key in ((T.rp[:, 0:C:16], 28, "rp0"), (whole, 23, "whole"), (fine, 18, "fine")):
+                    ts(out, T.racc[:], 1.5 * 2.0 ** e, OP.add, 1.5 * 2.0 ** e, OP.subtract, r=rk, w=[key])
+                tt(T.rp[:, 1:C:16], whole, T.rp[:, 0:C:16], OP.subtract, r=["whole", "rp0"], w=["rp1"])
+                tt(T.rp[:, 8:C:16], fine, whole, OP.subtract, r=["whole", "fine"], w=["rp8"])
+                tt(T.rp[:, 9:C:16], T.racc[:], fine, OP.subtract, r=rk + ["fine"], w=["rp9"])
+            elif k == "trr":
+                tr(T.k7[:, 1:4 * C:4], T.rp[:], r=["rp0", "rp1", "rp8", "rp9"], w=["ur"])
+            else:
+                mm(RANKB, "cs", 128 if n == 7 else 0, "k", koff[n], koff[n] + WIDTH[n], n == 0, n == 7, ["kq%d" % n, "csh" if n == 7 else "cs"])
+
+        plv, pla = PLV, PLA
+        if t == 0:
+            plv = plv.replace("q0", "k1 q0").replace("q2", "k2 q2").replace("parts", "k3 parts")
+            pla = "k0 " + pla + " jt"
+        weave({"P": PLP, "V": plv, "A": pla}, need, run)
+
+    def order(t, donor):
+        for a in range(4):
+            ts(T.wo[:, 128 * a:128 * a + 112], ps(RANKB, C, a, 4), tie, OP.is_lt, r=["tie"], w=["wo%d" % a], b=[RANKB])
+        qz("od", 0, 128, T.wo[:], r=["wo%d" % a for a in range(4)], w=["oq"])
+        mm(ORDB, "od", 0, "cc", 0, 128, True, True, ["oq", "cc"])
+        act(T["ord%d" % t][:], ps(ORDB, 128), AF.Exp, {"scale": math.log(2.0)}, w=["ord%d" % t], b=[ORDB])
+        send(T["got%d" % t][:], T["ord%d" % t][:], "ao%d" % t, donor, ["ord%d" % t])
+
+    def leaders(t, child):
+        tn, got, gk = "t%d" % t, T["got%d" % t], "got%d" % t
+        arrives(gk, "ao%d" % t, width(child, core))
+
+        def need(w):
+            return {"gx": ["tab"], "tr": ["gx0", "gx1"], "fl": ["tr"], "lcp": ["tr"], "dl": ["lcp"], "scan": ["fl"], "f": ["scan"], "nn": ["f2"],
+                    "km": ["dl", "nn0", "nn1"], "dp": ["tab"]}.get(parse(w)[0], [])
+
+        def run(q, w):
+            k, n, _ = parse(w)
+            if k == "tab":
+                tt(T.tab[:], ps(RANKB, C), T.jt[:], OP.add, r=["jt"], w=["tab"], b=[RANKB])
+                if t == 0:
+                    lists_of_candidates()
+                    for b in range(4):
+                        qz("e", 128 * b, 128 * b + 128, T.et[:, 3 - b:515 - b], r=["et"], w=["eq%d" % b])
+                for b in range(4):
+                    mm(b, "e", 128 * b, tn, 0, C, True, True, [tn + "_0", tn + "_1", "eq%d" % b])
+            elif k == "gx":
+                move(q, T.gx[:, 256 * n:256 * n + 256], T.tab[:].indirect(T.off1[:, 32 * t + 16 * n:32 * t + 16 * n + 16]), r=["tab", "off1"], w=["gx%d" % n])
+            elif k == "tr":
+                tr(T.ty[:], T.gx[:], r=["gx0", "gx1"], w=["ty"])
+            elif k == "fl":
+                ts(T.fl[:], T.ty[:], float(TH), OP.is_lt, r=["ty"], w=["fl"])
+            elif k == "lcp":
+                move(q, T.lcp[:], T.ty[:].indirect(T.offc[:, 40:56]), r=["ty", "offL"], w=["lcp"])
+            elif k == "dl":
+                tt(T.dl[:, 1:256], T.lcp[:, 1:256], T.lcp[:, 0:255], OP.subtract, r=["lcp"], w=["dl"])
+                ts(T.l7[:], T.lcp[:, 7:256:8], -float(C), OP.add, r=["lcp"], w=["l7"])
+                iota(T.dl[:, 0:256:8], [[0, 32]], -2 ** 20, 0, ["dl"])
+            elif k == "dp":
+                move(q, T.dp[:, C * n:C * n + C], ps(n, C), w=["dp%d" % n], b=[n])
+            elif k == "scan":
+                for i in range(4):
+                    scan(T.fs[:, 128 * i:128 * i + 128], got[:], T.fl[:, 128 * i:128 * i + 128], OP.mult, OP.add, r=[gk, "fl"], w=["fs%d" % i])
+            elif k == "f":
+                ts(T.f2[:], T.fs[:], 255.0 + 2.0 ** -8, OP.add, 256.0, OP.max, r=["fs%d" % i for i in range(4)], w=["f2"])
+            elif k == "nn":
+                args = (T.nn[:, 128 * n:128 * n + 128], T.f2[:].indirect(T.offc[:, 56 + 8 * n:64 + 8 * n]))
+                if q == "V":
+                    ts(*args, 256.0, OP.mult, -192.0 * 512, OP.add, r=["f2", "offN"], w=["nn%d" % n])
+                else:
+                    act(*args, AF.Copy, {"scale": 256.0, "bias": -192.0 * 512}, r=["f2", "offN"], w=["nn%d" % n])
+            else:
+                scan(T.km[:], T.dl[:], T.nn[:], OP.add, OP.max, r=["dl", "nn0", "nn1"], w=["km"])
+                for a in range(4):
+                    tt(T.tmp[0:32, a:128:4], T.l7[32 * a:32 * a + 32, :], T.km[32 * a:32 * a + 32, 7:256:8], OP.subtract, r=["km", "l7"], w=["tmp%d" % a])
+                for b in range(4):
+                    tr(T.tp[32 * b:32 * b + 32, :], T.tmp[0:32, 32 * b:32 * b + 32], r=["tmp%d" % a for a in range(4)], w=["tp%d" % b])
+                ts(T.ti[:], T.tp[:], 512.0, OP.mult, r=["tp%d" % b for b in range(4)], w=["ti"])
+                ts(T.tj[:], T.ti[:], 511, OP.bitwise_and, r=["ti"], w=["tj"])
+                cp(T.offz[:], T.tj[:], r=["tj"], w=["offz"])
+
+        weave({"V": CANV, "A": CANA}, need, run)
+
+    def layer(t, child):
+        hn = "h%d" % t
+        runs = RUNS[t + 1]
+
+        def need(w):
+            c = w[1]
+            return {"z": [], "g": ["q" + c], "q": ["z%s%d" % (c, b) for b in range(4)], "h": ["g%s%d" % (c, b) for b in range(4)]}[w[0]]
+
+        def run(q, w):
+            c = int(w[1])
+            a, e = runs[c]
+            if w[0] == "z":
+                b = int(w[2])
+                move(q, T.zt[:, 4 * a + b:4 * e:4], T.dp[:, C * b:C * b + C].indirect(T.offz[:, a // 16:e // 16]), r=["offz", "dp%d" % b], w=["z%d_%d" % (c, b)])
+            elif w[0] == "q":
+                qz("z", a, e, T.zt[:, 4 * a:4 * e], r=["z%d_%d" % (c, b) for b in range(4)], w=["zq%d" % c])
+                for b in (0, 2, 1, 3):
+                    mm(banks(c) + b, "wl", 128 * b, "z", a, e, True, True, ["zq%d" % c, "wq", "ws"])
+            elif w[0] == "g":
+                b = int(w[2])
+                k = {"w": ["g%d_%d" % (c, b)], "b": [banks(c) + b]}
+                if q == "V":
+                    ts(T.gt[:, 4 * a + b:4 * e:4], ps(banks(c) + b, e - a), 0.0, OP.max, 0.015625, OP.mult, **k)
+                else:
+                    act(T.gt[:, 4 * a + b:4 * e:4], ps(banks(c) + b, e - a), AF.Relu, {"scale": 0.015625}, **k)
+            else:
+                qz(hn, a, e, T.gt[:, 4 * a:4 * e], r=["g%d_%d" % (c, b) for b in range(4)], w=[hn + "_%d" % c])
+                sem = "ah%d_%d" % (t, c)
+                send(T["l%dq" % t][:, a:e].bitcast(dt.uint8), T[hn + "q"][:, a:e].bitcast(dt.uint8), sem, child, [hn + "_%d" % c])
+                send(T["l%ds" % t][:, a:e], T[hn + "s"][:, a:e], sem, child, [hn + "_%d" % c])
+
+        weave({"A": LAYA, "V": LAYV}, need, run)
+
+    def outputs(c):
+        nx = "t%d" % R
+        a, e = RUNS[R][c]
+        mm(banks(c), "v", 0, nx, a, e, True, True, [nx + "_%d" % c, "vq"])
+        dma("S", T.oc[:, 4 * a:4 * e], T[nx + "q"][:, a:e].bitcast(dt.uint8), r=[nx + "_%d" % c])
+        for k in range(4):
+            dma("AS"[k % 2], T.osc[4 * k:4 * k + 4, a:e], T[nx + "s"][32 * k:32 * k + 4, a:e], r=[nx + "_%d" % c])
+        cp(T.yb[:, a:e], ps(banks(c), e - a), w=["yb%d" % c], b=[banks(c)])
+        dma("A", T.y[:, a:e], T.yb[:, a:e], r=["yb%d" % c])
+
     for t in range(R):
         donor, child = T.cores[(rank + 1 + t) % N], T.cores[(rank - 1 - t) % N]
-        places_rest(t)
+        places(t)
         order(t, donor)
-        candidates(t)
         leaders(t, child)
         layer(t, child)
         if t == 0:
@@ -552,9 +593,9 @@ def rank_program(g, core, T, topo):
             act(T.elb[:], T.jrow[:].indirect(T.offz[:, 0:28]), AF.Copy, r=["jrow", "offz"], w=["elb"])
             dma("S", T.el[:], T.elb[0:128:16, :], r=["elb"])
         own_part(t)
-        state(t, 0, donor)
-        if t < R - 1:
-            places_first(t + 1)
-        state(t, 1, donor)
+        whole_state(t + 1, 0)
+    outputs(0)
+    whole_state(R, 1)
+    outputs(1)
     for s, n in total.items():
         wait("G", (s, n))

@@ -2,20 +2,26 @@ import math
 from concourse.mybir import dt, AluOpType as OP, ActivationFunctionType as AF
 
 C, R, TH = 448, 3, 320
-CUT = [192, 192, 192, 256]
+CUT = [192, 224, 224, 224]
 RUNS = [[(0, k), (k, C)] for k in CUT]
 NS = C // 32
 WIDTH = [C, 384, 320, 256, 192, 128, 128, C]
+EARLY = 4
+ONE = False
 SMALL = 2.0 ** -10
-PLV = "min0 tr0 u3 u2 x1.0 x1.1 u1.0 xq1 q5 u0 u1.1 min1 q6 tr1 u13 u12 q0 u9 u8 q2 q4 u6 u7.0 q3 eq parts trr q1 q7"
-PLA = "s5.1 s5.0 r5.1 r5.0 x1.2 x1.3 s4.0 s4.1 sum3 sum2 r4.0 r4.1 sum1 s11.0 s11.1 r11.0 r11.1 s10.0 s10.1 r10.0 sum13 r10.1 sum12 s7.1 r7.1 sum9 sum8 sum7 sum6"
-PLP = "sm0 sa0.1 sv0.0 sv0.1 sa0.0 dec1 sm1 sv1.0 sa1.0 sv1.1 sa1.1 rs13 rs12 col0 col5 col6 rs9 rs8 col2 col4 col3 col1 col7"
-CANV = "tab gx0 tr fl dl scan f2 nn0 km"
-CANA = "gx1 dp0 lcp dp1 nn1 dp2 dp3"
-LAYV = "z00 z01 q0 z10 g00 g01 h0 z11 q1 g10 g11 h1"
-LAYA = "z02 z03 z12 g02 g03 z13 g12 g13"
-MIXB, VB, AB = [4, 0], [[5, 6], [1, 2]], [[4, 7], [3, 0]]
-SUMB, RANKB, ORDB = [4, 5, 6], 7, 5
+PLV = "z0.0 z0.1 z1.0 zq0 z1.1 zq1 g0.0 g0.1 h0 g1.0 g1.1 h1 x0.0 x0.1 xq0 x1.0 x1.1 tr0 xq1 u3 u2 u1 u0 tr1 q5 q6 u13.0 u12.0 u13.1 u12.1 u9.0 q0 u9.1 u8 u7.0 q2 u7.1 u6 u5.0 q3 u4 q1 eq0 round eq1 parts q4 trr q7"
+PLA = "z0.2 z0.3 z1.2 z1.3 g0.2 g0.3 g1.2 g1.3 x0.2 x0.3 x1.2 x1.3 sum3 sum2 sum1 s11.1 s10.1 r11.1 s11.0 r10.1 s10.0 r11.0 r10.0 sum13 sum12 s5.1 sum9 r5.1 sum8 sum5 sum4 sum7 sum6"
+PLP = "w0 w1 own0 own1 dec0 dec1 sm0 sv0.0 sv0.1 sm1 sv1.0 sa1.1 sv1.1 sa1.0 rs13 rs12 col0 col5 col6 rs9 rs8 col2 rs7 rs6 col3 col1 col4 col7"
+CANV = "wo oq tab gx0 tr fl dl scan l7 nn km tmp"
+CANA = "exp gx1 lcp dp0 dp1 dp2 dp3"
+CANP = "om dm0 dm1 dm2 dm3"
+FIRST = {"tr0": "k2 tr0 k3", "tr1": "k4 tr1", "q0": "k1 q0", "q2": "k5 q2", "round": "round k6", "parts": "parts k7", "trr": "trr k8", "q7": "q7 k9"}
+ENDV = "z0.0 z0.1 z1.0 zq0 z1.1 zq1 g0.0 g0.1 g1.0 h0 g1.1 h1 x0.0 x0.1 xq0 x1.0 x1.1 out0 xq1 out1"
+ENDA = "z0.2 z0.3 z1.2 z1.3 g0.2 g0.3 g1.2 g1.3 el0 x0.2 x0.3 x1.2 x1.3 os0.0 os0.2 os1.0 os1.2"
+ENDP = "w0 w1 own0 own1 dec0 dec1 y0 y1"
+ENDS = "oc0 os0.1 os0.3 oc1 os1.1 os1.3"
+MIXB, VB, AB = [4, 0], [[5, 6], [1, 2]], [[4, 7], [3, 4]]
+SUMB, RANKB, ORDB = [0, 5, 6], 7, 5
 
 BF, F32, I32, U16, Q, U8 = "bfloat16", "float32", "int32", "uint16", "float8_e4m3fn_x4", "uint8"
 SCRATCH = {"ps": ("psum", [128, 4096], F32)}
@@ -34,11 +40,11 @@ for _n, _w, _d in [
     ("xin", 4 * C, BF), ("xt", 4 * C, BF), ("ut", 512, BF), ("vt", 512, BF), ("cds", 128, I32), ("cdg", 128, F32), ("cdt", 128, F32),
     ("off1", 96, U16), ("et", 520, BF), ("rt", 520, BF), ("ones", 520, BF), ("zer", 520, BF), ("cst", 512, BF), ("csh", 512, BF), ("c2", 512, BF),
     ("pb", 128, F32), ("pc", 128, F32), ("pi", 8, I32), ("ci", 8, I32), ("cf", 8, F32), ("col", 16, F32), ("ib", 72, F32), ("offc", 72, U16),
-    ("ig", 128, BF), ("ia", 128, BF), ("ca", 384, BF), ("cb", 384, BF), ("b1", 128, BF), ("r32", 32, BF), ("i32w", 32, F32), ("r32b", 32, BF),
-    ("cm0", 320, BF), ("cmask", 320, BF), ("j0", C, F32), ("jt", C, F32), ("jrow", C, F32),
+    ("ig", 128, BF), ("ia", 128, BF), ("ca", 384, BF), ("cb", 384, BF), ("r32", 32, BF), ("i32w", 32, F32), ("r32b", 32, BF),
+    ("j0", C, F32), ("jt", C, F32), ("jrow", C, F32),
     ("m1", C, F32), ("st", C, F32), ("sg", 16 * C, BF), ("junk", 5824, BF), ("racc", 28, F32), ("ra", 64, F32), ("rp", C, BF),
     ("wo", 512, BF), ("tab", C, F32), ("gx", 512, F32), ("ty", 512, F32), ("fl", 512, BF), ("lcp", 256, F32), ("dl", 256, F32), ("l7", 32, F32),
-    ("fs", 512, BF), ("f2", 512, BF), ("nn", 256, F32), ("km", 256, F32),
+    ("fs", 512, BF), ("nn", 256, I32), ("km", 256, F32),
     ("tmp", 128, F32), ("tp", 32, F32), ("ti", 32, I32), ("tj", 32, I32), ("offz", 32, U16),
     ("dp", 4 * C, BF), ("zt", 4 * C, BF), ("gt", 4 * C, BF), ("yb", C, F32), ("elb", C, F32),
 ]:
@@ -200,8 +206,8 @@ def rank_program(g, core, T, topo):
     def zero(out, w):
         iota(out, [[0, out.shape[1]]], 0, 0, w)
 
-    def sel(out, in_, pat, o, cm, base=0, **k):
-        op("G", lambda: g.affine_select(out, in_, pat, o, 0.0, base, cm), **k)
+    def sel(out, in_, pat, o, cm, base=0, fill=0.0, **k):
+        op("G", lambda: g.affine_select(out, in_, pat, o, fill, base, cm), **k)
 
     dma("A", T.ut[:], T.u[:], w=["ut"])
     for c, (a, e) in enumerate(RUNS[0]):
@@ -210,7 +216,6 @@ def rank_program(g, core, T, topo):
     iota(T.ib[:, 0:24], [[16, 3], [32, 4], [0, 2]], 0, 0, ["ibU"])
     iota(T.ig[:], [[0, 16], [1, 8]], 0, 0, ["ig"])
     iota(T.ia[:], [[1, 8], [-100, 2], [0, 8]], 100, 0, ["ia"])
-    iota(T.cm0[:], [[0, 10], [2, 32]], -1, 0, ["cm0"])
     ms(T.zer[:], 0.0, w=["zer"])
     act(T.ones[:], T.zer[:], AF.Exp, r=["zer"], w=["ones"])
     ms(T.cds[:], 0, w=["cds"])
@@ -219,21 +224,26 @@ def rank_program(g, core, T, topo):
     dma("S", T.wlq[:].bitcast(dt.uint8), T.wc[:], w=["wq"])
     dma("S", T.wls[:], T.ws[:], w=["ws"])
     dma("S", T.vt[:], T.v[:], w=["vt"])
-    for i, (sh, m) in enumerate([(5, 3), (4, 7), (0, 1), (1, 15), (3, 1), (0, 31), (0, 15)]):
+    for i, (sh, m) in enumerate([(5, 3), (4, 7), (0, 1), (3, 1), (0, 15)]):
         ts(T.ci[:, i:i + 1], T.pi[:, 0:1], sh, OP.logical_shift_right, m, OP.bitwise_and, r=["pi"], w=["ci%d" % i])
-    cp(T.cf[:, 0:7], T.ci[:, 0:7], r=["ci%d" % i for i in range(7)], w=["cf"])
-    run32, pg, odd, half, bit3, l32, l16 = [T.cf[:, i:i + 1] for i in range(7)]
-    pa0, pa1, pr, wr, not31, mix, m4, tie = [T.col[:, i:i + 1] for i in range(8)]
+    ms(T.rt[:], 0.0, w=["rt"])
+    cp(T.cf[:, 0:5], T.ci[:, 0:5], r=["ci%d" % i for i in range(5)], w=["cf"])
+    run32, pg, odd, bit3, l16 = [T.cf[:, i:i + 1] for i in range(5)]
+    pa0, pa1, pr, wr, mix, tie = [T.col[:, i:i + 1] for i in range(6)]
     cp(T.offc[:, 0:16], T.ib[:, 0:16], r=["ibU"], w=["offU"])
+    ms(T.k6[:, 256:512], 0.0, w=["kz6"])
+    ms(T.k6[:, 129:256:2], 0.0, w=["kz6b"])
     ts(mix, odd, 16.0, OP.mult, -32.0, OP.add, r=["cf"], w=["mix"])
     ts(pa0, run32, 2.0, OP.mult, r=["cf"], w=["pa0"])
     ts(pa1, run32, 2.0, OP.mult, 1.0, OP.add, r=["cf"], w=["pa1"])
     ts(pr, run32, 2.0, OP.mult, bit3, OP.add, r=["cf"], w=["pr"])
     ts(wr, bit3, 1.0 - 1.0 / SMALL, OP.mult, -1.0, OP.add, r=["cf"], w=["wr"])
-    ts(m4, half, 4.0, OP.mult, r=["cf"], w=["m4"])
-    ts(not31, l32, 31.0, OP.not_equal, r=["cf"], w=["not31"])
+    ms(T.racc[:], 0.0, w=["racc0"])
+    ms(T.csh[:, 3:512:4], 0.0, w=["csh3"])
     ts(T.offc[:, 16:24], T.ib[:, 16:24], mix, OP.add, r=["ibU", "mix"], w=["offM"])
-    act(T.rt[:], T.zer[:], AF.Copy, r=["zer"], w=["rt"])
+    for i in range(6):
+        ms(T["k%d" % i][:, 4 * WIDTH[i] - 127:4 * WIDTH[i]:2], 0.0, w=["kz%d" % i])
+    act(T.c2[:], T.zer[:, 0:512], AF.Copy, r=["zer"], w=["c2z"])
 
     def counter(n, out, colap, weight, keys, w):
         x0, x1 = T.ca[:, 128 * n:128 * n + 128], T.cb[:, 128 * n:128 * n + 128]
@@ -241,44 +251,34 @@ def rank_program(g, core, T, topo):
         ts(x1, T.ia[:], colap, OP.is_equal, weight, OP.mult, r=["ia"] + keys, w=["cb%d" % n])
         return lambda: tt(out, x0, x1, OP.subtract, r=["ca%d" % n, "cb%d" % n], w=[w])
 
-    counters = [counter(0, T.cst[:, 0:512:4], pa0, 1.0, ["pa0"], "cst0"), counter(1, T.b1[:], pa1, 1.0, ["pa1"], "b1"),
+    counters = [counter(0, T.cst[:, 0:512:4], pa0, 1.0, ["pa0"], "cst0"), counter(1, T.csh[:, 2:512:4], pa1, 1.0, ["pa1"], "csh2"),
                 counter(2, T.csh[:, 1:512:4], pr, wr, ["pr", "wr"], "csh1")]
-    ts(T.cmask[:], T.cm0[:], m4, OP.subtract, -1e28, OP.mult, r=["cm0", "m4"], w=["cmask"])
     qz("u", 0, 128, T.ut[:], r=["ut"], w=["uq"])
-    ms(T.cmask[:, 31:320:32], 1e28, w=["cmask"])
+    ms(T.rp[:], 0.0, w=["rp0", "rp1", "rp8", "rp9"])
     cp(T.ubq[:].bitcast(dt.uint32), T.uq[:].bitcast(dt.uint32).indirect(T.offc[:, 0:24]), r=["uq", "offU", "offM"], w=["ubq"])
     act(T.ubs[:], T.us[:].indirect(T.offc[:, 0:24]), AF.Copy, r=["uq", "offU", "offM"], w=["ubs"])
     for c, (a, e) in enumerate(RUNS[0]):
         qz("t0", a, e, T.xin[:, 4 * a:4 * e], r=["xin%d" % c], w=["t0_%d" % c])
     for last in counters:
         last()
-    zero(T.k6[:, 256:512], ["kz6"])
-    zero(T.k6[:, 129:256:2], ["kz6b"])
-    for i in (5, 4):
-        zero(T["k%d" % i][:, 4 * WIDTH[i] - 127:4 * WIDTH[i]:2], ["kz%d" % i])
-    zero(T.racc[:], ["racc0"])
-    sel(T.rt[:, 1:513:2], T.ones[:, 0:256], [[-1, 128], [0, 2]], OP.is_equal, 1, r=["ones"], w=["rt"])
-    sel(T.cst[:, 1:512:4], T.cst[:, 0:512:4], [[0, 128]], OP.is_ge, 0, r=["cst0"], w=["cst1"])
-    for i in (0, 2, 3, 1):
-        zero(T["k%d" % i][:, 4 * WIDTH[i] - 127:4 * WIDTH[i]:2], ["kz%d" % i])
-    zero(T.csh[:, 3:512:4], ["csh3"])
     iota(T.pb[:, 0:32], [[0, 2], [2000, 2], [0, 8]], 0, 0, ["pb2"])
     iota(T.pb[:, 96:128], [[0, 2], [100, 2], [-1, 8]], -100, 0, ["pb5"])
     for hf in range(2):
         iota(T.pb[:, 32 + 16 * hf:48 + 16 * hf], [[64, 2], [6, 4], [32, 2]], 0, 0, ["pb3%d" % hf])
         iota(T.pb[:, 64 + 16 * hf:80 + 16 * hf], [[32, 2], [128, 4], [16, 2]], 0, 0, ["pb4%d" % hf])
     iota(T.i32w[:], [[0, 4], [1, 8]], 0, 0, ["i32w"])
-    zero(T.c2[:], ["c2z"])
-    zero(T.rp[:], ["rp0", "rp1", "rp8", "rp9"])
-    zero(T.k7[:, 3:4 * C:4], ["kz7"])
-    zero(T.wo[:], ["wo0", "wo1", "wo2", "wo3"])
-    iota(T.j0[:], [[32 * 513, NS], [2, 16], [513, 2]], -512, 0, ["j0"])
+    iota(T.ib[:, 24:32], [[56, 2], [16, 2], [28, 2]], 0, 0, ["ibA"])
+    iota(T.ib[:, 32:40], [[1, 8]], 0, 0, ["ibB"])
+    iota(T.ib[:, 40:56], [[1, 8], [64, 2]], 0, 0, ["ibL"])
+    iota(T.ib[:, 56:72], [[1, 8], [64, 2]], 8, 0, ["ibN"])
+    sel(T.rt[:, 1:513:2], T.ones[:, 0:256], [[-1, 128], [0, 2]], OP.is_equal, 1, r=["ones"], w=["rt"])
+    sel(T.et[:, 0:516], T.ones[:, 0:516], [[-1, 516]], OP.is_equal, 4, 3, r=["ones"], w=["et"])
 
     def constants_0():
         for t in (2, 3):
-            act(T.cst[:, t:512:4], T.b1[:], AF.Copy, {"scale": 1.0 / SMALL}, r=["b1"], w=["cst%d" % t])
-        act(T.csh[:, 0:512:4], T.cst[:, 0:512:4], AF.Identity, {"scale": not31}, r=["cst0", "not31"], w=["csh0"])
-        act(T.csh[:, 2:512:4], T.b1[:], AF.Identity, {"scale": not31}, r=["b1", "not31"], w=["csh2"])
+            act(T.cst[:, t:512:4], T.csh[:, 2:512:4], AF.Copy, {"scale": 1.0 / SMALL}, r=["csh2"], w=["cst%d" % t])
+        act(T.cst[:, 1:512:4], T.cst[:, 0:512:4], AF.Copy, r=["cst0"], w=["cst1"])
+        act(T.csh[:, 0:512:4], T.cst[:, 0:512:4], AF.Copy, r=["cst0"], w=["csh0"])
 
     def constants_1():
         for o in range(2):
@@ -289,58 +289,97 @@ def rank_program(g, core, T, topo):
         tr(T.pc[:], T.pb[:], r=["pb2", "pb30", "pb31", "pb40", "pb41", "pb5"], w=["pc"])
         ts(T.r32[:], T.i32w[:], pg, OP.is_equal, r=["i32w", "cf"], w=["r32"])
         ts(T.r32b[:], T.i32w[:], -1.0, OP.add, pg, OP.is_equal, r=["i32w", "cf"], w=["r32b"])
+
+    def constants_3():
         ts(T.col[:, 8:9], T.pc[:, 96:97], pg, OP.add, 0.5, OP.min, r=["pc", "cf"], w=["tie0"])
         ts(T.r32b[:, 0:32:8], T.i32w[:, 0:32:8], 7.0, OP.add, pg, OP.is_equal, r=["i32w", "cf"], w=["r32b"])
+
+    def constants_4():
         ts(tie, T.col[:, 8:9], -0.5, OP.max, r=["tie0"], w=["tie"])
         tt(T.r32[:], T.r32[:], T.r32b[:], OP.subtract, r=["r32b"], w=["r32"])
         iota(T.r32[:, 0:32:16], [[0, 2]], -8, 0, ["r32"])
         for b in range(4):
             sel(T.c2[:, 129 * b:128 * b + 128:4], T.r32[:], [[0, 32]], OP.is_ge, 0, r=["r32", "c2z"], w=["c2r%d" % b])
-        iota(T.ib[:, 24:32], [[56, 2], [16, 2], [28, 2]], 0, 0, ["ibA"])
-        iota(T.ib[:, 32:40], [[1, 8]], 0, 0, ["ibB"])
-        iota(T.ib[:, 40:56], [[1, 8], [64, 2]], 0, 0, ["ibL"])
-        iota(T.ib[:, 56:72], [[1, 8], [64, 2]], 8, 0, ["ibN"])
-        sel(T.et[:, 0:516], T.ones[:, 0:516], [[-1, 516]], OP.is_equal, 4, 3, r=["ones"], w=["et"])
 
-    def constants_3():
+    def constants_5():
+        zero(T.k7[:, 3:4 * C:4], ["kz7"])
+        iota(T.j0[:], [[32 * 513, NS], [2, 16], [513, 2]], -512, 0, ["j0"])
+        zero(T.wo[:], ["wo0", "wo1", "wo2", "wo3"])
+        iota(T.jrow[:], [[1, C]], 0, 0, ["jrow"])
         qz("cs", 128, 256, T.csh[:], r=["csh%d" % t for t in range(4)], w=["csh"])
-        qz("cc", 0, 128, T.c2[:], r=["c2r%d" % b for b in range(4)], w=["cc"])
-
-    def lists_of_candidates():
         for nm, a, b_, c in (("A", 24, 32, l16), ("B", 32, 40, T.pc[:, 32:33]), ("L", 40, 56, T.pc[:, 64:65]), ("N", 56, 72, T.pc[:, 64:65])):
             ts(T.offc[:, a:b_], T.ib[:, a:b_], c, OP.add, r=["ib" + nm, "cf", "pc"], w=["off" + nm])
-        cp(T.cdg[:], T.cds[:].indirect(T.offc[:, 24:32]), r=["offA"] + ["cds%d" % a for a in range(4)], w=["cdg"])
-        tr(T.cdt[:], T.cdg[:], r=["cdg"], w=["cdt"])
-        cp(T.off1[:], T.cdt[:].indirect(T.offc[:, 32:38]), r=["cdt", "offB"], w=["off1"])
+
+    def unit(b):
+        qz("e", 128 * b, 128 * b + 128, T.et[:, 3 - b:515 - b], r=["et"], w=["eq%d" % b])
+
+    CONST = [constants_0, constants_1, constants_2, constants_3, constants_4, constants_5,
+             lambda: cp(T.cdg[:], T.cds[:].indirect(T.offc[:, 24:32]), r=["offA"] + ["cds%d" % a for a in range(4)], w=["cdg"]),
+             lambda: tr(T.cdt[:], T.cdg[:], r=["cdg"], w=["cdt"]),
+             lambda: [cp(T.off1[:], T.cdt[:].indirect(T.offc[:, 32:38]), r=["cdt", "offB"], w=["off1"]), unit(0)],
+             lambda: [qz("cc", 0, 128, T.c2[:], r=["c2r%d" % b for b in range(4)], w=["cc"]), unit(1), unit(2), unit(3)],
+             lambda: qz("v", 0, 128, T.vt[:], r=["vt"], w=["vq"])]
 
     def banks(c):
         return 4 * ((c + 1) % 2)
 
-    def own_part(t):
-        tn = "t%d" % t
-        for c, (a, e) in enumerate(RUNS[t + 1]):
-            for b in range(4):
-                mm(banks(c) + b, "e", 128 * b, tn, a, e, True, False, [tn + "_0", tn + "_1"])
+    def four(k, c):
+        return ["%s%d.%d" % (k, c, b) for b in range(4)]
 
-    def state(step, t, c, q="V", b=0):
-        ln, nx = "l%d" % (t - 1), "t%d" % t
+    LAYER = {"z": lambda c: [], "zq": lambda c: four("z", c), "w": lambda c: ["zq%d" % c], "g": lambda c: ["w%d" % c], "h": lambda c: four("g", c),
+             "own": lambda c: four("g", c), "dec": lambda c: ["own%d" % c], "x": lambda c: ["dec%d" % c], "xq": lambda c: four("x", c),
+             "y": lambda c: ["xq%d" % c], "out": lambda c: ["y%d" % c], "oc": lambda c: ["xq%d" % c], "os": lambda c: ["xq%d" % c], "el": lambda c: []}
+
+    def layer(q, k, c, b, t):
+        on, hn, ln, nx = "t%d" % (t - 1), "h%d" % (t - 1), "l%d" % (t - 1), "t%d" % t
         a, e = RUNS[t][c]
-        if t == 0:
-            return
-        if step == "dec":
-            arrives(ln + "_%d" % c, "ah%d_%d" % (t - 1, c), 2 * width(T.cores[(rank + t) % N], core))
+        donor, child = T.cores[(rank + t) % N], T.cores[(rank - t) % N]
+        if k == "z":
+            move(q, T.zt[:, 4 * a + b:4 * e:4], T.dp[:, C * b:C * b + C].indirect(T.offz[:, a // 16:e // 16]), r=["offz", "dp%d" % b], w=["z%d_%d" % (c, b)])
+        elif k == "zq":
+            qz("z", a, e, T.zt[:, 4 * a:4 * e], r=["z%d_%d" % (c, b) for b in range(4)], w=["zq%d" % c])
+        elif k == "w":
+            for b in (0, 2, 1, 3):
+                mm(banks(c) + b, "wl", 128 * b, "z", a, e, True, True, ["zq%d" % c, "wq", "ws"])
+        elif k == "g":
+            kw = {"w": ["g%d_%d" % (c, b)], "b": [banks(c) + b]}
+            if q == "V":
+                ts(T.gt[:, 4 * a + b:4 * e:4], ps(banks(c) + b, e - a), 0.0, OP.max, 0.015625, OP.mult, **kw)
+            else:
+                act(T.gt[:, 4 * a + b:4 * e:4], ps(banks(c) + b, e - a), AF.Relu, {"scale": 0.015625}, **kw)
+        elif k == "h":
+            qz(hn, a, e, T.gt[:, 4 * a:4 * e], r=["g%d_%d" % (c, b) for b in range(4)], w=[hn + "_%d" % c])
+            sem = "ah%d_%d" % (t - 1, c)
+            if ONE:
+                a, keys = 0, [hn + "_0", hn + "_1"]
+            else:
+                keys = [hn + "_%d" % c]
+            if c or not ONE:
+                send(T[ln + "q"][:, a:e].bitcast(dt.uint8), T[hn + "q"][:, a:e].bitcast(dt.uint8), sem, child, keys)
+                send(T[ln + "s"][:, a:e], T[hn + "s"][:, a:e], sem, child, keys)
+        elif k == "own":
+            for b in (0, 2, 1, 3):
+                mm(banks(c) + b, "e", 128 * b, on, a, e, True, False, [on + "_0", on + "_1"])
+        elif k == "dec":
+            arrives(ln + "_%d" % c, "ah%d_%d" % (t - 1, 1 if ONE else c), 2 * width(donor, core))
             for b in (0, 2, 1, 3):
                 mm(banks(c) + b, "e", 128 * b, ln, a, e, False, True, [ln + "_%d" % c])
-        elif step == "x":
+        elif k == "x":
             move(q, T.xt[:, 4 * a + b:4 * e:4], ps(banks(c) + b, e - a), w=["x%d_%d" % (c, b)], b=[banks(c) + b])
-        else:
+        elif k == "xq":
             qz(nx, a, e, T.xt[:, 4 * a:4 * e], r=["x%d_%d" % (c, b) for b in range(4)], w=[nx + "_%d" % c])
-
-    def whole_state(t, c):
-        state("dec", t, c)
-        for b in range(4):
-            state("x", t, c, "VVAA"[b], b)
-        state("xq", t, c)
+        elif k == "y":
+            mm(banks(c), "v", 0, nx, a, e, True, True, [nx + "_%d" % c, "vq"])
+        elif k == "oc":
+            dma(q, T.oc[:, 4 * a:4 * e], T[nx + "q"][:, a:e].bitcast(dt.uint8), r=[nx + "_%d" % c])
+        elif k == "os":
+            dma(q, T.osc[4 * b:4 * b + 4, a:e], T[nx + "s"][32 * b:32 * b + 4, a:e], r=[nx + "_%d" % c])
+        elif k == "out":
+            move(q, T.yb[:, a:e], ps(banks(c), e - a), w=["yb%d" % c], b=[banks(c)])
+            dma("A", T.y[:, a:e], T.yb[:, a:e], r=["yb%d" % c])
+        else:
+            act(T.elb[:], T.jrow[:].indirect(T.offz[:, 0:28]), AF.Copy, r=["jrow", "offz"], w=["elb"])
+            dma("S", T.el[:], T.elb[0:128:16, :], r=["elb"])
 
     koff = [sum(WIDTH[:i]) for i in range(8)]
 
@@ -366,38 +405,41 @@ def rank_program(g, core, T, topo):
 
     def places(t):
         tn, CH = "t%d" % t, RUNS[t]
-        cut = CUT[t] // 32
+        cut = EARLY
 
         def made(blocks):
             return [x % (s, h) for s in blocks for h in range(2) for x in ("u%d.%d", "r%d.%d")] + ["u%d" % s for s in blocks]
 
         early = made(range(cut))
+        rk = ["racc0"] + ["racc%d_%d" % (s, h) for s in range(NS) for h in range(2)]
+        whole, fine = T.ra[:, 0:28], T.ra[:, 32:60]
 
         def need(w):
             k, n, h = parse(w)
             c = int(n is not None and n >= cut)
+            if k in LAYER:
+                return LAYER[k](n)
             if k in ("u", "s"):
-                return ["tr%d" % c] + ["s%s%d.%d" % ("v" if k == "u" else "a", c, x) for x in range(2) if h in (None, x)]
+                return ["tr%d" % int(32 * n >= CUT[t])] + ["s%s%d.%d" % ("v" if k == "u" else "a", c, x) for x in range(2) if h in (None, x)]
             if k in ("sm", "sv", "sa"):
-                return ["xq%d" % n] + (["min%d" % n] if k == "sa" and AB[n][h] == MIXB[n] else [])
+                return ["xq%d" % n] + (["tr0"] + ["s%d.0" % s for s in range(cut) if n] if k == "sa" and AB[n][h] == MIXB[0] else [])
             if k == "rs":
-                return ["q%d" % tile_of(n)] + ["sum%d" % s for s in BY_PE[:max(0, BY_PE.index(n) + 1 - len(SUMB))]] + early
+                return ["k1", "q%d" % tile_of(n)] + ["sum%d" % s for s in BY_PE[:max(0, BY_PE.index(n) + 1 - len(SUMB))]] + early
             if k == "q":
-                return made([NS - 1 - 2 * n, NS - 2 - 2 * n]) if n < 7 else ["trr", "eq"]
-            return {"x": ["dec1"], "xq": ["x1.%d" % b for b in range(4)], "min": ["sm%s" % n], "tr": ["min%s" % n], "r": ["s%s.%s" % (n, h)],
-                    "eq": ["tr0", "tr1", "sv1.0", "sv1.1"], "sum": ["rs%s" % n] + made([n or 0]), "col": ["q%s" % n] + early,
-                    "parts": ["sum%d" % s for s in range(NS)] + made(range(NS)), "trr": ["parts"]}.get(k, [])
+                return made([NS - 1 - 2 * n, NS - 2 - 2 * n]) if n < 7 else ["trr", "eq0", "eq1"]
+            return {"k": {1: ["k0"], 5: ["k0", "mask"]}.get(n, []), "jt": ["k5"], "mask": ["tr0", "tr1", "k4"], "tr": ["sm%s" % n], "r": ["s%s.%s" % (n, h)],
+                    "eq": ["mask", "sv1.0", "sv1.1"], "sum": ["rs%s" % n] + made([n or 0]), "col": ["k1", "q%s" % n] + early,
+                    "round": ["sum%d" % s for s in range(NS)] + made(range(NS)), "parts": ["round"], "trr": ["parts"]}.get(k, [])
 
         def unit_in(s, h, bk):
-            c = int(s >= cut)
-            return bk[c][h], T.st[:, 32 * s + 30 + h:32 * s + 31 + h], ["st%d" % c], 32 * s + 32
+            return bk[int(s >= cut)][h], T.st[:, 32 * s + 30 + h:32 * s + 31 + h], ["st%d" % int(32 * s >= CUT[t])], 32 * s + 32
 
         def run(q, w):
             k, n, h = parse(w)
-            if k in ("x", "xq", "dec"):
-                state(k, t, n, q, h)
+            if k in LAYER:
+                layer(q, k, n, h, t)
             elif k == "k":
-                [constants_0, constants_1, constants_2, constants_3][n]()
+                CONST[n]()
             elif k == "jt":
                 act(T.jt[:], T.j0[:], AF.Identity, {"scale": 2.0 ** -9, "bias": T.pc[:, 0:1]}, r=["j0", "pc"], w=["jt"])
             elif k in ("sm", "sv", "sa"):
@@ -406,18 +448,19 @@ def rank_program(g, core, T, topo):
                 if k == "sm":
                     mm(MIXB[n], "ub", 256, tn, a, e, True, True, keys)
                 else:
-                    mm((VB if k == "sv" else AB)[n][h], "ub", 128 * h, tn, 0, e, True, True, keys)
-            elif k == "min":
-                a, e = CH[n]
-                tt(T.m1[:, a:e], ps(MIXB[n], e - a), T.cmask[:, 0:e - a], OP.min, r=["cmask"], w=["m1%d" % n], b=[MIXB[n]])
+                    mm((VB if k == "sv" else AB)[n][h], "ub", 128 * h, tn, 0, e if n else max(128, 32 * cut), True, True, keys)
             elif k == "tr":
                 a, e = CH[n]
-                tr(T.st[:, a:e], T.m1[:, a:e], r=["m1%d" % n], w=["st%d" % n])
+                tr(T.st[:, a:e], ps(MIXB[n], e - a), w=["st%d" % n], b=[MIXB[n]])
+            elif k == "mask":
+                for i in range(4):
+                    wait("G", ("qG", total["qG"]))
+                    sel(T.m1[32 * i:32 * i + 32, :], T.st[32 * i:32 * i + 32, :], [[0, NS], [2, 16], [0, 2]], OP.is_ge, -1, 0, -1e28, r=["st0", "st1"], w=["m1%d" % i])
+                wait("G", ("qG", total["qG"]))
             elif k == "eq":
-                for h in range(2):
-                    for o in range(2):
-                        tt(T.k7[:, 4 * o + 2 * h:4 * C:8], ps(VB[1][h], C, o, 2), T.st[:, h:C:2], OP.is_equal,
-                           r=["st0", "st1"], w=["ue%d%d" % (h, o)], b=[VB[1][h]])
+                for o in range(2):
+                    tt(T.k7[:, 4 * o + 2 * n:4 * C:8], ps(VB[1][n], C, o, 2), T.m1[:, n:C:2], OP.is_equal,
+                       r=["m1%d" % i for i in range(4)], w=["ue%d%d" % (n, o)], b=[VB[1][n]])
             elif k == "u":
                 for h in range(2) if h is None else [h]:
                     b, sc, keys, m = unit_in(n, h, VB)
@@ -455,11 +498,10 @@ def rank_program(g, core, T, topo):
                     act(junk(n, 2 * m), slot(n, 0, 0, m, 2), AF.Copy, {"accum_out": acc(n, 0)}, r=["racc0", ukeys(n, 0)[0], ukeys(n, 1)[0]], w=["racc%d_0" % n, "junk%d" % n])
                 else:
                     act(junk(n, m), slot(n, mine[0], 0, m), AF.Copy, {"accum_out": acc(n, mine[0])}, r=["racc0", ukeys(n, mine[0])[0]], w=["racc%d_%d" % (n, mine[0]), "junk%d" % n])
-            elif k == "parts":
-                rk = ["racc0"] + ["racc%d_%d" % (s, h) for s in range(NS) for h in range(2)]
-                whole, fine = T.ra[:, 0:28], T.ra[:, 32:60]
+            elif k == "round":
                 for out, e, key in ((T.rp[:, 0:C:16], 28, "rp0"), (whole, 23, "whole"), (fine, 18, "fine")):
                     ts(out, T.racc[:], 1.5 * 2.0 ** e, OP.add, 1.5 * 2.0 ** e, OP.subtract, r=rk, w=[key])
+            elif k == "parts":
                 tt(T.rp[:, 1:C:16], whole, T.rp[:, 0:C:16], OP.subtract, r=["whole", "rp0"], w=["rp1"])
                 tt(T.rp[:, 8:C:16], fine, whole, OP.subtract, r=["whole", "fine"], w=["rp8"])
                 tt(T.rp[:, 9:C:16], T.racc[:], fine, OP.subtract, r=rk + ["fine"], w=["rp9"])
@@ -468,38 +510,43 @@ def rank_program(g, core, T, topo):
             else:
                 mm(RANKB, "cs", 128 if n == 7 else 0, "k", koff[n], koff[n] + WIDTH[n], n == 0, n == 7, ["kq%d" % n, "csh" if n == 7 else "cs"])
 
-        plv, pla = PLV, PLA
+        queues = {"P": PLP, "G": "mask", "V": PLV, "A": PLA}
         if t == 0:
-            plv = plv.replace("q0", "k1 q0").replace("q2", "k2 q2").replace("parts", "k3 parts")
-            pla = "k0 " + pla + " jt"
-        weave({"P": PLP, "V": plv, "A": pla}, need, run)
+            queues = {q: " ".join(w for w in s.split() if parse(w)[0] not in LAYER) for q, s in queues.items()}
+            queues["V"] = " ".join(FIRST.get(w, w) for w in queues["V"].split())
+            queues["A"] = "k0 " + queues["A"] + " jt"
+        if t == 1:
+            queues["V"] = queues["V"].replace("h1", "h1 k10")
+        if t == R:
+            queues = {"P": ENDP, "V": ENDV, "A": ENDA, "S": ENDS}
+        weave(queues, need, run)
 
-    def order(t, donor):
-        for a in range(4):
-            ts(T.wo[:, 128 * a:128 * a + 112], ps(RANKB, C, a, 4), tie, OP.is_lt, r=["tie"], w=["wo%d" % a], b=[RANKB])
-        qz("od", 0, 128, T.wo[:], r=["wo%d" % a for a in range(4)], w=["oq"])
-        mm(ORDB, "od", 0, "cc", 0, 128, True, True, ["oq", "cc"])
-        act(T["ord%d" % t][:], ps(ORDB, 128), AF.Exp, {"scale": math.log(2.0)}, w=["ord%d" % t], b=[ORDB])
-        send(T["got%d" % t][:], T["ord%d" % t][:], "ao%d" % t, donor, ["ord%d" % t])
-
-    def leaders(t, child):
+    def leaders(t):
         tn, got, gk = "t%d" % t, T["got%d" % t], "got%d" % t
+        donor, child = T.cores[(rank + 1 + t) % N], T.cores[(rank - 1 - t) % N]
         arrives(gk, "ao%d" % t, width(child, core))
 
         def need(w):
-            return {"gx": ["tab"], "tr": ["gx0", "gx1"], "fl": ["tr"], "lcp": ["tr"], "dl": ["lcp"], "scan": ["fl"], "f": ["scan"], "nn": ["f2"],
-                    "km": ["dl", "nn0", "nn1"], "dp": ["tab"]}.get(parse(w)[0], [])
+            k, n, _ = parse(w)
+            return {"oq": ["wo"], "om": ["oq"], "exp": ["om"], "gx": ["tab", "lists"], "tr": ["gx0", "gx1"], "fl": ["tr"], "lcp": ["tr"], "dl": ["lcp"], "l": ["lcp"],
+                    "scan": ["fl"], "nn": ["scan"], "km": ["dl", "nn"], "tmp": ["km", "l7"], "dm": ["unit"], "dp": ["dm%s" % n]}.get(k, [])
 
         def run(q, w):
             k, n, _ = parse(w)
-            if k == "tab":
+            if k == "wo":
+                for a in range(4):
+                    ts(T.wo[:, 128 * a:128 * a + 112], ps(RANKB, C, a, 4), tie, OP.is_lt, r=["tie"], w=["wo%d" % a], b=[RANKB])
+            elif k == "oq":
+                qz("od", 0, 128, T.wo[:], r=["wo%d" % a for a in range(4)], w=["oq"])
+            elif k == "om":
+                mm(ORDB, "od", 0, "cc", 0, 128, True, True, ["oq", "cc"])
+            elif k == "exp":
+                act(T["ord%d" % t][:], ps(ORDB, 128), AF.Exp, {"scale": math.log(2.0)}, w=["ord%d" % t], b=[ORDB])
+                send(got[:], T["ord%d" % t][:], "ao%d" % t, donor, ["ord%d" % t])
+            elif k == "tab":
                 tt(T.tab[:], ps(RANKB, C), T.jt[:], OP.add, r=["jt"], w=["tab"], b=[RANKB])
-                if t == 0:
-                    lists_of_candidates()
-                    for b in range(4):
-                        qz("e", 128 * b, 128 * b + 128, T.et[:, 3 - b:515 - b], r=["et"], w=["eq%d" % b])
-                for b in range(4):
-                    mm(b, "e", 128 * b, tn, 0, C, True, True, [tn + "_0", tn + "_1", "eq%d" % b])
+            elif k == "dm":
+                mm(n, "e", 128 * n, tn, 0, C, True, True, [tn + "_0", tn + "_1", "eq%d" % n])
             elif k == "gx":
                 move(q, T.gx[:, 256 * n:256 * n + 256], T.tab[:].indirect(T.off1[:, 32 * t + 16 * n:32 * t + 16 * n + 16]), r=["tab", "off1"], w=["gx%d" % n])
             elif k == "tr":
@@ -507,95 +554,35 @@ def rank_program(g, core, T, topo):
             elif k == "fl":
                 ts(T.fl[:], T.ty[:], float(TH), OP.is_lt, r=["ty"], w=["fl"])
             elif k == "lcp":
-                move(q, T.lcp[:], T.ty[:].indirect(T.offc[:, 40:56]), r=["ty", "offL"], w=["lcp"])
+                act(T.lcp[:], T.ty[:].indirect(T.offc[:, 40:56]), AF.Copy, {"scale": 2.0 ** -9}, r=["ty", "offL"], w=["lcp"])
             elif k == "dl":
                 tt(T.dl[:, 1:256], T.lcp[:, 1:256], T.lcp[:, 0:255], OP.subtract, r=["lcp"], w=["dl"])
-                ts(T.l7[:], T.lcp[:, 7:256:8], -float(C), OP.add, r=["lcp"], w=["l7"])
-                iota(T.dl[:, 0:256:8], [[0, 32]], -2 ** 20, 0, ["dl"])
+                iota(T.dl[:, 0:256:8], [[0, 32]], -1000, 0, ["dl"])
+            elif k == "l":
+                ts(T.l7[:], T.lcp[:, 7:256:8], -C * 2.0 ** -9, OP.add, r=["lcp"], w=["l7"])
             elif k == "dp":
                 move(q, T.dp[:, C * n:C * n + C], ps(n, C), w=["dp%d" % n], b=[n])
             elif k == "scan":
                 for i in range(4):
                     scan(T.fs[:, 128 * i:128 * i + 128], got[:], T.fl[:, 128 * i:128 * i + 128], OP.mult, OP.add, r=[gk, "fl"], w=["fs%d" % i])
-            elif k == "f":
-                ts(T.f2[:], T.fs[:], 255.0 + 2.0 ** -8, OP.add, 256.0, OP.max, r=["fs%d" % i for i in range(4)], w=["f2"])
             elif k == "nn":
-                args = (T.nn[:, 128 * n:128 * n + 128], T.f2[:].indirect(T.offc[:, 56 + 8 * n:64 + 8 * n]))
-                if q == "V":
-                    ts(*args, 256.0, OP.mult, -192.0 * 512, OP.add, r=["f2", "offN"], w=["nn%d" % n])
-                else:
-                    act(*args, AF.Copy, {"scale": 256.0, "bias": -192.0 * 512}, r=["f2", "offN"], w=["nn%d" % n])
+                ts(T.nn[:], T.fs[:].indirect(T.offc[:, 56:72]), 0.5, OP.mult, -64.5 + 2.0 ** -10, OP.add, r=["fs%d" % i for i in range(4)] + ["offN"], w=["nn"])
+            elif k == "km":
+                scan(T.km[:], T.dl[:], T.nn[:], OP.add, OP.max, r=["dl", "nn"], w=["km"])
             else:
-                scan(T.km[:], T.dl[:], T.nn[:], OP.add, OP.max, r=["dl", "nn0", "nn1"], w=["km"])
                 for a in range(4):
                     tt(T.tmp[0:32, a:128:4], T.l7[32 * a:32 * a + 32, :], T.km[32 * a:32 * a + 32, 7:256:8], OP.subtract, r=["km", "l7"], w=["tmp%d" % a])
                 for b in range(4):
                     tr(T.tp[32 * b:32 * b + 32, :], T.tmp[0:32, 32 * b:32 * b + 32], r=["tmp%d" % a for a in range(4)], w=["tp%d" % b])
-                ts(T.ti[:], T.tp[:], 512.0, OP.mult, r=["tp%d" % b for b in range(4)], w=["ti"])
+                ts(T.ti[:], T.tp[:], 2.0 ** 18, OP.mult, r=["tp%d" % b for b in range(4)], w=["ti"])
                 ts(T.tj[:], T.ti[:], 511, OP.bitwise_and, r=["ti"], w=["tj"])
                 cp(T.offz[:], T.tj[:], r=["tj"], w=["offz"])
 
-        weave({"V": CANV, "A": CANA}, need, run)
-
-    def layer(t, child):
-        hn = "h%d" % t
-        runs = RUNS[t + 1]
-
-        def need(w):
-            c = w[1]
-            return {"z": [], "g": ["q" + c], "q": ["z%s%d" % (c, b) for b in range(4)], "h": ["g%s%d" % (c, b) for b in range(4)]}[w[0]]
-
-        def run(q, w):
-            c = int(w[1])
-            a, e = runs[c]
-            if w[0] == "z":
-                b = int(w[2])
-                move(q, T.zt[:, 4 * a + b:4 * e:4], T.dp[:, C * b:C * b + C].indirect(T.offz[:, a // 16:e // 16]), r=["offz", "dp%d" % b], w=["z%d_%d" % (c, b)])
-            elif w[0] == "q":
-                qz("z", a, e, T.zt[:, 4 * a:4 * e], r=["z%d_%d" % (c, b) for b in range(4)], w=["zq%d" % c])
-                for b in (0, 2, 1, 3):
-                    mm(banks(c) + b, "wl", 128 * b, "z", a, e, True, True, ["zq%d" % c, "wq", "ws"])
-            elif w[0] == "g":
-                b = int(w[2])
-                k = {"w": ["g%d_%d" % (c, b)], "b": [banks(c) + b]}
-                if q == "V":
-                    ts(T.gt[:, 4 * a + b:4 * e:4], ps(banks(c) + b, e - a), 0.0, OP.max, 0.015625, OP.mult, **k)
-                else:
-                    act(T.gt[:, 4 * a + b:4 * e:4], ps(banks(c) + b, e - a), AF.Relu, {"scale": 0.015625}, **k)
-            else:
-                qz(hn, a, e, T.gt[:, 4 * a:4 * e], r=["g%d_%d" % (c, b) for b in range(4)], w=[hn + "_%d" % c])
-                sem = "ah%d_%d" % (t, c)
-                send(T["l%dq" % t][:, a:e].bitcast(dt.uint8), T[hn + "q"][:, a:e].bitcast(dt.uint8), sem, child, [hn + "_%d" % c])
-                send(T["l%ds" % t][:, a:e], T[hn + "s"][:, a:e], sem, child, [hn + "_%d" % c])
-
-        weave({"A": LAYA, "V": LAYV}, need, run)
-
-    def outputs(c):
-        nx = "t%d" % R
-        a, e = RUNS[R][c]
-        mm(banks(c), "v", 0, nx, a, e, True, True, [nx + "_%d" % c, "vq"])
-        dma("S", T.oc[:, 4 * a:4 * e], T[nx + "q"][:, a:e].bitcast(dt.uint8), r=[nx + "_%d" % c])
-        for k in range(4):
-            dma("AS"[k % 2], T.osc[4 * k:4 * k + 4, a:e], T[nx + "s"][32 * k:32 * k + 4, a:e], r=[nx + "_%d" % c])
-        cp(T.yb[:, a:e], ps(banks(c), e - a), w=["yb%d" % c], b=[banks(c)])
-        dma("A", T.y[:, a:e], T.yb[:, a:e], r=["yb%d" % c])
+        weave({"V": CANV, "A": CANA, "P": CANP}, need, run)
 
     for t in range(R):
-        donor, child = T.cores[(rank + 1 + t) % N], T.cores[(rank - 1 - t) % N]
         places(t)
-        order(t, donor)
-        leaders(t, child)
-        layer(t, child)
-        if t == 0:
-            iota(T.jrow[:], [[1, C]], 0, 0, ["jrow"])
-            qz("v", 0, 128, T.vt[:], r=["vt"], w=["vq"])
-        if t == R - 1:
-            act(T.elb[:], T.jrow[:].indirect(T.offz[:, 0:28]), AF.Copy, r=["jrow", "offz"], w=["elb"])
-            dma("S", T.el[:], T.elb[0:128:16, :], r=["elb"])
-        own_part(t)
-        whole_state(t + 1, 0)
-    outputs(0)
-    whole_state(R, 1)
-    outputs(1)
+        leaders(t)
+    places(R)
     for s, n in total.items():
         wait("G", (s, n))

@@ -2,25 +2,35 @@ import math
 from concourse.mybir import dt, AluOpType as OP, ActivationFunctionType as AF
 
 C, R, TH = 448, 3, 320
-CUT = [192, 224, 224, 224]
+CUT = [192, 256, 256, 256]
 RUNS = [[(0, k), (k, C)] for k in CUT]
 NS = C // 32
 WIDTH = [C, 384, 320, 256, 192, 128, 128, C]
-EARLY = 4
-ONE = False
+EARLY = 5
+EARLY0 = 6
+SPLIT = True
+TABCUT = 192
+GXCUT = 22
+ZCUT = 96
+PIECE = 128
+BORD = (2, 0, 3, 1)
+UNIT = 2.0 ** -9
 SMALL = 2.0 ** -10
-PLV = "z0.0 z0.1 z1.0 zq0 z1.1 zq1 g0.0 g0.1 h0 g1.0 g1.1 h1 x0.0 x0.1 xq0 x1.0 x1.1 tr0 xq1 u3 u2 u1 u0 tr1 q5 q6 u13.0 u12.0 u13.1 u12.1 u9.0 q0 u9.1 u8 u7.0 q2 u7.1 u6 u5.0 q3 u4 q1 eq0 round eq1 parts q4 trr q7"
-PLA = "z0.2 z0.3 z1.2 z1.3 g0.2 g0.3 g1.2 g1.3 x0.2 x0.3 x1.2 x1.3 sum3 sum2 sum1 s11.1 s10.1 r11.1 s11.0 r10.1 s10.0 r11.0 r10.0 sum13 sum12 s5.1 sum9 r5.1 sum8 sum5 sum4 sum7 sum6"
-PLP = "w0 w1 own0 own1 dec0 dec1 sm0 sv0.0 sv0.1 sm1 sv1.0 sa1.1 sv1.1 sa1.0 rs13 rs12 col0 col5 col6 rs9 rs8 col2 rs7 rs6 col3 col1 col4 col7"
-CANV = "wo oq tab gx0 tr fl dl scan l7 nn km tmp"
+PLV = "z0.0 z0.1 z1.0 zq0 z1.1 z2.0 zq1 g0.0 g0.1 za2.1 h0 zb2.1 g1.0 g1.1 zq2 h1 g2.0 g2.1 h2 x0.0 x0.1 xq0 tr0 x1.0 x1.1 u4.0 xq1 u4.1 u3 u2 u1.0 tr1 u1.1 u0 u13.0 u12.0 u13.1 u12.1 u7.0 q0 u7.1 u9 u8 u6.0 q2 u6.1 u5 q5 q1 eq0 eq1 round q4 parts q3 trr q6 q7"
+PLA = "z0.2 z0.3 z1.2 z1.3 z2.2 g0.2 g0.3 z2.3 g1.2 g1.3 g2.2 g2.3 x0.2 x0.3 x1.2 x1.3 sum4 sum3 sum2 s11.1 s10.1 r11.1 s11.0 r10.1 s10.0 r11.0 r10.0 sum1 sum7 sum13 sum12 sum6 sum9 sum8 sum5"
+PLP = "w0 w1 w2 own1 own0 dec0 sm0 dec1 sv0.0 sv0.1 sm1 sv1.0 sa1.1 sv1.1 sa1.0 rs13 rs12 col0 rs9 rs8 col2 col5 col1 col4 col3 col6 col7"
+CANV = "wo tab0 oq tab1 gx0 tr fl dl scan l7 nn km tmp"
 CANA = "exp gx1 lcp dp0 dp1 dp2 dp3"
 CANP = "om dm0 dm1 dm2 dm3"
-FIRST = {"tr0": "k2 tr0 k3", "tr1": "k4 tr1", "q0": "k1 q0", "q2": "k5 q2", "round": "round k6", "parts": "parts k7", "trr": "trr k8", "q7": "q7 k9"}
-ENDV = "z0.0 z0.1 z1.0 zq0 z1.1 zq1 g0.0 g0.1 g1.0 h0 g1.1 h1 x0.0 x0.1 xq0 x1.0 x1.1 out0 xq1 out1"
-ENDA = "z0.2 z0.3 z1.2 z1.3 g0.2 g0.3 g1.2 g1.3 el0 x0.2 x0.3 x1.2 x1.3 os0.0 os0.2 os1.0 os1.2"
-ENDP = "w0 w1 own0 own1 dec0 dec1 y0 y1"
-ENDS = "oc0 os0.1 os0.3 oc1 os1.1 os1.3"
-MIXB, VB, AB = [4, 0], [[5, 6], [1, 2]], [[4, 7], [3, 4]]
+FIRSTV = "xq0 k19 xq1 tr0 k11 k2 tr1 k1 k3 u3 u2 u1 u0 u4 u13.0 u12.0 u13.1 u12.1 u7.0 q0 u7.1 u9 u8 u6.0 q2 u6.1 q5 k4 q1 k12 k5 eq0 eq1 round q4 parts q3 trr q6 q7 k14 k9 k6"
+FIRSTA = "k0 s5.1 s5.0 r5.1 r5.0 sum3 sum2 s11.1 s10.1 r11.1 s11.0 r10.1 s10.0 r11.0 r10.0 sum1 sum4 sum7 sum13 sum12 sum6 sum9 sum8 k17 jt"
+FIRSTP = "sm0 sa0.1 sm1 sv0.0 sv0.1 sa0.0 sv1.0 sa1.1 sv1.1 sa1.0 rs13 rs12 col0 rs9 rs8 col2 col5 col1 col4 col3 col6 col7"
+FIRSTC = "wo k7 oq k8 tab0 tab1 unit0 gx0 tr unit1 fl unit2 dl scan l7 unit3 nn km tmp"
+ENDV = "z0.0 z0.1 z1.0 zq0 z1.1 z2.0 zq1 g0.0 g0.1 za2.1 h0 zb2.1 g1.0 g1.1 zq2 h1 g2.0 g2.1 h2 x0.0 x0.1 xq0 x1.0 x1.1 out0 xq1 out1"
+ENDA = "z0.2 z0.3 z1.2 z1.3 z2.2 g0.2 g0.3 z2.3 g1.2 g1.3 g2.2 g2.3 el0 x0.2 x0.3 x1.2 x1.3"
+ENDP = "w0 w1 w2 own1 own0 dec0 dec1 y0 y1"
+ENDS = "oc0 os0.0 os0.1 os0.2 os0.3 oc1 os1.0 os1.1 os1.2 os1.3"
+MIX, VB, AB = [4, 0], [[5, 6], [1, 2]], [[4, 7], [3, 4]]
 SUMB, RANKB, ORDB = [0, 5, 6], 7, 5
 
 BF, F32, I32, U16, Q, U8 = "bfloat16", "float32", "int32", "uint16", "float8_e4m3fn_x4", "uint8"
@@ -39,13 +49,13 @@ def _mx(name, n):
 for _n, _w, _d in [
     ("xin", 4 * C, BF), ("xt", 4 * C, BF), ("ut", 512, BF), ("vt", 512, BF), ("cds", 128, I32), ("cdg", 128, F32), ("cdt", 128, F32),
     ("off1", 96, U16), ("et", 520, BF), ("rt", 520, BF), ("ones", 520, BF), ("zer", 520, BF), ("cst", 512, BF), ("csh", 512, BF), ("c2", 512, BF),
-    ("pb", 128, F32), ("pc", 128, F32), ("pi", 8, I32), ("ci", 8, I32), ("cf", 8, F32), ("col", 16, F32), ("ib", 72, F32), ("offc", 72, U16),
+    ("pb", 168, F32), ("pc", 160, F32), ("pi", 8, I32), ("ci", 8, I32), ("cf", 8, F32), ("col", 16, F32), ("ib", 72, F32), ("offc", 88, U16),
     ("ig", 128, BF), ("ia", 128, BF), ("ca", 384, BF), ("cb", 384, BF), ("r32", 32, BF), ("i32w", 32, F32), ("r32b", 32, BF),
     ("j0", C, F32), ("jt", C, F32), ("jrow", C, F32),
     ("m1", C, F32), ("st", C, F32), ("sg", 16 * C, BF), ("junk", 5824, BF), ("racc", 28, F32), ("ra", 64, F32), ("rp", C, BF),
-    ("wo", 512, BF), ("tab", C, F32), ("gx", 512, F32), ("ty", 512, F32), ("fl", 512, BF), ("lcp", 256, F32), ("dl", 256, F32), ("l7", 32, F32),
+    ("wo", 512, BF), ("tab", C, F32), ("gx", 512, F32), ("ty", 640, F32), ("fl", 512, BF), ("lcp", 256, F32), ("dl", 256, F32), ("l7", 32, F32),
     ("fs", 512, BF), ("nn", 256, I32), ("km", 256, F32),
-    ("tmp", 128, F32), ("tp", 32, F32), ("ti", 32, I32), ("tj", 32, I32), ("offz", 32, U16),
+    ("tmp", 128, F32), ("tp", 232, F32), ("tq", 224, F32), ("offz", 32, U16),
     ("dp", 4 * C, BF), ("zt", 4 * C, BF), ("gt", 4 * C, BF), ("yb", C, F32), ("elb", C, F32),
 ]:
     _sb(_n, _w, _d)
@@ -68,10 +78,6 @@ def parse(w):
     k = w.rstrip("0123456789.")
     n = [int(x) for x in w[len(k):].split(".") if x]
     return (k, n[0] if n else None, n[1] if len(n) > 1 else None)
-
-
-BY_ACT = [parse(w)[1:] for w in PLA.split() if parse(w)[0] == "s"]
-BY_PE = [parse(w)[1] for w in PLP.split() if parse(w)[0] == "rs"]
 
 
 def rank_program(g, core, T, topo):
@@ -217,16 +223,19 @@ def rank_program(g, core, T, topo):
     iota(T.ig[:], [[0, 16], [1, 8]], 0, 0, ["ig"])
     iota(T.ia[:], [[1, 8], [-100, 2], [0, 8]], 100, 0, ["ia"])
     ms(T.zer[:], 0.0, w=["zer"])
-    act(T.ones[:], T.zer[:], AF.Exp, r=["zer"], w=["ones"])
     ms(T.cds[:], 0, w=["cds"])
+    for out, n, w in ((T.rt[:], 520, ["rt"]), (T.c2[:], 512, ["c2z"]), (T.wo[:], 512, ["wo0", "wo1", "wo2", "wo3"]), (T.k7[:, 3:4 * C:4], C, ["kz7"]),
+                      (T.rp[:], C, ["rp0", "rp1", "rp8", "rp9"])):
+        act(out, T.zer[:, 0:n], AF.Copy, r=["zer"], w=w)
     for a in range(4):
-        dma("S", T.cds[32 * a:32 * a + 24, 0:112], T.cd[a::4, :], r=["cds"], w=["cds%d" % a])
+        dma("S", T.cds[32 * a:32 * a + 24, 0:112], T.cd[a::4, :], r=["cds", "xin0", "xin1"], w=["cds%d" % a])
     dma("S", T.wlq[:].bitcast(dt.uint8), T.wc[:], w=["wq"])
     dma("S", T.wls[:], T.ws[:], w=["ws"])
     dma("S", T.vt[:], T.v[:], w=["vt"])
     for i, (sh, m) in enumerate([(5, 3), (4, 7), (0, 1), (3, 1), (0, 15)]):
         ts(T.ci[:, i:i + 1], T.pi[:, 0:1], sh, OP.logical_shift_right, m, OP.bitwise_and, r=["pi"], w=["ci%d" % i])
-    ms(T.rt[:], 0.0, w=["rt"])
+    ms(T.ones[:], 1.0, w=["ones"])
+    sel(T.rt[:, 1:513:2], T.ones[:, 0:256], [[-1, 128], [0, 2]], OP.is_equal, 1, r=["ones"], w=["rt"])
     cp(T.cf[:, 0:5], T.ci[:, 0:5], r=["ci%d" % i for i in range(5)], w=["cf"])
     run32, pg, odd, bit3, l16 = [T.cf[:, i:i + 1] for i in range(5)]
     pa0, pa1, pr, wr, mix, tie = [T.col[:, i:i + 1] for i in range(6)]
@@ -237,13 +246,10 @@ def rank_program(g, core, T, topo):
     ts(pa0, run32, 2.0, OP.mult, r=["cf"], w=["pa0"])
     ts(pa1, run32, 2.0, OP.mult, 1.0, OP.add, r=["cf"], w=["pa1"])
     ts(pr, run32, 2.0, OP.mult, bit3, OP.add, r=["cf"], w=["pr"])
-    ts(wr, bit3, 1.0 - 1.0 / SMALL, OP.mult, -1.0, OP.add, r=["cf"], w=["wr"])
+    ts(wr, bit3, UNIT - UNIT / SMALL, OP.mult, -UNIT, OP.add, r=["cf"], w=["wr"])
     ms(T.racc[:], 0.0, w=["racc0"])
     ms(T.csh[:, 3:512:4], 0.0, w=["csh3"])
     ts(T.offc[:, 16:24], T.ib[:, 16:24], mix, OP.add, r=["ibU", "mix"], w=["offM"])
-    for i in range(6):
-        ms(T["k%d" % i][:, 4 * WIDTH[i] - 127:4 * WIDTH[i]:2], 0.0, w=["kz%d" % i])
-    act(T.c2[:], T.zer[:, 0:512], AF.Copy, r=["zer"], w=["c2z"])
 
     def counter(n, out, colap, weight, keys, w):
         x0, x1 = T.ca[:, 128 * n:128 * n + 128], T.cb[:, 128 * n:128 * n + 128]
@@ -251,28 +257,34 @@ def rank_program(g, core, T, topo):
         ts(x1, T.ia[:], colap, OP.is_equal, weight, OP.mult, r=["ia"] + keys, w=["cb%d" % n])
         return lambda: tt(out, x0, x1, OP.subtract, r=["ca%d" % n, "cb%d" % n], w=[w])
 
-    counters = [counter(0, T.cst[:, 0:512:4], pa0, 1.0, ["pa0"], "cst0"), counter(1, T.csh[:, 2:512:4], pa1, 1.0, ["pa1"], "csh2"),
+    counters = [counter(0, T.cst[:, 0:512:4], pa0, UNIT, ["pa0"], "cst0"), counter(1, T.csh[:, 2:512:4], pa1, UNIT, ["pa1"], "csh2"),
                 counter(2, T.csh[:, 1:512:4], pr, wr, ["pr", "wr"], "csh1")]
+    for i in range(6):
+        ms(T["k%d" % i][:, 4 * WIDTH[i] - 127:4 * WIDTH[i]:2], 0.0, w=["kz%d" % i])
+    for o in range(2):
+        qz("rs", 128 * o, 128 * o + 128, T.rt[:, 1 - o:513 - o], r=["rt"], w=["rs%d" % o])
     qz("u", 0, 128, T.ut[:], r=["ut"], w=["uq"])
-    ms(T.rp[:], 0.0, w=["rp0", "rp1", "rp8", "rp9"])
-    cp(T.ubq[:].bitcast(dt.uint32), T.uq[:].bitcast(dt.uint32).indirect(T.offc[:, 0:24]), r=["uq", "offU", "offM"], w=["ubq"])
-    act(T.ubs[:], T.us[:].indirect(T.offc[:, 0:24]), AF.Copy, r=["uq", "offU", "offM"], w=["ubs"])
-    for c, (a, e) in enumerate(RUNS[0]):
-        qz("t0", a, e, T.xin[:, 4 * a:4 * e], r=["xin%d" % c], w=["t0_%d" % c])
-    for last in counters:
-        last()
+    counters[0]()
+    counters[1]()
+
+    def repeat_u(c, i, j):
+        cp(T.ubq[:, 16 * i:16 * j].bitcast(dt.uint32), T.uq[:].bitcast(dt.uint32).indirect(T.offc[:, i:j]), r=["uq", "offU", "offM"], w=["ubq%d" % c])
+        act(T.ubs[:, 16 * i:16 * j], T.us[:].indirect(T.offc[:, i:j]), AF.Copy, r=["uq", "offU", "offM"], w=["ubs%d" % c])
+
+    repeat_u(0, 16, 24)
     iota(T.pb[:, 0:32], [[0, 2], [2000, 2], [0, 8]], 0, 0, ["pb2"])
     iota(T.pb[:, 96:128], [[0, 2], [100, 2], [-1, 8]], -100, 0, ["pb5"])
     for hf in range(2):
         iota(T.pb[:, 32 + 16 * hf:48 + 16 * hf], [[64, 2], [6, 4], [32, 2]], 0, 0, ["pb3%d" % hf])
         iota(T.pb[:, 64 + 16 * hf:80 + 16 * hf], [[32, 2], [128, 4], [16, 2]], 0, 0, ["pb4%d" % hf])
+        iota(T.pb[:, 129 + 16 * hf:145 + 16 * hf], [[32, 2], [128, 4], [16, 2]], 0, 0, ["pb6"])
+    iota(T.pb[:, 128:160:8], [[0, 4]], 512, 0, ["pb6"])
     iota(T.i32w[:], [[0, 4], [1, 8]], 0, 0, ["i32w"])
     iota(T.ib[:, 24:32], [[56, 2], [16, 2], [28, 2]], 0, 0, ["ibA"])
     iota(T.ib[:, 32:40], [[1, 8]], 0, 0, ["ibB"])
     iota(T.ib[:, 40:56], [[1, 8], [64, 2]], 0, 0, ["ibL"])
     iota(T.ib[:, 56:72], [[1, 8], [64, 2]], 8, 0, ["ibN"])
-    sel(T.rt[:, 1:513:2], T.ones[:, 0:256], [[-1, 128], [0, 2]], OP.is_equal, 1, r=["ones"], w=["rt"])
-    sel(T.et[:, 0:516], T.ones[:, 0:516], [[-1, 516]], OP.is_equal, 4, 3, r=["ones"], w=["et"])
+    iota(T.j0[:], [[32 * 513, NS], [2, 16], [513, 2]], -512 - C // 2, 0, ["j0"])
 
     def constants_0():
         for t in (2, 3):
@@ -281,12 +293,10 @@ def rank_program(g, core, T, topo):
         act(T.csh[:, 0:512:4], T.cst[:, 0:512:4], AF.Copy, r=["cst0"], w=["csh0"])
 
     def constants_1():
-        for o in range(2):
-            qz("rs", 128 * o, 128 * o + 128, T.rt[:, 1 - o:513 - o], r=["rt"], w=["rs%d" % o])
         qz("cs", 0, 128, T.cst[:], r=["cst%d" % t for t in range(4)], w=["cs"])
 
     def constants_2():
-        tr(T.pc[:], T.pb[:], r=["pb2", "pb30", "pb31", "pb40", "pb41", "pb5"], w=["pc"])
+        tr(T.pc[:], T.pb[:, 0:160], r=["pb2", "pb30", "pb31", "pb40", "pb41", "pb5", "pb6"], w=["pc"])
         ts(T.r32[:], T.i32w[:], pg, OP.is_equal, r=["i32w", "cf"], w=["r32"])
         ts(T.r32b[:], T.i32w[:], -1.0, OP.add, pg, OP.is_equal, r=["i32w", "cf"], w=["r32b"])
 
@@ -295,20 +305,27 @@ def rank_program(g, core, T, topo):
         ts(T.r32b[:, 0:32:8], T.i32w[:, 0:32:8], 7.0, OP.add, pg, OP.is_equal, r=["i32w", "cf"], w=["r32b"])
 
     def constants_4():
-        ts(tie, T.col[:, 8:9], -0.5, OP.max, r=["tie0"], w=["tie"])
+        ts(tie, T.col[:, 8:9], -0.5, OP.max, UNIT, OP.mult, r=["tie0"], w=["tie"])
         tt(T.r32[:], T.r32[:], T.r32b[:], OP.subtract, r=["r32b"], w=["r32"])
-        iota(T.r32[:, 0:32:16], [[0, 2]], -8, 0, ["r32"])
+
+    def ratios():
         for b in range(4):
-            sel(T.c2[:, 129 * b:128 * b + 128:4], T.r32[:], [[0, 32]], OP.is_ge, 0, r=["r32", "c2z"], w=["c2r%d" % b])
+            act(T.c2[:, 129 * b:128 * b + 128:4], T.r32[:], AF.Copy, r=["r32", "c2z"], w=["c2r%d" % b])
+
+    def after_mask():
+        sel(T.et[:, 0:516], T.ones[:, 0:516], [[-1, 516]], OP.is_equal, 4, 3, r=["ones"], w=["et"])
+        big = int(1.5 * 2 ** 23 * UNIT)
+        for i, c in ((0, 0), (2, 1), (3, -1), (4, -1), (5, big), (6, -big)):
+            iota(T.tp[:, i:232:7], [[0, len(range(i, 232, 7))]], c, 0, ["steps%d" % i] if i < 6 else ["steps"])
+        iota(T.jrow[:], [[1, C]], 0, 0, ["jrow"])
 
     def constants_5():
-        zero(T.k7[:, 3:4 * C:4], ["kz7"])
-        iota(T.j0[:], [[32 * 513, NS], [2, 16], [513, 2]], -512, 0, ["j0"])
-        zero(T.wo[:], ["wo0", "wo1", "wo2", "wo3"])
-        iota(T.jrow[:], [[1, C]], 0, 0, ["jrow"])
         qz("cs", 128, 256, T.csh[:], r=["csh%d" % t for t in range(4)], w=["csh"])
+
+    def lists():
         for nm, a, b_, c in (("A", 24, 32, l16), ("B", 32, 40, T.pc[:, 32:33]), ("L", 40, 56, T.pc[:, 64:65]), ("N", 56, 72, T.pc[:, 64:65])):
             ts(T.offc[:, a:b_], T.ib[:, a:b_], c, OP.add, r=["ib" + nm, "cf", "pc"], w=["off" + nm])
+        ts(T.offc[:, 72:88], T.ib[:, 40:56], T.pc[:, 128:129], OP.add, r=["ibL", "pc"], w=["offP"])
 
     def unit(b):
         qz("e", 128 * b, 128 * b + 128, T.et[:, 3 - b:515 - b], r=["et"], w=["eq%d" % b])
@@ -316,9 +333,12 @@ def rank_program(g, core, T, topo):
     CONST = [constants_0, constants_1, constants_2, constants_3, constants_4, constants_5,
              lambda: cp(T.cdg[:], T.cds[:].indirect(T.offc[:, 24:32]), r=["offA"] + ["cds%d" % a for a in range(4)], w=["cdg"]),
              lambda: tr(T.cdt[:], T.cdg[:], r=["cdg"], w=["cdt"]),
-             lambda: [cp(T.off1[:], T.cdt[:].indirect(T.offc[:, 32:38]), r=["cdt", "offB"], w=["off1"]), unit(0)],
-             lambda: [qz("cc", 0, 128, T.c2[:], r=["c2r%d" % b for b in range(4)], w=["cc"]), unit(1), unit(2), unit(3)],
-             lambda: qz("v", 0, 128, T.vt[:], r=["vt"], w=["vq"])]
+             lambda: cp(T.off1[:], T.cdt[:].indirect(T.offc[:, 32:38]), r=["cdt", "offB"], w=["off1"]),
+             lambda: qz("cc", 0, 128, T.c2[:], r=["c2r%d" % b for b in range(4)], w=["cc"]),
+             lambda: qz("v", 0, 128, T.vt[:], r=["vt"], w=["vq"]),
+             counters[2], lambda: ms(T.r32[:, 0:32:16], -8.0, w=["r32"]),
+             lambda: ms(T.racc[:], 0.0, w=["racc0"] + ["racc%d_%d" % (s, h) for s in range(NS) for h in range(2)]),
+             lists, None, None, ratios, after_mask, lambda: repeat_u(1, 0, 16)]
 
     def banks(c):
         return 4 * ((c + 1) % 2)
@@ -326,20 +346,23 @@ def rank_program(g, core, T, topo):
     def four(k, c):
         return ["%s%d.%d" % (k, c, b) for b in range(4)]
 
-    LAYER = {"z": lambda c: [], "zq": lambda c: four("z", c), "w": lambda c: ["zq%d" % c], "g": lambda c: ["w%d" % c], "h": lambda c: four("g", c),
-             "own": lambda c: four("g", c), "dec": lambda c: ["own%d" % c], "x": lambda c: ["dec%d" % c], "xq": lambda c: four("x", c),
+    LAYER = {"z": lambda c: [], "za": lambda c: [], "zb": lambda c: [], "zq": lambda c: four("z", c) + four("za", c) + four("zb", c),
+             "w": lambda c: ["zq%d" % c] + four("g", c - 2), "g": lambda c: ["w%d" % c], "h": lambda c: four("g", c) + ["h%d" % (c - 1)],
+             "own": lambda c: four("g", c) + four("g", c + 2), "dec": lambda c: ["own%d" % c], "x": lambda c: ["dec%d" % c], "xq": lambda c: four("x", c),
              "y": lambda c: ["xq%d" % c], "out": lambda c: ["y%d" % c], "oc": lambda c: ["xq%d" % c], "os": lambda c: ["xq%d" % c], "el": lambda c: []}
 
     def layer(q, k, c, b, t):
         on, hn, ln, nx = "t%d" % (t - 1), "h%d" % (t - 1), "l%d" % (t - 1), "t%d" % t
-        a, e = RUNS[t][c]
+        a, e = [(0, PIECE), (PIECE, CUT[t]), (CUT[t], C)][c] if k in ("z", "za", "zb", "zq", "w", "g", "h") else RUNS[t][c]
         donor, child = T.cores[(rank + t) % N], T.cores[(rank - t) % N]
-        if k == "z":
-            move(q, T.zt[:, 4 * a + b:4 * e:4], T.dp[:, C * b:C * b + C].indirect(T.offz[:, a // 16:e // 16]), r=["offz", "dp%d" % b], w=["z%d_%d" % (c, b)])
+        if k in ("z", "za", "zb"):
+            a, e = a + ZCUT * (k == "zb"), a + ZCUT if k == "za" else e
+            move(q, T.zt[:, 4 * a + b:4 * e:4], T.dp[:, C * b:C * b + C].indirect(T.offz[:, a // 16:e // 16]), r=["offz", "dp%d" % b],
+                 w=["%s%d_%d" % (x, c, b) for x in (("za", "zb") if k == "z" else (k,))])
         elif k == "zq":
-            qz("z", a, e, T.zt[:, 4 * a:4 * e], r=["z%d_%d" % (c, b) for b in range(4)], w=["zq%d" % c])
+            qz("z", a, e, T.zt[:, 4 * a:4 * e], r=["%s%d_%d" % (x, c, b) for x in ("za", "zb") for b in range(4)], w=["zq%d" % c])
         elif k == "w":
-            for b in (0, 2, 1, 3):
+            for b in BORD:
                 mm(banks(c) + b, "wl", 128 * b, "z", a, e, True, True, ["zq%d" % c, "wq", "ws"])
         elif k == "g":
             kw = {"w": ["g%d_%d" % (c, b)], "b": [banks(c) + b]}
@@ -349,23 +372,22 @@ def rank_program(g, core, T, topo):
                 act(T.gt[:, 4 * a + b:4 * e:4], ps(banks(c) + b, e - a), AF.Relu, {"scale": 0.015625}, **kw)
         elif k == "h":
             qz(hn, a, e, T.gt[:, 4 * a:4 * e], r=["g%d_%d" % (c, b) for b in range(4)], w=[hn + "_%d" % c])
-            sem = "ah%d_%d" % (t - 1, c)
-            if ONE:
-                a, keys = 0, [hn + "_0", hn + "_1"]
-            else:
-                keys = [hn + "_%d" % c]
-            if c or not ONE:
-                send(T[ln + "q"][:, a:e].bitcast(dt.uint8), T[hn + "q"][:, a:e].bitcast(dt.uint8), sem, child, keys)
-                send(T[ln + "s"][:, a:e], T[hn + "s"][:, a:e], sem, child, keys)
+            sem = "ah%d_%d" % (t - 1, c // 2)
+            send(T[ln + "q"][:, a:e].bitcast(dt.uint8), T[hn + "q"][:, a:e].bitcast(dt.uint8), sem, child, [hn + "_%d" % c])
+            if c:
+                a = RUNS[t][c // 2][0]
+                send(T[ln + "s"][:, a:e], T[hn + "s"][:, a:e], sem, child, [hn + "_0", hn + "_%d" % c])
         elif k == "own":
             for b in (0, 2, 1, 3):
                 mm(banks(c) + b, "e", 128 * b, on, a, e, True, False, [on + "_0", on + "_1"])
         elif k == "dec":
-            arrives(ln + "_%d" % c, "ah%d_%d" % (t - 1, 1 if ONE else c), 2 * width(donor, core))
-            for b in (0, 2, 1, 3):
+            arrives(ln + "_%d" % c, "ah%d_%d" % (t - 1, c), (3 - c) * width(donor, core))
+            for b in BORD:
                 mm(banks(c) + b, "e", 128 * b, ln, a, e, False, True, [ln + "_%d" % c])
         elif k == "x":
             move(q, T.xt[:, 4 * a + b:4 * e:4], ps(banks(c) + b, e - a), w=["x%d_%d" % (c, b)], b=[banks(c) + b])
+        elif k == "xq" and t == 0:
+            qz(nx, a, e, T.xin[:, 4 * a:4 * e], r=["xin%d" % c], w=[nx + "_%d" % c])
         elif k == "xq":
             qz(nx, a, e, T.xt[:, 4 * a:4 * e], r=["x%d_%d" % (c, b) for b in range(4)], w=[nx + "_%d" % c])
         elif k == "y":
@@ -405,10 +427,18 @@ def rank_program(g, core, T, topo):
 
     def places(t):
         tn, CH = "t%d" % t, RUNS[t]
-        cut = EARLY
+        cut, MIXB = EARLY if t else EARLY0, MIX
+        queues = {"P": PLP, "G": "mask0 mask1", "V": PLV.replace("h2", "h2 k10 k13") if t == 1 else PLV, "A": PLA}
+        if t == 0:
+            queues = {"P": FIRSTP, "G": "mask0 mask1 k18", "V": FIRSTV, "A": FIRSTA}
+        if t == R:
+            queues = {"P": ENDP, "V": ENDV, "A": ENDA, "S": ENDS}
+        BY_ACT = [parse(w)[1:] for w in queues["A"].split() if parse(w)[0] == "s"]
+        OWN = [parse(w)[1:] for w in queues["V"].split() if parse(w)[0] == "d"]
+        BY_PE = [parse(w)[1] for w in queues["P"].split() if parse(w)[0] == "rs"]
 
         def made(blocks):
-            return [x % (s, h) for s in blocks for h in range(2) for x in ("u%d.%d", "r%d.%d")] + ["u%d" % s for s in blocks]
+            return [x % (s, h) for s in blocks for h in range(2) for x in ("u%d.%d", "r%d.%d", "d%d.%d")] + ["u%d" % s for s in blocks]
 
         early = made(range(cut))
         rk = ["racc0"] + ["racc%d_%d" % (s, h) for s in range(NS) for h in range(2)]
@@ -419,16 +449,17 @@ def rank_program(g, core, T, topo):
             c = int(n is not None and n >= cut)
             if k in LAYER:
                 return LAYER[k](n)
-            if k in ("u", "s"):
-                return ["tr%d" % int(32 * n >= CUT[t])] + ["s%s%d.%d" % ("v" if k == "u" else "a", c, x) for x in range(2) if h in (None, x)]
+            if k in ("u", "s", "d"):
+                return ["tr%d" % int(32 * n >= CUT[t])] + ["s%s%d.%d" % ("a" if k == "s" else "v", c, x) for x in range(2) if h in (None, x)]
             if k in ("sm", "sv", "sa"):
-                return ["xq%d" % n] + (["tr0"] + ["s%d.0" % s for s in range(cut) if n] if k == "sa" and AB[n][h] == MIXB[0] else [])
+                return ["xq%d" % n] + ["k19"] * (k != "sm") + (["tr0"] + ["s%d.0" % s for s in range(cut) if n] if k == "sa" and AB[n][h] == MIXB[0] else [])
             if k == "rs":
-                return ["k1", "q%d" % tile_of(n)] + ["sum%d" % s for s in BY_PE[:max(0, BY_PE.index(n) + 1 - len(SUMB))]] + early
+                return ["q%d" % tile_of(n)] + ["sum%d" % s for s in BY_PE[:max(0, BY_PE.index(n) + 1 - len(SUMB))]] + early
             if k == "q":
                 return made([NS - 1 - 2 * n, NS - 2 - 2 * n]) if n < 7 else ["trr", "eq0", "eq1"]
-            return {"k": {1: ["k0"], 5: ["k0", "mask"]}.get(n, []), "jt": ["k5"], "mask": ["tr0", "tr1", "k4"], "tr": ["sm%s" % n], "r": ["s%s.%s" % (n, h)],
-                    "eq": ["mask", "sv1.0", "sv1.1"], "sum": ["rs%s" % n] + made([n or 0]), "col": ["k1", "q%s" % n] + early,
+            return {"k": {0: ["k19"], 1: ["k0"], 3: ["k2"], 4: ["k3"], 5: ["k0", "k11"], 6: ["k14"], 7: ["k6"], 8: ["k7"], 9: ["k17"], 12: ["k4"], 14: ["k2"], 15: ["k18"], 16: ["k18"],
+                          17: ["k12"], 18: ["mask1"]}.get(n, []), "jt": ["k2"], "mask": ["tr0", "tr%s" % n], "tr": ["sm%s" % n], "r": ["s%s.%s" % (n, h)],
+                    "eq": ["mask0", "mask1", "sv1.0", "sv1.1"], "sum": ["rs%s" % n] + made([n or 0]), "col": ["k1", "q%s" % n] + early + ["k5"] * (n == 7),
                     "round": ["sum%d" % s for s in range(NS)] + made(range(NS)), "parts": ["round"], "trr": ["parts"]}.get(k, [])
 
         def unit_in(s, h, bk):
@@ -441,10 +472,11 @@ def rank_program(g, core, T, topo):
             elif k == "k":
                 CONST[n]()
             elif k == "jt":
-                act(T.jt[:], T.j0[:], AF.Identity, {"scale": 2.0 ** -9, "bias": T.pc[:, 0:1]}, r=["j0", "pc"], w=["jt"])
+                act(T.jt[:], T.j0[:], AF.Identity, {"scale": UNIT * UNIT, "bias": T.pc[:, 0:1]}, r=["j0", "pc"], w=["jt"])
+                act(T.ty[:, 512:640], T.zer[:, 0:128], AF.Exp, {"bias": 7.0}, r=["zer"], w=["far"])
             elif k in ("sm", "sv", "sa"):
                 a, e = CH[n]
-                keys = [tn + "_%d" % i for i in range(n + 1)] + ["ubq", "ubs"]
+                keys = [tn + "_%d" % i for i in range(n if k == "sm" else 0, n + 1)] + ["ubq%d" % (k != "sm"), "ubs%d" % (k != "sm")]
                 if k == "sm":
                     mm(MIXB[n], "ub", 256, tn, a, e, True, True, keys)
                 else:
@@ -453,21 +485,23 @@ def rank_program(g, core, T, topo):
                 a, e = CH[n]
                 tr(T.st[:, a:e], ps(MIXB[n], e - a), w=["st%d" % n], b=[MIXB[n]])
             elif k == "mask":
-                for i in range(4):
-                    wait("G", ("qG", total["qG"]))
-                    sel(T.m1[32 * i:32 * i + 32, :], T.st[32 * i:32 * i + 32, :], [[0, NS], [2, 16], [0, 2]], OP.is_ge, -1, 0, -1e28, r=["st0", "st1"], w=["m1%d" % i])
+                a, e = CH[n] if SPLIT else (0, C)
+                wait("G", ("qG", total["qG"]))
+                for i in range(4 if SPLIT or n else 0):
+                    sel(T.m1[32 * i:32 * i + 32, a:e], T.st[32 * i:32 * i + 32, a:e], [[0, (e - a) // 32], [2, 16], [0, 2]], OP.is_ge, -1, 0, -1e28,
+                        r=["st%d" % n] if SPLIT else ["st0", "st1"], w=["m1%d%d" % (n, i)])
                 wait("G", ("qG", total["qG"]))
             elif k == "eq":
                 for o in range(2):
                     tt(T.k7[:, 4 * o + 2 * n:4 * C:8], ps(VB[1][n], C, o, 2), T.m1[:, n:C:2], OP.is_equal,
-                       r=["m1%d" % i for i in range(4)], w=["ue%d%d" % (n, o)], b=[VB[1][n]])
+                       r=["m1%d%d" % (c, i) for c in range(2) for i in range(4)], w=["ue%d%d" % (n, o)], b=[VB[1][n]])
             elif k == "u":
                 for h in range(2) if h is None else [h]:
                     b, sc, keys, m = unit_in(n, h, VB)
                     ts(slot(n, h, 0, m), ps(b, m), sc, OP.is_lt, [1.0, SMALL][h], OP.mult, r=keys, w=ukeys(n, h), b=[b])
             elif k == "s":
                 b, sc, keys, m = unit_in(n, h, AB)
-                i = BY_ACT.index((n, h))
+                i, m = BY_ACT.index((n, h)), m - 32 * ((n, h) in OWN)
                 act(T.sg[:, C * i:C * i + m], ps(b, m), AF.Sign, {"bias": sc, "scale": -1.0}, r=keys, w=["sg%d" % i], b=[b])
             elif k == "r":
                 i, m = BY_ACT.index((n, h)), 32 * n
@@ -476,7 +510,11 @@ def rank_program(g, core, T, topo):
                     act(slot(n, h, 0, m + 32), T.sg[:, C * i:C * i + m + 32], AF.Relu, kw, r=keys, w=ukeys(n, h))
                 else:
                     act(slot(n, h, 0, m), T.sg[:, C * i:C * i + m], AF.Relu, dict(kw, accum_out=acc(n, h)), r=keys + ["racc0"], w=[ukeys(n, h)[0], "racc%d_%d" % (n, h)])
-                    act(slot(n, h, m, m + 32), T.sg[:, C * i + m:C * i + m + 32], AF.Relu, kw, r=keys, w=[ukeys(n, h)[1]])
+                    if (n, h) not in OWN:
+                        act(slot(n, h, m, m + 32), T.sg[:, C * i + m:C * i + m + 32], AF.Relu, kw, r=keys, w=[ukeys(n, h)[1]])
+            elif k == "d":
+                b, sc, keys, m = unit_in(n, h, VB)
+                ts(slot(n, h, m - 32, m), ps(b, m, m - 32), sc, OP.is_lt, [1.0, SMALL][h], OP.mult, r=keys, w=[ukeys(n, h)[1]], b=[b])
             elif k == "q":
                 keys = ["kz%d" % n, "kz%db" % n]
                 if n < 7:
@@ -510,15 +548,6 @@ def rank_program(g, core, T, topo):
             else:
                 mm(RANKB, "cs", 128 if n == 7 else 0, "k", koff[n], koff[n] + WIDTH[n], n == 0, n == 7, ["kq%d" % n, "csh" if n == 7 else "cs"])
 
-        queues = {"P": PLP, "G": "mask", "V": PLV, "A": PLA}
-        if t == 0:
-            queues = {q: " ".join(w for w in s.split() if parse(w)[0] not in LAYER) for q, s in queues.items()}
-            queues["V"] = " ".join(FIRST.get(w, w) for w in queues["V"].split())
-            queues["A"] = "k0 " + queues["A"] + " jt"
-        if t == 1:
-            queues["V"] = queues["V"].replace("h1", "h1 k10")
-        if t == R:
-            queues = {"P": ENDP, "V": ENDV, "A": ENDA, "S": ENDS}
         weave(queues, need, run)
 
     def leaders(t):
@@ -528,8 +557,8 @@ def rank_program(g, core, T, topo):
 
         def need(w):
             k, n, _ = parse(w)
-            return {"oq": ["wo"], "om": ["oq"], "exp": ["om"], "gx": ["tab", "lists"], "tr": ["gx0", "gx1"], "fl": ["tr"], "lcp": ["tr"], "dl": ["lcp"], "l": ["lcp"],
-                    "scan": ["fl"], "nn": ["scan"], "km": ["dl", "nn"], "tmp": ["km", "l7"], "dm": ["unit"], "dp": ["dm%s" % n]}.get(k, [])
+            return {"oq": ["wo"], "om": ["oq", "k9"], "exp": ["om"], "gx": ["tab0", "tab1", "k8"], "tr": ["gx0", "gx1"], "fl": ["tr"], "lcp": ["tr"], "dl": ["lcp"], "l": ["lcp"],
+                    "scan": ["fl"], "nn": ["scan"], "km": ["dl", "nn"], "tmp": ["km", "l7"], "dm": ["unit%s" % n], "dp": ["dm%s" % n]}.get(k, [])
 
         def run(q, w):
             k, n, _ = parse(w)
@@ -544,41 +573,45 @@ def rank_program(g, core, T, topo):
                 act(T["ord%d" % t][:], ps(ORDB, 128), AF.Exp, {"scale": math.log(2.0)}, w=["ord%d" % t], b=[ORDB])
                 send(got[:], T["ord%d" % t][:], "ao%d" % t, donor, ["ord%d" % t])
             elif k == "tab":
-                tt(T.tab[:], ps(RANKB, C), T.jt[:], OP.add, r=["jt"], w=["tab"], b=[RANKB])
+                a, e = (0, TABCUT) if n == 0 else (TABCUT, C)
+                tt(T.tab[:, a:e], ps(RANKB, e, a), T.jt[:, a:e], OP.add, r=["jt"], w=["tab%d" % n], b=[RANKB])
+            elif k == "k":
+                CONST[n]()
+            elif k == "unit":
+                unit(n)
             elif k == "dm":
                 mm(n, "e", 128 * n, tn, 0, C, True, True, [tn + "_0", tn + "_1", "eq%d" % n])
             elif k == "gx":
-                move(q, T.gx[:, 256 * n:256 * n + 256], T.tab[:].indirect(T.off1[:, 32 * t + 16 * n:32 * t + 16 * n + 16]), r=["tab", "off1"], w=["gx%d" % n])
+                a, e = (0, GXCUT) if n == 0 else (GXCUT, 32)
+                move(q, T.gx[:, 16 * a:16 * e], T.tab[:].indirect(T.off1[:, 32 * t + a:32 * t + e]), r=["tab0", "tab1", "off1"], w=["gx%d" % n])
             elif k == "tr":
-                tr(T.ty[:], T.gx[:], r=["gx0", "gx1"], w=["ty"])
+                tr(T.ty[:, 0:512], T.gx[:], r=["gx0", "gx1"], w=["ty"])
             elif k == "fl":
-                ts(T.fl[:], T.ty[:], float(TH), OP.is_lt, r=["ty"], w=["fl"])
+                ts(T.fl[:], T.ty[:, 0:512], (TH - 0.5) * UNIT, OP.is_lt, r=["ty"], w=["fl"])
             elif k == "lcp":
-                act(T.lcp[:], T.ty[:].indirect(T.offc[:, 40:56]), AF.Copy, {"scale": 2.0 ** -9}, r=["ty", "offL"], w=["lcp"])
+                move(q, T.lcp[:], T.ty[:, 0:512].indirect(T.offc[:, 40:56]), r=["ty", "offL"], w=["lcp"])
             elif k == "dl":
-                tt(T.dl[:, 1:256], T.lcp[:, 1:256], T.lcp[:, 0:255], OP.subtract, r=["lcp"], w=["dl"])
-                iota(T.dl[:, 0:256:8], [[0, 32]], -1000, 0, ["dl"])
+                tt(T.dl[:], T.ty[:].indirect(T.offc[:, 72:88]), T.lcp[:], OP.subtract, r=["ty", "far", "offP", "lcp"], w=["dl"])
             elif k == "l":
-                ts(T.l7[:], T.lcp[:, 7:256:8], -C * 2.0 ** -9, OP.add, r=["lcp"], w=["l7"])
+                ts(T.l7[:], T.lcp[:, 7:256:8], -C * UNIT, OP.add, r=["lcp"], w=["l7"])
             elif k == "dp":
                 move(q, T.dp[:, C * n:C * n + C], ps(n, C), w=["dp%d" % n], b=[n])
             elif k == "scan":
                 for i in range(4):
                     scan(T.fs[:, 128 * i:128 * i + 128], got[:], T.fl[:, 128 * i:128 * i + 128], OP.mult, OP.add, r=[gk, "fl"], w=["fs%d" % i])
             elif k == "nn":
-                ts(T.nn[:], T.fs[:].indirect(T.offc[:, 56:72]), 0.5, OP.mult, -64.5 + 2.0 ** -10, OP.add, r=["fs%d" % i for i in range(4)] + ["offN"], w=["nn"])
+                ts(T.nn[:], T.fs[:].indirect(T.offc[:, 56:72]), -0.5, OP.mult, 64.5 - 2.0 ** -10, OP.add, r=["fs%d" % i for i in range(4)] + ["offN"], w=["nn"])
             elif k == "km":
-                scan(T.km[:], T.dl[:], T.nn[:], OP.add, OP.max, r=["dl", "nn"], w=["km"])
+                scan(T.km[:], T.dl[:], T.nn[:], OP.add, OP.min, r=["dl", "nn"], w=["km"])
             else:
                 for a in range(4):
-                    tt(T.tmp[0:32, a:128:4], T.l7[32 * a:32 * a + 32, :], T.km[32 * a:32 * a + 32, 7:256:8], OP.subtract, r=["km", "l7"], w=["tmp%d" % a])
+                    tt(T.tmp[0:32, a:128:4], T.l7[32 * a:32 * a + 32, :], T.km[32 * a:32 * a + 32, 7:256:8], OP.add, r=["km", "l7"], w=["tmp%d" % a])
                 for b in range(4):
-                    tr(T.tp[32 * b:32 * b + 32, :], T.tmp[0:32, 32 * b:32 * b + 32], r=["tmp%d" % a for a in range(4)], w=["tp%d" % b])
-                ts(T.ti[:], T.tp[:], 2.0 ** 18, OP.mult, r=["tp%d" % b for b in range(4)], w=["ti"])
-                ts(T.tj[:], T.ti[:], 511, OP.bitwise_and, r=["ti"], w=["tj"])
-                cp(T.offz[:], T.tj[:], r=["tj"], w=["offz"])
+                    tr(T.tp[32 * b:32 * b + 32, 8:232:7], T.tmp[0:32, 32 * b:32 * b + 32], r=["tmp%d" % a for a in range(4)], w=["tp%d" % b])
+                scan(T.tq[:], T.tp[:, 7:231], T.tp[:, 4:228], OP.mult, OP.add, r=["steps"] + ["steps%d" % i for i in range(6)] + ["tp%d" % b for b in range(4)], w=["tq"])
+                ts(T.offz[:], T.tq[:, 4:224:7], 1.0 / (UNIT * UNIT), OP.mult, C / 2.0, OP.add, r=["tq"], w=["offz"])
 
-        weave({"V": CANV, "A": CANA, "P": CANP}, need, run)
+        weave({"V": FIRSTC if t == 0 else CANV, "A": CANA, "P": CANP}, need, run)
 
     for t in range(R):
         places(t)

import math
from concourse.mybir import dt, AluOpType as OP, ActivationFunctionType as AF

C, R, TH = 448, 3, 320
CUT = [192, 256, 256, 256]
RUNS = [[(0, k), (k, C)] for k in CUT]
NS = C // 32
WIDTH = [C, 384, 320, 256, 192, 128, 128, C]
EARLY = 5
EARLY0 = 6
SPLIT = True
TABCUT = 192
GXCUT = 22
ZCUT = 96
PIECE = 128
BORD = (2, 0, 3, 1)
UNIT = 2.0 ** -9
SMALL = 2.0 ** -10
PLV = "z0.0 z0.1 z1.0 zq0 z1.1 z2.0 zq1 g0.0 g0.1 za2.1 h0 zb2.1 g1.0 g1.1 zq2 h1 g2.0 g2.1 h2 x0.0 x0.1 xq0 tr0 x1.0 x1.1 u4.0 xq1 u4.1 u3 u2 u1.0 tr1 u1.1 u0 u13.0 u12.0 u13.1 u12.1 u7.0 q0 u7.1 u9 u8 u6.0 q2 u6.1 u5 q5 q1 eq0 eq1 round q4 parts q3 trr q6 q7"
PLA = "z0.2 z0.3 z1.2 z1.3 z2.2 g0.2 g0.3 z2.3 g1.2 g1.3 g2.2 g2.3 x0.2 x0.3 x1.2 x1.3 sum4 sum3 sum2 s11.1 s10.1 r11.1 s11.0 r10.1 s10.0 r11.0 r10.0 sum1 sum7 sum13 sum12 sum6 sum9 sum8 sum5"
PLP = "w0 w1 w2 own1 own0 dec0 sm0 dec1 sv0.0 sv0.1 sm1 sv1.0 sa1.1 sv1.1 sa1.0 rs13 rs12 col0 rs9 rs8 col2 col5 col1 col4 col3 col6 col7"
CANV = "wo tab0 oq tab1 gx0 tr fl dl scan l7 nn km tmp"
CANA = "exp gx1 lcp dp0 dp1 dp2 dp3"
CANP = "om dm0 dm1 dm2 dm3"
FIRSTV = "xq0 k19 xq1 tr0 k11 k2 tr1 k1 k3 u3 u2 u1 u0 u4 u13.0 u12.0 u13.1 u12.1 u7.0 q0 u7.1 u9 u8 u6.0 q2 u6.1 q5 k4 q1 k12 k5 eq0 eq1 round q4 parts q3 trr q6 q7 k14 k9 k6"
FIRSTA = "k0 s5.1 s5.0 r5.1 r5.0 sum3 sum2 s11.1 s10.1 r11.1 s11.0 r10.1 s10.0 r11.0 r10.0 sum1 sum4 sum7 sum13 sum12 sum6 sum9 sum8 k17 jt"
FIRSTP = "sm0 sa0.1 sm1 sv0.0 sv0.1 sa0.0 sv1.0 sa1.1 sv1.1 sa1.0 rs13 rs12 col0 rs9 rs8 col2 col5 col1 col4 col3 col6 col7"
FIRSTC = "wo k7 oq k8 tab0 tab1 unit0 gx0 tr unit1 fl unit2 dl scan l7 unit3 nn km tmp"
ENDV = "z0.0 z0.1 z1.0 zq0 z1.1 z2.0 zq1 g0.0 g0.1 za2.1 h0 zb2.1 g1.0 g1.1 zq2 h1 g2.0 g2.1 h2 x0.0 x0.1 xq0 x1.0 x1.1 out0 xq1 out1"
ENDA = "z0.2 z0.3 z1.2 z1.3 z2.2 g0.2 g0.3 z2.3 g1.2 g1.3 g2.2 g2.3 el0 x0.2 x0.3 x1.2 x1.3"
ENDP = "w0 w1 w2 own1 own0 dec0 dec1 y0 y1"
ENDS = "oc0 os0.0 os0.1 os0.2 os0.3 oc1 os1.0 os1.1 os1.2 os1.3"
MIX, VB, AB = [4, 0], [[5, 6], [1, 2]], [[4, 7], [3, 4]]
SUMB, RANKB, ORDB = [0, 5, 6], 7, 5

BF, F32, I32, U16, Q, U8 = "bfloat16", "float32", "int32", "uint16", "float8_e4m3fn_x4", "uint8"
SCRATCH = {"ps": ("psum", [128, 4096], F32)}


def _sb(name, n, d):
    SCRATCH[name] = ("sbuf", [128, n], d)


def _mx(name, n):
    _sb(name + "q", n, Q)
    _sb(name + "s", n, U8)


for _n, _w, _d in [
    ("xin", 4 * C, BF), ("xt", 4 * C, BF), ("ut", 512, BF), ("vt", 512, BF), ("cds", 128, I32), ("cdg", 128, F32), ("cdt", 128, F32),
    ("off1", 96, U16), ("et", 520, BF), ("rt", 520, BF), ("ones", 520, BF), ("zer", 520, BF), ("cst", 512, BF), ("csh", 512, BF), ("c2", 512, BF),
    ("pb", 168, F32), ("pc", 160, F32), ("pi", 8, I32), ("ci", 8, I32), ("cf", 8, F32), ("col", 16, F32), ("ib", 72, F32), ("offc", 88, U16),
    ("ig", 128, BF), ("ia", 128, BF), ("ca", 384, BF), ("cb", 384, BF), ("r32", 32, BF), ("i32w", 32, F32), ("r32b", 32, BF),
    ("j0", C, F32), ("jt", C, F32), ("jrow", C, F32),
    ("m1", C, F32), ("st", C, F32), ("sg", 16 * C, BF), ("junk", 5824, BF), ("racc", 28, F32), ("ra", 64, F32), ("rp", C, BF),
    ("wo", 512, BF), ("tab", C, F32), ("gx", 512, F32), ("ty", 640, F32), ("fl", 512, BF), ("lcp", 256, F32), ("dl", 256, F32), ("l7", 32, F32),
    ("fs", 512, BF), ("nn", 256, I32), ("km", 256, F32),
    ("tmp", 128, F32), ("tp", 232, F32), ("tq", 224, F32), ("offz", 32, U16),
    ("dp", 4 * C, BF), ("zt", 4 * C, BF), ("gt", 4 * C, BF), ("yb", C, F32), ("elb", C, F32),
]:
    _sb(_n, _w, _d)
for _i in range(8):
    _sb("k%d" % _i, 4 * WIDTH[_i], BF)
for _n, _w in [("u", 128), ("ub", 384), ("v", 128), ("wl", 512), ("e", 512), ("cs", 256), ("rs", 256), ("cc", 128), ("k", sum(WIDTH)), ("od", 128), ("z", C)]:
    _mx(_n, _w)
for _t in range(R + 1):
    _mx("t%d" % _t, C)
for _t in range(R):
    _mx("h%d" % _t, C)
    _mx("l%d" % _t, C)
    _sb("ord%d" % _t, 128, BF)
    _sb("got%d" % _t, 128, BF)

SEMAPHORES = ["qV", "qA", "qP", "qG", "sent"] + ["d%d" % i for i in range(48)] + ["ao%d" % t for t in range(R)] + ["ah%d_%d" % (t, c) for t in range(R) for c in range(2)]


def parse(w):
    k = w.rstrip("0123456789.")
    n = [int(x) for x in w[len(k):].split(".") if x]
    return (k, n[0] if n else None, n[1] if len(n) > 1 else None)


def rank_program(g, core, T, topo):
    rank = T.rank_of(core)
    if rank is None:
        return
    N = len(T.cores)
    eng = {"V": g.vector, "A": g.scalar, "P": g.tensor, "G": g, "S": g.sync}
    total = {}
    known = {q: {} for q in eng}
    snap = {}
    wrote, read, bank = {}, {}, {}
    ndma = [0]

    def wait(q, ev):
        s, n = ev
        if known[q].get(s, 0) >= n:
            return
        eng[q].wait_ge(T.sem[s], n)
        known[q][s] = n
        for s2, n2 in snap.get(ev, {}).items():
            if known[q].get(s2, 0) < n2:
                known[q][s2] = n2

    def deps(q, r, w, b):
        need = {}
        evs = [wrote[k] for k in list(r) + list(w) if k in wrote]
        for k in w:
            evs += read.get(k, [])
        for k in b:
            evs += [ev for q2, ev in bank.get(k, {}).items() if q2 != q]
        for s, n in evs:
            need[s] = max(need.get(s, 0), n)
        for s, n in sorted(need.items(), key=lambda e: e[0] == "q" + q):
            wait(q, (s, n))

    def note(q, ev, r, w, b):
        snap[ev] = dict(known[q])
        for k in r:
            read.setdefault(k, []).append(ev)
        for k in w:
            wrote[k] = ev
            read[k] = []
        for k in b:
            bank.setdefault(k, {})[q] = ev

    def op(q, call, r=(), w=(), b=()):
        deps(q, r, w, b)
        s = "q" + q
        total[s] = total.get(s, 0) + 1
        call().then_inc(T.sem[s], 1)
        note(q, (s, total[s]), r, w, b)

    def dma(q, out, in_, r=(), w=()):
        deps(q, r, w, ())
        s = "d%d" % ndma[0]
        ndma[0] += 1
        total[s] = 16
        eng[q].dma_start(out, in_).then_inc(T.sem[s], 16)
        note(q, (s, 16), r, w, ())

    def width(src, dst):
        return len(topo.engines(src, dst))

    def send(out, in_, sem, dst, r):
        deps("G", r, (), ())
        rid, pid, _ = topo.addr(dst)
        g.remote_dma(out, in_, T.sem[sem], T.sem["sent"], pid, rid, topo.mask(core, dst))
        total["sent"] = total.get("sent", 0) + width(core, dst)

    def arrives(key, sem, n):
        total[sem] = n
        wrote[key] = (sem, n)

    def weave(queues, need, run):
        todo, made = {q: s.split() for q, s in queues.items()}, set()
        every = set(w for q in todo.values() for w in q)
        while any(todo.values()):
            moved = False
            for q, steps in todo.items():
                while steps and all(x in made or x not in every for x in need(steps[0])):
                    run(q, steps[0])
                    made.add(steps.pop(0))
                    moved = True
            assert moved, todo

    V, A, P = g.vector, g.scalar, g.tensor

    def ps(b, n, a=0, step=1):
        return T.ps[:, 512 * b + a:512 * b + n:step]

    def ts(out, in0, s1, o0, s2=None, o1=None, **k):
        if o1 is None:
            op("V", lambda: V.tensor_scalar(out, in0, s1, None, o0), **k)
        else:
            op("V", lambda: V.tensor_scalar(out, in0, s1, s2, o0, o1), **k)

    def tt(out, a, b_, o, **k):
        op("V", lambda: V.tensor_tensor(out, a, b_, o), **k)

    def cp(out, a, **k):
        op("V", lambda: V.tensor_copy(out, a), **k)

    def tr(out, a, **k):
        op("V", lambda: V.transpose(out, a), **k)

    def ms(out, c, **k):
        op("V", lambda: V.memset(out, c), **k)

    def scan(out, d0, d1, o0, o1, **k):
        op("V", lambda: V.tensor_tensor_scan(out, d0, d1, 0.0, o0, o1), **k)

    def act(out, a, f, kw=None, **k):
        op("A", lambda: A.activation(out, a, f, **(kw or {})), **k)

    def move(q, out, a, **k):
        if q == "V":
            cp(out, a, **k)
        else:
            act(out, a, AF.Copy, **k)

    def qz(name, a, b_, tile, **k):
        op("V", lambda: V.quantize_mx(T[name + "q"][:, a:b_], T[name + "s"][:, a:b_], tile), **k)

    def mm(b, st, sa, mv, a, b_, start, stop, r):
        op("P", lambda: P.matmul_mx(ps(b, b_ - a), T[st + "q"][:, sa:sa + 128], T[st + "s"][:, sa:sa + 128],
                                    T[mv + "q"][:, a:b_], T[mv + "s"][:, a:b_], start, stop), r=r, b=[b])

    def iota(out, pat, base, cm, w):
        op("G", lambda: g.iota(out, pat, base, cm, allow_small_or_imprecise_dtypes=True), w=w)

    def zero(out, w):
        iota(out, [[0, out.shape[1]]], 0, 0, w)

    def sel(out, in_, pat, o, cm, base=0, fill=0.0, **k):
        op("G", lambda: g.affine_select(out, in_, pat, o, fill, base, cm), **k)

    dma("A", T.ut[:], T.u[:], w=["ut"])
    for c, (a, e) in enumerate(RUNS[0]):
        dma("S", T.xin[:, 4 * a:4 * e], T.x[:, 4 * a:4 * e], w=["xin%d" % c])
    op("G", lambda: g.iota(T.pi[:, 0:1], [[0, 1]], 0, 1), w=["pi"])
    iota(T.ib[:, 0:24], [[16, 3], [32, 4], [0, 2]], 0, 0, ["ibU"])
    iota(T.ig[:], [[0, 16], [1, 8]], 0, 0, ["ig"])
    iota(T.ia[:], [[1, 8], [-100, 2], [0, 8]], 100, 0, ["ia"])
    ms(T.zer[:], 0.0, w=["zer"])
    ms(T.cds[:], 0, w=["cds"])
    for out, n, w in ((T.rt[:], 520, ["rt"]), (T.c2[:], 512, ["c2z"]), (T.wo[:], 512, ["wo0", "wo1", "wo2", "wo3"]), (T.k7[:, 3:4 * C:4], C, ["kz7"]),
                      (T.rp[:], C, ["rp0", "rp1", "rp8", "rp9"])):
        act(out, T.zer[:, 0:n], AF.Copy, r=["zer"], w=w)
    for a in range(4):
        dma("S", T.cds[32 * a:32 * a + 24, 0:112], T.cd[a::4, :], r=["cds", "xin0", "xin1"], w=["cds%d" % a])
    dma("S", T.wlq[:].bitcast(dt.uint8), T.wc[:], w=["wq"])
    dma("S", T.wls[:], T.ws[:], w=["ws"])
    dma("S", T.vt[:], T.v[:], w=["vt"])
    for i, (sh, m) in enumerate([(5, 3), (4, 7), (0, 1), (3, 1), (0, 15)]):
        ts(T.ci[:, i:i + 1], T.pi[:, 0:1], sh, OP.logical_shift_right, m, OP.bitwise_and, r=["pi"], w=["ci%d" % i])
    ms(T.ones[:], 1.0, w=["ones"])
    sel(T.rt[:, 1:513:2], T.ones[:, 0:256], [[-1, 128], [0, 2]], OP.is_equal, 1, r=["ones"], w=["rt"])
    cp(T.cf[:, 0:5], T.ci[:, 0:5], r=["ci%d" % i for i in range(5)], w=["cf"])
    run32, pg, odd, bit3, l16 = [T.cf[:, i:i + 1] for i in range(5)]
    pa0, pa1, pr, wr, mix, tie = [T.col[:, i:i + 1] for i in range(6)]
    cp(T.offc[:, 0:16], T.ib[:, 0:16], r=["ibU"], w=["offU"])
    ms(T.k6[:, 256:512], 0.0, w=["kz6"])
    ms(T.k6[:, 129:256:2], 0.0, w=["kz6b"])
    ts(mix, odd, 16.0, OP.mult, -32.0, OP.add, r=["cf"], w=["mix"])
    ts(pa0, run32, 2.0, OP.mult, r=["cf"], w=["pa0"])
    ts(pa1, run32, 2.0, OP.mult, 1.0, OP.add, r=["cf"], w=["pa1"])
    ts(pr, run32, 2.0, OP.mult, bit3, OP.add, r=["cf"], w=["pr"])
    ts(wr, bit3, UNIT - UNIT / SMALL, OP.mult, -UNIT, OP.add, r=["cf"], w=["wr"])
    ms(T.racc[:], 0.0, w=["racc0"])
    ms(T.csh[:, 3:512:4], 0.0, w=["csh3"])
    ts(T.offc[:, 16:24], T.ib[:, 16:24], mix, OP.add, r=["ibU", "mix"], w=["offM"])

    def counter(n, out, colap, weight, keys, w):
        x0, x1 = T.ca[:, 128 * n:128 * n + 128], T.cb[:, 128 * n:128 * n + 128]
        ts(x0, T.ig[:], colap, OP.is_equal, weight, OP.mult, r=["ig"] + keys, w=["ca%d" % n])
        ts(x1, T.ia[:], colap, OP.is_equal, weight, OP.mult, r=["ia"] + keys, w=["cb%d" % n])
        return lambda: tt(out, x0, x1, OP.subtract, r=["ca%d" % n, "cb%d" % n], w=[w])

    counters = [counter(0, T.cst[:, 0:512:4], pa0, UNIT, ["pa0"], "cst0"), counter(1, T.csh[:, 2:512:4], pa1, UNIT, ["pa1"], "csh2"),
                counter(2, T.csh[:, 1:512:4], pr, wr, ["pr", "wr"], "csh1")]
    for i in range(6):
        ms(T["k%d" % i][:, 4 * WIDTH[i] - 127:4 * WIDTH[i]:2], 0.0, w=["kz%d" % i])
    for o in range(2):
        qz("rs", 128 * o, 128 * o + 128, T.rt[:, 1 - o:513 - o], r=["rt"], w=["rs%d" % o])
    qz("u", 0, 128, T.ut[:], r=["ut"], w=["uq"])
    counters[0]()
    counters[1]()

    def repeat_u(c, i, j):
        cp(T.ubq[:, 16 * i:16 * j].bitcast(dt.uint32), T.uq[:].bitcast(dt.uint32).indirect(T.offc[:, i:j]), r=["uq", "offU", "offM"], w=["ubq%d" % c])
        act(T.ubs[:, 16 * i:16 * j], T.us[:].indirect(T.offc[:, i:j]), AF.Copy, r=["uq", "offU", "offM"], w=["ubs%d" % c])

    repeat_u(0, 16, 24)
    iota(T.pb[:, 0:32], [[0, 2], [2000, 2], [0, 8]], 0, 0, ["pb2"])
    iota(T.pb[:, 96:128], [[0, 2], [100, 2], [-1, 8]], -100, 0, ["pb5"])
    for hf in range(2):
        iota(T.pb[:, 32 + 16 * hf:48 + 16 * hf], [[64, 2], [6, 4], [32, 2]], 0, 0, ["pb3%d" % hf])
        iota(T.pb[:, 64 + 16 * hf:80 + 16 * hf], [[32, 2], [128, 4], [16, 2]], 0, 0, ["pb4%d" % hf])
        iota(T.pb[:, 129 + 16 * hf:145 + 16 * hf], [[32, 2], [128, 4], [16, 2]], 0, 0, ["pb6"])
    iota(T.pb[:, 128:160:8], [[0, 4]], 512, 0, ["pb6"])
    iota(T.i32w[:], [[0, 4], [1, 8]], 0, 0, ["i32w"])
    iota(T.ib[:, 24:32], [[56, 2], [16, 2], [28, 2]], 0, 0, ["ibA"])
    iota(T.ib[:, 32:40], [[1, 8]], 0, 0, ["ibB"])
    iota(T.ib[:, 40:56], [[1, 8], [64, 2]], 0, 0, ["ibL"])
    iota(T.ib[:, 56:72], [[1, 8], [64, 2]], 8, 0, ["ibN"])
    iota(T.j0[:], [[32 * 513, NS], [2, 16], [513, 2]], -512 - C // 2, 0, ["j0"])

    def constants_0():
        for t in (2, 3):
            act(T.cst[:, t:512:4], T.csh[:, 2:512:4], AF.Copy, {"scale": 1.0 / SMALL}, r=["csh2"], w=["cst%d" % t])
        act(T.cst[:, 1:512:4], T.cst[:, 0:512:4], AF.Copy, r=["cst0"], w=["cst1"])
        act(T.csh[:, 0:512:4], T.cst[:, 0:512:4], AF.Copy, r=["cst0"], w=["csh0"])

    def constants_1():
        qz("cs", 0, 128, T.cst[:], r=["cst%d" % t for t in range(4)], w=["cs"])

    def constants_2():
        tr(T.pc[:], T.pb[:, 0:160], r=["pb2", "pb30", "pb31", "pb40", "pb41", "pb5", "pb6"], w=["pc"])
        ts(T.r32[:], T.i32w[:], pg, OP.is_equal, r=["i32w", "cf"], w=["r32"])
        ts(T.r32b[:], T.i32w[:], -1.0, OP.add, pg, OP.is_equal, r=["i32w", "cf"], w=["r32b"])

    def constants_3():
        ts(T.col[:, 8:9], T.pc[:, 96:97], pg, OP.add, 0.5, OP.min, r=["pc", "cf"], w=["tie0"])
        ts(T.r32b[:, 0:32:8], T.i32w[:, 0:32:8], 7.0, OP.add, pg, OP.is_equal, r=["i32w", "cf"], w=["r32b"])

    def constants_4():
        ts(tie, T.col[:, 8:9], -0.5, OP.max, UNIT, OP.mult, r=["tie0"], w=["tie"])
        tt(T.r32[:], T.r32[:], T.r32b[:], OP.subtract, r=["r32b"], w=["r32"])

    def ratios():
        for b in range(4):
            act(T.c2[:, 129 * b:128 * b + 128:4], T.r32[:], AF.Copy, r=["r32", "c2z"], w=["c2r%d" % b])

    def after_mask():
        sel(T.et[:, 0:516], T.ones[:, 0:516], [[-1, 516]], OP.is_equal, 4, 3, r=["ones"], w=["et"])
        big = int(1.5 * 2 ** 23 * UNIT)
        for i, c in ((0, 0), (2, 1), (3, -1), (4, -1), (5, big), (6, -big)):
            iota(T.tp[:, i:232:7], [[0, len(range(i, 232, 7))]], c, 0, ["steps%d" % i] if i < 6 else ["steps"])
        iota(T.jrow[:], [[1, C]], 0, 0, ["jrow"])

    def constants_5():
        qz("cs", 128, 256, T.csh[:], r=["csh%d" % t for t in range(4)], w=["csh"])

    def lists():
        for nm, a, b_, c in (("A", 24, 32, l16), ("B", 32, 40, T.pc[:, 32:33]), ("L", 40, 56, T.pc[:, 64:65]), ("N", 56, 72, T.pc[:, 64:65])):
            ts(T.offc[:, a:b_], T.ib[:, a:b_], c, OP.add, r=["ib" + nm, "cf", "pc"], w=["off" + nm])
        ts(T.offc[:, 72:88], T.ib[:, 40:56], T.pc[:, 128:129], OP.add, r=["ibL", "pc"], w=["offP"])

    def unit(b):
        qz("e", 128 * b, 128 * b + 128, T.et[:, 3 - b:515 - b], r=["et"], w=["eq%d" % b])

    CONST = [constants_0, constants_1, constants_2, constants_3, constants_4, constants_5,
             lambda: cp(T.cdg[:], T.cds[:].indirect(T.offc[:, 24:32]), r=["offA"] + ["cds%d" % a for a in range(4)], w=["cdg"]),
             lambda: tr(T.cdt[:], T.cdg[:], r=["cdg"], w=["cdt"]),
             lambda: cp(T.off1[:], T.cdt[:].indirect(T.offc[:, 32:38]), r=["cdt", "offB"], w=["off1"]),
             lambda: qz("cc", 0, 128, T.c2[:], r=["c2r%d" % b for b in range(4)], w=["cc"]),
             lambda: qz("v", 0, 128, T.vt[:], r=["vt"], w=["vq"]),
             counters[2], lambda: ms(T.r32[:, 0:32:16], -8.0, w=["r32"]),
             lambda: ms(T.racc[:], 0.0, w=["racc0"] + ["racc%d_%d" % (s, h) for s in range(NS) for h in range(2)]),
             lists, None, None, ratios, after_mask, lambda: repeat_u(1, 0, 16)]

    def banks(c):
        return 4 * ((c + 1) % 2)

    def four(k, c):
        return ["%s%d.%d" % (k, c, b) for b in range(4)]

    LAYER = {"z": lambda c: [], "za": lambda c: [], "zb": lambda c: [], "zq": lambda c: four("z", c) + four("za", c) + four("zb", c),
             "w": lambda c: ["zq%d" % c] + four("g", c - 2), "g": lambda c: ["w%d" % c], "h": lambda c: four("g", c) + ["h%d" % (c - 1)],
             "own": lambda c: four("g", c) + four("g", c + 2), "dec": lambda c: ["own%d" % c], "x": lambda c: ["dec%d" % c], "xq": lambda c: four("x", c),
             "y": lambda c: ["xq%d" % c], "out": lambda c: ["y%d" % c], "oc": lambda c: ["xq%d" % c], "os": lambda c: ["xq%d" % c], "el": lambda c: []}

    def layer(q, k, c, b, t):
        on, hn, ln, nx = "t%d" % (t - 1), "h%d" % (t - 1), "l%d" % (t - 1), "t%d" % t
        a, e = [(0, PIECE), (PIECE, CUT[t]), (CUT[t], C)][c] if k in ("z", "za", "zb", "zq", "w", "g", "h") else RUNS[t][c]
        donor, child = T.cores[(rank + t) % N], T.cores[(rank - t) % N]
        if k in ("z", "za", "zb"):
            a, e = a + ZCUT * (k == "zb"), a + ZCUT if k == "za" else e
            move(q, T.zt[:, 4 * a + b:4 * e:4], T.dp[:, C * b:C * b + C].indirect(T.offz[:, a // 16:e // 16]), r=["offz", "dp%d" % b],
                 w=["%s%d_%d" % (x, c, b) for x in (("za", "zb") if k == "z" else (k,))])
        elif k == "zq":
            qz("z", a, e, T.zt[:, 4 * a:4 * e], r=["%s%d_%d" % (x, c, b) for x in ("za", "zb") for b in range(4)], w=["zq%d" % c])
        elif k == "w":
            for b in BORD:
                mm(banks(c) + b, "wl", 128 * b, "z", a, e, True, True, ["zq%d" % c, "wq", "ws"])
        elif k == "g":
            kw = {"w": ["g%d_%d" % (c, b)], "b": [banks(c) + b]}
            if q == "V":
                ts(T.gt[:, 4 * a + b:4 * e:4], ps(banks(c) + b, e - a), 0.0, OP.max, 0.015625, OP.mult, **kw)
            else:
                act(T.gt[:, 4 * a + b:4 * e:4], ps(banks(c) + b, e - a), AF.Relu, {"scale": 0.015625}, **kw)
        elif k == "h":
            qz(hn, a, e, T.gt[:, 4 * a:4 * e], r=["g%d_%d" % (c, b) for b in range(4)], w=[hn + "_%d" % c])
            sem = "ah%d_%d" % (t - 1, c // 2)
            send(T[ln + "q"][:, a:e].bitcast(dt.uint8), T[hn + "q"][:, a:e].bitcast(dt.uint8), sem, child, [hn + "_%d" % c])
            if c:
                a = RUNS[t][c // 2][0]
                send(T[ln + "s"][:, a:e], T[hn + "s"][:, a:e], sem, child, [hn + "_0", hn + "_%d" % c])
        elif k == "own":
            for b in (0, 2, 1, 3):
                mm(banks(c) + b, "e", 128 * b, on, a, e, True, False, [on + "_0", on + "_1"])
        elif k == "dec":
            arrives(ln + "_%d" % c, "ah%d_%d" % (t - 1, c), (3 - c) * width(donor, core))
            for b in BORD:
                mm(banks(c) + b, "e", 128 * b, ln, a, e, False, True, [ln + "_%d" % c])
        elif k == "x":
            move(q, T.xt[:, 4 * a + b:4 * e:4], ps(banks(c) + b, e - a), w=["x%d_%d" % (c, b)], b=[banks(c) + b])
        elif k == "xq" and t == 0:
            qz(nx, a, e, T.xin[:, 4 * a:4 * e], r=["xin%d" % c], w=[nx + "_%d" % c])
        elif k == "xq":
            qz(nx, a, e, T.xt[:, 4 * a:4 * e], r=["x%d_%d" % (c, b) for b in range(4)], w=[nx + "_%d" % c])
        elif k == "y":
            mm(banks(c), "v", 0, nx, a, e, True, True, [nx + "_%d" % c, "vq"])
        elif k == "oc":
            dma(q, T.oc[:, 4 * a:4 * e], T[nx + "q"][:, a:e].bitcast(dt.uint8), r=[nx + "_%d" % c])
        elif k == "os":
            dma(q, T.osc[4 * b:4 * b + 4, a:e], T[nx + "s"][32 * b:32 * b + 4, a:e], r=[nx + "_%d" % c])
        elif k == "out":
            move(q, T.yb[:, a:e], ps(banks(c), e - a), w=["yb%d" % c], b=[banks(c)])
            dma("A", T.y[:, a:e], T.yb[:, a:e], r=["yb%d" % c])
        else:
            act(T.elb[:], T.jrow[:].indirect(T.offz[:, 0:28]), AF.Copy, r=["jrow", "offz"], w=["elb"])
            dma("S", T.el[:], T.elb[0:128:16, :], r=["elb"])

    koff = [sum(WIDTH[:i]) for i in range(8)]

    def tile_of(s):
        return (NS - 1 - s) // 2

    def slot(s, h, a, n, step=4):
        return T["k%d" % tile_of(s)][:, 4 * a + 2 * h + 1 - s % 2:4 * n:step]

    def ukeys(s, h):
        return ["u%d_%d" % (s, h), "u%d_%dd" % (s, h)]

    def acc(s, which):
        return T.racc[:, 2 * s + which:2 * s + which + 1]

    def junk(s, n):
        return T.junk[:, 32 * s * (s - 1):32 * s * (s - 1) + n]

    def pieces(s):
        m = 32 * s
        k = m // 128
        return [0] + [m - 2 * (m // 2 // k) * x for x in range(k - 1, -1, -1)]

    def places(t):
        tn, CH = "t%d" % t, RUNS[t]
        cut, MIXB = EARLY if t else EARLY0, MIX
        queues = {"P": PLP, "G": "mask0 mask1", "V": PLV.replace("h2", "h2 k10 k13") if t == 1 else PLV, "A": PLA}
        if t == 0:
            queues = {"P": FIRSTP, "G": "mask0 mask1 k18", "V": FIRSTV, "A": FIRSTA}
        if t == R:
            queues = {"P": ENDP, "V": ENDV, "A": ENDA, "S": ENDS}
        BY_ACT = [parse(w)[1:] for w in queues["A"].split() if parse(w)[0] == "s"]
        OWN = [parse(w)[1:] for w in queues["V"].split() if parse(w)[0] == "d"]
        BY_PE = [parse(w)[1] for w in queues["P"].split() if parse(w)[0] == "rs"]

        def made(blocks):
            return [x % (s, h) for s in blocks for h in range(2) for x in ("u%d.%d", "r%d.%d", "d%d.%d")] + ["u%d" % s for s in blocks]

        early = made(range(cut))
        rk = ["racc0"] + ["racc%d_%d" % (s, h) for s in range(NS) for h in range(2)]
        whole, fine = T.ra[:, 0:28], T.ra[:, 32:60]

        def need(w):
            k, n, h = parse(w)
            c = int(n is not None and n >= cut)
            if k in LAYER:
                return LAYER[k](n)
            if k in ("u", "s", "d"):
                return ["tr%d" % int(32 * n >= CUT[t])] + ["s%s%d.%d" % ("a" if k == "s" else "v", c, x) for x in range(2) if h in (None, x)]
            if k in ("sm", "sv", "sa"):
                return ["xq%d" % n] + ["k19"] * (k != "sm") + (["tr0"] + ["s%d.0" % s for s in range(cut) if n] if k == "sa" and AB[n][h] == MIXB[0] else [])
            if k == "rs":
                return ["q%d" % tile_of(n)] + ["sum%d" % s for s in BY_PE[:max(0, BY_PE.index(n) + 1 - len(SUMB))]] + early
            if k == "q":
                return made([NS - 1 - 2 * n, NS - 2 - 2 * n]) if n < 7 else ["trr", "eq0", "eq1"]
            return {"k": {0: ["k19"], 1: ["k0"], 3: ["k2"], 4: ["k3"], 5: ["k0", "k11"], 6: ["k14"], 7: ["k6"], 8: ["k7"], 9: ["k17"], 12: ["k4"], 14: ["k2"], 15: ["k18"], 16: ["k18"],
                          17: ["k12"], 18: ["mask1"]}.get(n, []), "jt": ["k2"], "mask": ["tr0", "tr%s" % n], "tr": ["sm%s" % n], "r": ["s%s.%s" % (n, h)],
                    "eq": ["mask0", "mask1", "sv1.0", "sv1.1"], "sum": ["rs%s" % n] + made([n or 0]), "col": ["k1", "q%s" % n] + early + ["k5"] * (n == 7),
                    "round": ["sum%d" % s for s in range(NS)] + made(range(NS)), "parts": ["round"], "trr": ["parts"]}.get(k, [])

        def unit_in(s, h, bk):
            return bk[int(s >= cut)][h], T.st[:, 32 * s + 30 + h:32 * s + 31 + h], ["st%d" % int(32 * s >= CUT[t])], 32 * s + 32

        def run(q, w):
            k, n, h = parse(w)
            if k in LAYER:
                layer(q, k, n, h, t)
            elif k == "k":
                CONST[n]()
            elif k == "jt":
                act(T.jt[:], T.j0[:], AF.Identity, {"scale": UNIT * UNIT, "bias": T.pc[:, 0:1]}, r=["j0", "pc"], w=["jt"])
                act(T.ty[:, 512:640], T.zer[:, 0:128], AF.Exp, {"bias": 7.0}, r=["zer"], w=["far"])
            elif k in ("sm", "sv", "sa"):
                a, e = CH[n]
                keys = [tn + "_%d" % i for i in range(n if k == "sm" else 0, n + 1)] + ["ubq%d" % (k != "sm"), "ubs%d" % (k != "sm")]
                if k == "sm":
                    mm(MIXB[n], "ub", 256, tn, a, e, True, True, keys)
                else:
                    mm((VB if k == "sv" else AB)[n][h], "ub", 128 * h, tn, 0, e if n else max(128, 32 * cut), True, True, keys)
            elif k == "tr":
                a, e = CH[n]
                tr(T.st[:, a:e], ps(MIXB[n], e - a), w=["st%d" % n], b=[MIXB[n]])
            elif k == "mask":
                a, e = CH[n] if SPLIT else (0, C)
                wait("G", ("qG", total["qG"]))
                for i in range(4 if SPLIT or n else 0):
                    sel(T.m1[32 * i:32 * i + 32, a:e], T.st[32 * i:32 * i + 32, a:e], [[0, (e - a) // 32], [2, 16], [0, 2]], OP.is_ge, -1, 0, -1e28,
                        r=["st%d" % n] if SPLIT else ["st0", "st1"], w=["m1%d%d" % (n, i)])
                wait("G", ("qG", total["qG"]))
            elif k == "eq":
                for o in range(2):
                    tt(T.k7[:, 4 * o + 2 * n:4 * C:8], ps(VB[1][n], C, o, 2), T.m1[:, n:C:2], OP.is_equal,
                       r=["m1%d%d" % (c, i) for c in range(2) for i in range(4)], w=["ue%d%d" % (n, o)], b=[VB[1][n]])
            elif k == "u":
                for h in range(2) if h is None else [h]:
                    b, sc, keys, m = unit_in(n, h, VB)
                    ts(slot(n, h, 0, m), ps(b, m), sc, OP.is_lt, [1.0, SMALL][h], OP.mult, r=keys, w=ukeys(n, h), b=[b])
            elif k == "s":
                b, sc, keys, m = unit_in(n, h, AB)
                i, m = BY_ACT.index((n, h)), m - 32 * ((n, h) in OWN)
                act(T.sg[:, C * i:C * i + m], ps(b, m), AF.Sign, {"bias": sc, "scale": -1.0}, r=keys, w=["sg%d" % i], b=[b])
            elif k == "r":
                i, m = BY_ACT.index((n, h)), 32 * n
                kw, keys = {"scale": [1.0, SMALL][h]}, ["sg%d" % i]
                if n in BY_PE or n == 0:
                    act(slot(n, h, 0, m + 32), T.sg[:, C * i:C * i + m + 32], AF.Relu, kw, r=keys, w=ukeys(n, h))
                else:
                    act(slot(n, h, 0, m), T.sg[:, C * i:C * i + m], AF.Relu, dict(kw, accum_out=acc(n, h)), r=keys + ["racc0"], w=[ukeys(n, h)[0], "racc%d_%d" % (n, h)])
                    if (n, h) not in OWN:
                        act(slot(n, h, m, m + 32), T.sg[:, C * i + m:C * i + m + 32], AF.Relu, kw, r=keys, w=[ukeys(n, h)[1]])
            elif k == "d":
                b, sc, keys, m = unit_in(n, h, VB)
                ts(slot(n, h, m - 32, m), ps(b, m, m - 32), sc, OP.is_lt, [1.0, SMALL][h], OP.mult, r=keys, w=[ukeys(n, h)[1]], b=[b])
            elif k == "q":
                keys = ["kz%d" % n, "kz%db" % n]
                if n < 7:
                    keys += [x for s in (NS - 1 - 2 * n, NS - 2 - 2 * n) for h in range(2) for x in ukeys(s, h)]
                else:
                    keys += ["ur"] + ["ue%d%d" % (h, o) for h in range(2) for o in range(2)]
                qz("k", koff[n], koff[n] + WIDTH[n], T["k%d" % n][:], r=keys, w=["kq%d" % n])
            elif k == "rs":
                i, ends, b = tile_of(n), pieces(n), SUMB[BY_PE.index(n) % len(SUMB)]
                for x in range(len(ends) - 1):
                    mm(b, "rs", 128 * (1 - n % 2), "k", koff[i] + ends[x], koff[i] + ends[x + 1], x == 0, x == len(ends) - 2, ["kq%d" % i, "rs0", "rs1"])
            elif k == "sum":
                m = 32 * n
                mine = [h for h in range(2) if (n, h) not in BY_ACT]
                if n in BY_PE:
                    m, b = pieces(n)[1], SUMB[BY_PE.index(n) % len(SUMB)]
                    act(junk(n, m), ps(b, m), AF.Copy, {"accum_out": acc(n, 0)}, r=["racc0"], w=["racc%d_0" % n, "junk%d" % n], b=[b])
                elif len(mine) == 2:
                    act(junk(n, 2 * m), slot(n, 0, 0, m, 2), AF.Copy, {"accum_out": acc(n, 0)}, r=["racc0", ukeys(n, 0)[0], ukeys(n, 1)[0]], w=["racc%d_0" % n, "junk%d" % n])
                else:
                    act(junk(n, m), slot(n, mine[0], 0, m), AF.Copy, {"accum_out": acc(n, mine[0])}, r=["racc0", ukeys(n, mine[0])[0]], w=["racc%d_%d" % (n, mine[0]), "junk%d" % n])
            elif k == "round":
                for out, e, key in ((T.rp[:, 0:C:16], 28, "rp0"), (whole, 23, "whole"), (fine, 18, "fine")):
                    ts(out, T.racc[:], 1.5 * 2.0 ** e, OP.add, 1.5 * 2.0 ** e, OP.subtract, r=rk, w=[key])
            elif k == "parts":
                tt(T.rp[:, 1:C:16], whole, T.rp[:, 0:C:16], OP.subtract, r=["whole", "rp0"], w=["rp1"])
                tt(T.rp[:, 8:C:16], fine, whole, OP.subtract, r=["whole", "fine"], w=["rp8"])
                tt(T.rp[:, 9:C:16], T.racc[:], fine, OP.subtract, r=rk + ["fine"], w=["rp9"])
            elif k == "trr":
                tr(T.k7[:, 1:4 * C:4], T.rp[:], r=["rp0", "rp1", "rp8", "rp9"], w=["ur"])
            else:
                mm(RANKB, "cs", 128 if n == 7 else 0, "k", koff[n], koff[n] + WIDTH[n], n == 0, n == 7, ["kq%d" % n, "csh" if n == 7 else "cs"])

        weave(queues, need, run)

    def leaders(t):
        tn, got, gk = "t%d" % t, T["got%d" % t], "got%d" % t
        donor, child = T.cores[(rank + 1 + t) % N], T.cores[(rank - 1 - t) % N]
        arrives(gk, "ao%d" % t, width(child, core))

        def need(w):
            k, n, _ = parse(w)
            return {"oq": ["wo"], "om": ["oq", "k9"], "exp": ["om"], "gx": ["tab0", "tab1", "k8"], "tr": ["gx0", "gx1"], "fl": ["tr"], "lcp": ["tr"], "dl": ["lcp"], "l": ["lcp"],
                    "scan": ["fl"], "nn": ["scan"], "km": ["dl", "nn"], "tmp": ["km", "l7"], "dm": ["unit%s" % n], "dp": ["dm%s" % n]}.get(k, [])

        def run(q, w):
            k, n, _ = parse(w)
            if k == "wo":
                for a in range(4):
                    ts(T.wo[:, 128 * a:128 * a + 112], ps(RANKB, C, a, 4), tie, OP.is_lt, r=["tie"], w=["wo%d" % a], b=[RANKB])
            elif k == "oq":
                qz("od", 0, 128, T.wo[:], r=["wo%d" % a for a in range(4)], w=["oq"])
            elif k == "om":
                mm(ORDB, "od", 0, "cc", 0, 128, True, True, ["oq", "cc"])
            elif k == "exp":
                act(T["ord%d" % t][:], ps(ORDB, 128), AF.Exp, {"scale": math.log(2.0)}, w=["ord%d" % t], b=[ORDB])
                send(got[:], T["ord%d" % t][:], "ao%d" % t, donor, ["ord%d" % t])
            elif k == "tab":
                a, e = (0, TABCUT) if n == 0 else (TABCUT, C)
                tt(T.tab[:, a:e], ps(RANKB, e, a), T.jt[:, a:e], OP.add, r=["jt"], w=["tab%d" % n], b=[RANKB])
            elif k == "k":
                CONST[n]()
            elif k == "unit":
                unit(n)
            elif k == "dm":
                mm(n, "e", 128 * n, tn, 0, C, True, True, [tn + "_0", tn + "_1", "eq%d" % n])
            elif k == "gx":
                a, e = (0, GXCUT) if n == 0 else (GXCUT, 32)
                move(q, T.gx[:, 16 * a:16 * e], T.tab[:].indirect(T.off1[:, 32 * t + a:32 * t + e]), r=["tab0", "tab1", "off1"], w=["gx%d" % n])
            elif k == "tr":
                tr(T.ty[:, 0:512], T.gx[:], r=["gx0", "gx1"], w=["ty"])
            elif k == "fl":
                ts(T.fl[:], T.ty[:, 0:512], (TH - 0.5) * UNIT, OP.is_lt, r=["ty"], w=["fl"])
            elif k == "lcp":
                move(q, T.lcp[:], T.ty[:, 0:512].indirect(T.offc[:, 40:56]), r=["ty", "offL"], w=["lcp"])
            elif k == "dl":
                tt(T.dl[:], T.ty[:].indirect(T.offc[:, 72:88]), T.lcp[:], OP.subtract, r=["ty", "far", "offP", "lcp"], w=["dl"])
            elif k == "l":
                ts(T.l7[:], T.lcp[:, 7:256:8], -C * UNIT, OP.add, r=["lcp"], w=["l7"])
            elif k == "dp":
                move(q, T.dp[:, C * n:C * n + C], ps(n, C), w=["dp%d" % n], b=[n])
            elif k == "scan":
                for i in range(4):
                    scan(T.fs[:, 128 * i:128 * i + 128], got[:], T.fl[:, 128 * i:128 * i + 128], OP.mult, OP.add, r=[gk, "fl"], w=["fs%d" % i])
            elif k == "nn":
                ts(T.nn[:], T.fs[:].indirect(T.offc[:, 56:72]), -0.5, OP.mult, 64.5 - 2.0 ** -10, OP.add, r=["fs%d" % i for i in range(4)] + ["offN"], w=["nn"])
            elif k == "km":
                scan(T.km[:], T.dl[:], T.nn[:], OP.add, OP.min, r=["dl", "nn"], w=["km"])
            else:
                for a in range(4):
                    tt(T.tmp[0:32, a:128:4], T.l7[32 * a:32 * a + 32, :], T.km[32 * a:32 * a + 32, 7:256:8], OP.add, r=["km", "l7"], w=["tmp%d" % a])
                for b in range(4):
                    tr(T.tp[32 * b:32 * b + 32, 8:232:7], T.tmp[0:32, 32 * b:32 * b + 32], r=["tmp%d" % a for a in range(4)], w=["tp%d" % b])
                scan(T.tq[:], T.tp[:, 7:231], T.tp[:, 4:228], OP.mult, OP.add, r=["steps"] + ["steps%d" % i for i in range(6)] + ["tp%d" % b for b in range(4)], w=["tq"])
                ts(T.offz[:], T.tq[:, 4:224:7], 1.0 / (UNIT * UNIT), OP.mult, C / 2.0, OP.add, r=["tq"], w=["offz"])

        weave({"V": FIRSTC if t == 0 else CANV, "A": CANA, "P": CANP}, need, run)

    for t in range(R):
        places(t)
        leaders(t)
    places(R)
    for s, n in total.items():
        wait("G", (s, n))
